import numpy as np
import ml_dtypes


def mxq(x, axis, fmt="e4m3"):
    dtype, down = {"e4m3": (ml_dtypes.float8_e4m3fn, 7), "e5m2": (ml_dtypes.float8_e5m2, 14)}[fmt]
    v = np.moveaxis(np.asarray(x, np.float32).astype(ml_dtypes.bfloat16).astype(np.float64), axis, -1)
    blocks = v.reshape(v.shape[:-1] + (-1, 32))
    amax = np.abs(blocks).max(-1, keepdims=True)
    byte = np.maximum(np.where(amax > 0, np.frexp(amax)[1] - 1 + 127, 0) - down, 1)
    scale = np.exp2(byte - 127.0)
    codes = (blocks / scale).astype(np.float32).astype(dtype).astype(np.float64)
    return np.moveaxis((codes * scale).reshape(v.shape), -1, axis)


WIDE = False


def mx_kscale(k):
    if not WIDE:
        return np.ones(k)
    levels = np.array([10, -10, 5, -5, 0])
    if k % 512:
        return np.exp2(np.random.permutation(np.resize(levels, k // 32))).repeat(32)
    a = np.empty((k // 512, 16))
    for p in range(k // 512):
        a[p, :8] = np.random.permutation(np.resize(levels, 8))
        for g in range(8):
            far = levels[np.abs(levels - a[p, g]) >= 10]
            a[p, g + 8] = far[np.random.randint(len(far))]
    return np.exp2(a.ravel()).repeat(32)


def f64(x):
    return np.asarray(x).astype(np.float64)


def striped(idx):
    return np.tile(idx.reshape(-1, 16).T, (8, 1)).astype(np.uint16)


def unstriped(offs):
    return offs[:16].T.reshape(-1).astype(np.int64)


E2M1 = np.array([0.0, 0.5, 1.0, 1.5, 2.0, 3.0, 4.0, 6.0, -0.0, -0.5, -1.0, -1.5, -2.0, -3.0, -4.0, -6.0])


def pack_weight(w, fmt):
    k, n = w.shape
    w = f64(np.asarray(w, np.float32).astype(ml_dtypes.bfloat16)).reshape(k // 32, 32, n)
    amax = np.abs(w).max(1)
    if fmt == "e4m3":
        byte = np.frexp(amax)[1] - 1 + 127 - 7
    else:
        mant, ex = np.frexp(amax / 6.0)
        byte = np.where(mant > 0.5, ex, ex - 1) + 127
    byte = np.clip(np.where(amax > 0, byte, 1), 1, 254)
    scaled = (w * np.exp2(127.0 - byte)[:, None, :]).reshape(k, n).astype(np.float32)
    by_word = np.ascontiguousarray(scaled.reshape(k // 512, 128, 4, n).transpose(0, 1, 3, 2))
    if fmt == "e4m3":
        words = by_word.astype(ml_dtypes.float8_e4m3fn).view(np.uint8)
    else:
        c = by_word.astype(ml_dtypes.float4_e2m1fn).view(np.uint8) & 0xF
        words = (c[..., 0::2] | (c[..., 1::2] << 4)).reshape(k // 512, 128, 2 * n)
    return np.ascontiguousarray(words), np.ascontiguousarray(byte.astype(np.uint8).reshape(k // 512, 16, n))


def unpack_weight(words, scales, fmt):
    g, _, n = scales.shape
    words = np.ascontiguousarray(words).reshape(g, 128, n, -1)
    if fmt == "e4m3":
        vals = words.view(ml_dtypes.float8_e4m3fn).astype(np.float64)
    else:
        nib = np.empty((g, 128, n, 4), np.uint8)
        nib[..., 0::2] = words & 0xF
        nib[..., 1::2] = words >> 4
        vals = E2M1[nib]
    vals = vals * np.repeat(np.exp2(scales.astype(np.float64) - 127.0), 8, axis=1)[..., None]
    return vals.transpose(0, 1, 3, 2).reshape(g * 512, n)


def silu(v):
    return v / (1.0 + np.exp(-np.maximum(v, -700.0)))


K, T, S1, S2 = 512, 2048, 1024, 1024


def setup_inputs():
    n = np.random.standard_normal
    s = mx_kscale(K)
    u = mx_kscale(K)
    first, second = np.random.permutation(T)[:S1], np.random.permutation(T)[:S2]
    xf = n((K, T))
    x = pack_weight(xf * s[:, None], "e4m3")
    w1 = pack_weight(n((K, K)) / np.sqrt(K) / s[:, None] * u, "e2m1")
    w2 = pack_weight(n((K, K)) / np.sqrt(K) / u[:, None] * u, "e4m3")
    return {
        "x_words": x[0],
        "x_scales": x[1],
        "xr": (xf * u[:, None]).astype(np.float32),
        "w1_words": w1[0],
        "w1_scales": w1[1],
        "w2_words": w2[0],
        "w2_scales": w2[1],
        "gate1": (np.tile(np.random.uniform(0.2, 1.0, S1), (128, 1))).astype(np.float32),
        "gate2": (np.tile(np.random.uniform(0.2, 1.0, S2), (128, 1))).astype(np.float32),
        "offs": striped(first),
        "offs2": striped(second),
    }


def reference(x_words, x_scales, xr, w1_words, w1_scales, w2_words, w2_scales, gate1, gate2, offs, offs2):
    w1 = unpack_weight(w1_words, w1_scales, "e2m1")
    w2 = unpack_weight(w2_words, w2_scales, "e4m3")
    idx, idx2 = unstriped(offs), unstriped(offs2)
    r = f64(xr)
    r[:, idx] += f64(gate1[:1]) * silu(w1.T @ unpack_weight(x_words, x_scales, "e4m3")[:, idx])
    r2 = r.copy()
    r2[:, idx2] += f64(gate2[:1]) * silu(w2.T @ mxq(r[:, idx2], 0, "e4m3"))
    return r2

@@ -1,0 +1,183 @@
+from contextlib import ExitStack
+
+import concourse.mybir as mybir
+
+K, T, S = 512, 2048, 1024
+P = 128
+PACK = 4
+HALF = 512
+FLOPS = 2 * 2 * K * K * S
+
+F32 = mybir.dt.float32
+BF16 = mybir.dt.bfloat16
+I32 = mybir.dt.int32
+U32 = mybir.dt.uint32
+U16 = mybir.dt.uint16
+U8 = mybir.dt.uint8
+FP8X4 = mybir.dt.float8_e4m3fn_x4
+FP4X4 = mybir.dt.float4_e2m1fn_x4
+SILU = mybir.ActivationFunctionType.Silu
+COPY = mybir.ActivationFunctionType.Copy
+MULT = mybir.AluOpType.mult
+ADD = mybir.AluOpType.add
+
+ORDER = (2, 0, 1, 3)
+
+
+def tile_moe_mod_silu_kernel(
+    tc, x_words, x_scales, xr, w1_words, w1_scales, w2_words, w2_scales, gate1, gate2, offs, offs2, out
+):
+    nc = tc.nc
+    with ExitStack() as ctx:
+        lists = ctx.enter_context(tc.tile_pool(name="lists", bufs=1))
+        keep = ctx.enter_context(tc.tile_pool(name="keep", bufs=1))
+        psum = ctx.enter_context(tc.psum_pool(name="psum", bufs=4))
+
+        def half_of(lst, h):
+            return lst[:, h * (HALF // 16) : (h + 1) * (HALF // 16)]
+
+        def load_scale_rows(plane, rows):
+            words = rows.bitcast(I32)
+            for q in range(4):
+                nc.sync.dma_start(
+                    out=plane[32 * q : 32 * (q + 1), :].bitcast(I32),
+                    in_=words[4 * q : 4 * (q + 1), :].partition_broadcast(8),
+                )
+
+        idx1 = lists.tile([P, S // 16], U16, name="idx1")
+        idx2 = lists.tile([P, S // 16], U16, name="idx2")
+        xs = keep.tile([P, T], U8, name="xs", align_bytes=64)
+        xw = keep.tile([P, T], U32, name="xw", align_bytes=64)
+        w1_raw = keep.tile([P, 2 * K], U8, name="w1_raw", align_bytes=64)
+        s1_raw = keep.tile([P, K], U8, name="s1_raw", align_bytes=64)
+        g1 = [keep.tile([P, HALF], F32, name="g1_%d" % h, align_bytes=64) for h in range(2)]
+        g2 = keep.tile([P, S], F32, name="g2")
+        res = {t: keep.tile([P, T], F32, name="res%d" % t) for t in ORDER}
+        z1 = [keep.tile([P, T], F32, name="z1_%d" % b) for b in range(2)]
+        z2 = [keep.tile([P, T], F32, name="z2_%d" % b) for b in range(2)]
+
+        nc.vector.memset(z1[1][:], 0.0)
+        nc.vector.memset(z1[0][:], 0.0)
+        nc.scalar.activation(z2[0][:], z1[1][:], SILU)
+        nc.scalar.copy(z2[1][:], z1[1][:])
+
+        nc.sync.dma_start(idx1[:], offs)
+        load_scale_rows(xs, x_scales[0])
+        nc.sync.dma_start(out=xw[:].bitcast(I32), in_=x_words[0].rearrange("p t d -> p (t d)").bitcast(I32))
+        load_scale_rows(s1_raw, w1_scales[0])
+        nc.sync.dma_start(out=w1_raw[:].bitcast(I32), in_=w1_words[0].bitcast(I32))
+        for h in range(2):
+            nc.sync.dma_start(out=g1[h][:], in_=gate1[:, h * HALF : (h + 1) * HALF])
+        xr_rows = xr.rearrange("(p t) w -> t p w", t=PACK)
+        out_rows = out.rearrange("(p t) w -> t p w", t=PACK)
+        for t in ORDER:
+            nc.sync.dma_start(out=res[t][:], in_=xr_rows[t])
+        nc.sync.dma_start(idx2[:], offs2)
+        nc.sync.dma_start(out=g2[:], in_=gate2)
+
+        w1 = keep.tile([P, 2 * K], U8, name="w1", align_bytes=64)
+        s1 = keep.tile([P, K], U8, name="s1", align_bytes=64)
+        w2 = keep.tile([P, K], U32, name="w2", align_bytes=64)
+        s2 = keep.tile([P, K], U8, name="s2", align_bytes=64)
+
+        def by_plane(ap):
+            return ap.rearrange("p (m t) -> p t m", t=PACK)
+
+        def as_planes(ap):
+            return ap.rearrange("p (t m) -> p t m", t=PACK)
+
+        gs = keep.tile([P, S], U8, name="gs", align_bytes=64)
+        gw = [keep.tile([P, HALF], U32, name="gw%d" % h, align_bytes=64) for h in range(2)]
+        nc.vector.tensor_copy(gs[:], xs[:].indirect(idx1[:]))
+        nc.vector.tensor_copy(as_planes(w1[:].bitcast(U16)), by_plane(w1_raw[:].bitcast(U16)))
+        nc.gpsimd.tensor_copy(as_planes(s1[:]), by_plane(s1_raw[:]))
+        for h in range(2):
+            nc.vector.tensor_copy(gw[h][:], xw[:].indirect(half_of(idx1, h)))
+
+        def products(name, lhs, lhs_scale, rhs, rhs_scale):
+            ys = {}
+            for t in ORDER:
+                y = keep.tile([P, S], F32, name="%s%d" % (name, t), tag="y%d" % t)
+                for h in range(2):
+                    acc = psum.tile([P, HALF], F32, name="acc")
+                    nc.tensor.matmul_mx(
+                        out=acc[:], lhsT=lhs(t), lhsT_scale=lhs_scale[:, t * P : (t + 1) * P],
+                        rhs=rhs[h][:].bitcast(FP8X4), rhs_scale=rhs_scale(h), start=True, stop=True,
+                    )
+                    nc.scalar.activation(y[:, h * HALF : (h + 1) * HALF], acc[:], SILU)
+                ys[t] = y
+            return ys
+
+        def gate_half(eng, y, gate, h):
+            cols = slice(h * HALF, (h + 1) * HALF)
+            eng.tensor_tensor(y[:, cols], y[:, cols], gate(h), MULT)
+
+        def gate_whole(y, gate):
+            for h in range(2):
+                gate_half(nc.gpsimd, y, gate, h)
+
+        def layer(ys, gate, z, idx, add, after_gates):
+            y = [ys[t] for t in ORDER]
+            gate_half(nc.vector, y[0], gate, 0)
+            gate_half(nc.gpsimd, y[0], gate, 1)
+            for h in range(2):
+                nc.vector.tensor_copy(z[0][:].indirect(half_of(idx, h)), y[0][:, h * HALF : (h + 1) * HALF])
+            gate_whole(y[1], gate)
+            gate_whole(y[2], gate)
+            nc.vector.tensor_copy(z[1][:].indirect(idx[:]), y[1][:])
+            add(0)
+            gate_whole(y[3], gate)
+            nc.vector.tensor_copy(z[0][:].indirect(idx[:]), y[2][:])
+            add(1)
+            after_gates()
+            add(2)
+            nc.vector.tensor_copy(z[1][:].indirect(idx[:]), y[3][:])
+            add(3)
+
+        y1 = products("y1", lambda t: w1[:, 2 * P * t : 2 * P * (t + 1)].bitcast(FP4X4), s1, gw,
+                      lambda h: gs[:, h * HALF : (h + 1) * HALF])
+        grouped = [keep.tile([P, HALF, PACK], BF16, name="grouped%d" % h, align_bytes=64) for h in range(2)]
+
+        def add1(n):
+            t = ORDER[n]
+            if n < 3:
+                nc.gpsimd.tensor_tensor(res[t][:], res[t][:], z1[n % 2][:], ADD)
+                rb = keep.tile([P, T], BF16, name="rb%d" % t, tag="win" if n == 0 else "rb%d" % t)
+                nc.scalar.copy(rb[:], res[t][:])
+                for h in range(2):
+                    nc.scalar.activation(grouped[h][:, :, t], rb[:].indirect(half_of(idx2, h)), COPY)
+            else:
+                last = keep.tile([P, T], F32, name="last", tag="win")
+                nc.vector.tensor_tensor(last[:], res[t][:], z1[n % 2][:], ADD)
+                res[t] = last
+
+        def second_weights():
+            w2_raw = keep.tile([P, K], U32, name="w2_raw", tag="g1_0", align_bytes=64)
+            s2_raw = keep.tile([P, K], U8, name="s2_raw", tag="g1_1", align_bytes=64)
+            nc.sync.dma_start(out=w2_raw[:].bitcast(I32), in_=w2_words[0].rearrange("p n d -> p (n d)").bitcast(I32))
+            load_scale_rows(s2_raw, w2_scales[0])
+            nc.gpsimd.tensor_copy(as_planes(w2[:]), by_plane(w2_raw[:]))
+            nc.gpsimd.tensor_copy(as_planes(s2[:]), by_plane(s2_raw[:]))
+
+        layer(y1, lambda h: g1[h][:], z1, idx1, add1, second_weights)
+        codes = [keep.tile([P, HALF], U32, name="codes%d" % h, align_bytes=64) for h in range(2)]
+        scales = [keep.tile([P, HALF], U8, name="scales%d" % h, align_bytes=64) for h in range(2)]
+        for h in range(2):
+            nc.vector.tensor_copy(grouped[h][:, :, ORDER[3]], res[ORDER[3]][:].indirect(half_of(idx2, h)))
+            nc.vector.quantize_mx(out=codes[h][:].bitcast(FP8X4), scales=scales[h][:],
+                                  in_=grouped[h][:].rearrange("p s t -> p (s t)"))
+
+        y2 = products("y2", lambda t: w2[:, P * t : P * (t + 1)].bitcast(FP8X4), s2, codes, lambda h: scales[h][:])
+
+        def add2(n):
+            t = ORDER[n]
+            if n < 3:
+                nc.gpsimd.tensor_tensor(res[t][:], res[t][:], z2[n % 2][:], ADD)
+                nc.sync.dma_start(out=out_rows[t], in_=res[t][:])
+            else:
+                for c in range(4):
+                    cols = slice(c * HALF, (c + 1) * HALF)
+                    nc.vector.tensor_tensor(res[t][:, cols], res[t][:, cols], z2[n % 2][:, cols], ADD)
+                    nc.sync.dma_start(out=out_rows[t][:, cols], in_=res[t][:, cols])
+
+        layer(y2, lambda h: g2[:, h * HALF : (h + 1) * HALF], z2, idx2, add2, lambda: None)

@@ -22,6 +22,10 @@ MULT = mybir.AluOpType.mult
 ADD = mybir.AluOpType.add
 
 ORDER = (2, 0, 1, 3)
+HALVES = (slice(0, 512), slice(512, 1024))
+PIECES = (slice(0, 256), slice(256, 512), slice(512, 1024))
+TAGS1 = ("y0", "y1", "slot_a", "slot_b", "res%d" % ORDER[1])
+TAGS2 = ("y0", "y1", "slot_c", "slot_d", "slot_b")
 
 
 def tile_moe_mod_silu_kernel(
@@ -33,8 +37,8 @@ def tile_moe_mod_silu_kernel(
         keep = ctx.enter_context(tc.tile_pool(name="keep", bufs=1))
         psum = ctx.enter_context(tc.psum_pool(name="psum", bufs=4))
 
-        def half_of(lst, h):
-            return lst[:, h * (HALF // 16) : (h + 1) * (HALF // 16)]
+        def entries(lst, piece):
+            return lst[:, piece.start // 16 : piece.stop // 16]
 
         def load_scale_rows(plane, rows):
             words = rows.bitcast(I32)
@@ -49,36 +53,38 @@ def tile_moe_mod_silu_kernel(
         xs = keep.tile([P, T], U8, name="xs", align_bytes=64)
         xw = keep.tile([P, T], U32, name="xw", align_bytes=64)
         w1_raw = keep.tile([P, 2 * K], U8, name="w1_raw", align_bytes=64)
-        s1_raw = keep.tile([P, K], U8, name="s1_raw", align_bytes=64)
-        g1 = [keep.tile([P, HALF], F32, name="g1_%d" % h, align_bytes=64) for h in range(2)]
+        s1_raw = keep.tile([P, K], U8, name="s1_raw", tag="s1_raw", align_bytes=64)
+        s2_raw = keep.tile([P, K], U8, name="s2_raw", align_bytes=64)
+        w2_raw = keep.tile([P, K], U32, name="w2_raw", align_bytes=64)
+        g1 = keep.tile([P, S], F32, name="g1", tag="g1", align_bytes=64)
         g2 = keep.tile([P, S], F32, name="g2")
-        res = {t: keep.tile([P, T], F32, name="res%d" % t) for t in ORDER}
-        z1 = [keep.tile([P, T], F32, name="z1_%d" % b) for b in range(2)]
+        res = {t: keep.tile([P, T], F32, name="res%d" % t, tag="res%d" % t, align_bytes=64) for t in ORDER}
+        z1 = {b: keep.tile([P, T], F32, name="z1_%d" % b, tag="z1_%d" % b) for b in (0, 2)}
         z2 = [keep.tile([P, T], F32, name="z2_%d" % b) for b in range(2)]
 
-        nc.vector.memset(z1[1][:], 0.0)
+        nc.vector.memset(z1[2][:], 0.0)
         nc.vector.memset(z1[0][:], 0.0)
-        nc.scalar.activation(z2[0][:], z1[1][:], SILU)
-        nc.scalar.copy(z2[1][:], z1[1][:])
+        nc.scalar.activation(z2[0][:], z1[2][:], SILU)
+        nc.scalar.copy(z2[1][:], z1[2][:])
 
         nc.sync.dma_start(idx1[:], offs)
         load_scale_rows(xs, x_scales[0])
+        nc.sync.dma_start(out=w1_raw[:].bitcast(I32), in_=w1_words[0].bitcast(I32))
         nc.sync.dma_start(out=xw[:].bitcast(I32), in_=x_words[0].rearrange("p t d -> p (t d)").bitcast(I32))
         load_scale_rows(s1_raw, w1_scales[0])
-        nc.sync.dma_start(out=w1_raw[:].bitcast(I32), in_=w1_words[0].bitcast(I32))
         for h in range(2):
-            nc.sync.dma_start(out=g1[h][:], in_=gate1[:, h * HALF : (h + 1) * HALF])
+            nc.sync.dma_start(out=g1[:, h * HALF : (h + 1) * HALF], in_=gate1[:, h * HALF : (h + 1) * HALF])
         xr_rows = xr.rearrange("(p t) w -> t p w", t=PACK)
         out_rows = out.rearrange("(p t) w -> t p w", t=PACK)
         for t in ORDER:
             nc.sync.dma_start(out=res[t][:], in_=xr_rows[t])
         nc.sync.dma_start(idx2[:], offs2)
+        load_scale_rows(s2_raw, w2_scales[0])
         nc.sync.dma_start(out=g2[:], in_=gate2)
+        nc.sync.dma_start(out=w2_raw[:].bitcast(I32), in_=w2_words[0].rearrange("p n d -> p (n d)").bitcast(I32))
 
         w1 = keep.tile([P, 2 * K], U8, name="w1", align_bytes=64)
         s1 = keep.tile([P, K], U8, name="s1", align_bytes=64)
-        w2 = keep.tile([P, K], U32, name="w2", align_bytes=64)
-        s2 = keep.tile([P, K], U8, name="s2", align_bytes=64)
 
         def by_plane(ap):
             return ap.rearrange("p (m t) -> p t m", t=PACK)
@@ -87,97 +93,101 @@ def tile_moe_mod_silu_kernel(
             return ap.rearrange("p (t m) -> p t m", t=PACK)
 
         gs = keep.tile([P, S], U8, name="gs", align_bytes=64)
-        gw = [keep.tile([P, HALF], U32, name="gw%d" % h, align_bytes=64) for h in range(2)]
+        gw = keep.tile([P, S], U32, name="gw", align_bytes=64)
         nc.vector.tensor_copy(gs[:], xs[:].indirect(idx1[:]))
         nc.vector.tensor_copy(as_planes(w1[:].bitcast(U16)), by_plane(w1_raw[:].bitcast(U16)))
         nc.gpsimd.tensor_copy(as_planes(s1[:]), by_plane(s1_raw[:]))
-        for h in range(2):
-            nc.vector.tensor_copy(gw[h][:], xw[:].indirect(half_of(idx1, h)))
+        z1[1] = keep.tile([P, T], F32, name="z1_1", tag="s1_raw", align_bytes=64)
+        nc.gpsimd.memset(z1[1][:], 0.0)
+        for piece in PIECES:
+            nc.vector.tensor_copy(gw[:, piece], xw[:].indirect(entries(idx1, piece)))
 
-        def products(name, lhs, lhs_scale, rhs, rhs_scale):
-            ys = {}
-            for t in ORDER:
-                y = keep.tile([P, S], F32, name="%s%d" % (name, t), tag="y%d" % t)
-                for h in range(2):
+        def products(name, tags, lhs, lhs_scale, rhs, rhs_scale):
+            ys = []
+            for n, t in enumerate(ORDER):
+                y = keep.tile([P, S], F32, name="%s%d" % (name, t), tag=tags[n], align_bytes=64)
+                for piece in PIECES if n == 0 else HALVES:
+                    width = piece.stop - piece.start
                     acc = psum.tile([P, HALF], F32, name="acc")
                     nc.tensor.matmul_mx(
-                        out=acc[:], lhsT=lhs(t), lhsT_scale=lhs_scale[:, t * P : (t + 1) * P],
-                        rhs=rhs[h][:].bitcast(FP8X4), rhs_scale=rhs_scale(h), start=True, stop=True,
+                        out=acc[:, :width], lhsT=lhs(t), lhsT_scale=lhs_scale[:, t * P : (t + 1) * P],
+                        rhs=rhs[:, piece].bitcast(FP8X4), rhs_scale=rhs_scale[:, piece], start=True, stop=True,
                     )
-                    nc.scalar.activation(y[:, h * HALF : (h + 1) * HALF], acc[:], SILU)
-                ys[t] = y
+                    nc.scalar.activation(y[:, piece], acc[:, :width], SILU)
+                ys.append(y)
             return ys
 
-        def gate_half(eng, y, gate, h):
-            cols = slice(h * HALF, (h + 1) * HALF)
-            eng.tensor_tensor(y[:, cols], y[:, cols], gate(h), MULT)
-
-        def gate_whole(y, gate):
-            for h in range(2):
-                gate_half(nc.gpsimd, y, gate, h)
-
-        def layer(ys, gate, z, idx, add, after_gates):
-            y = [ys[t] for t in ORDER]
-            gate_half(nc.vector, y[0], gate, 0)
-            gate_half(nc.gpsimd, y[0], gate, 1)
-            for h in range(2):
-                nc.vector.tensor_copy(z[0][:].indirect(half_of(idx, h)), y[0][:, h * HALF : (h + 1) * HALF])
-            gate_whole(y[1], gate)
-            gate_whole(y[2], gate)
+        def layer(y, tag_last, gate, z, idx, add, after_adds):
+            for k, piece in enumerate(PIECES):
+                eng = nc.vector if k == 0 else nc.gpsimd
+                eng.tensor_tensor(y[0][:, piece], y[0][:, piece], gate[:, piece], MULT)
+                nc.vector.tensor_copy(z[0][:].indirect(entries(idx, piece)), y[0][:, piece])
+            nc.gpsimd.tensor_tensor(y[1][:], y[1][:], gate[:], MULT)
+            yg2 = keep.tile([P, S], F32, name="yg2", tag="yg2")
+            nc.gpsimd.tensor_tensor(yg2[:], y[2][:], gate[:], MULT)
             nc.vector.tensor_copy(z[1][:].indirect(idx[:]), y[1][:])
             add(0)
-            gate_whole(y[3], gate)
-            nc.vector.tensor_copy(z[0][:].indirect(idx[:]), y[2][:])
+            yg3 = keep.tile([P, S], F32, name="yg3", tag=tag_last, align_bytes=64)
+            nc.gpsimd.tensor_tensor(yg3[:], y[3][:], gate[:], MULT)
+            nc.vector.tensor_copy(z[2][:].indirect(idx[:]), yg2[:])
             add(1)
-            after_gates()
             add(2)
-            nc.vector.tensor_copy(z[1][:].indirect(idx[:]), y[3][:])
+            after_adds()
+            nc.vector.tensor_copy(z[0][:].indirect(idx[:]), yg3[:])
             add(3)
 
-        y1 = products("y1", lambda t: w1[:, 2 * P * t : 2 * P * (t + 1)].bitcast(FP4X4), s1, gw,
-                      lambda h: gs[:, h * HALF : (h + 1) * HALF])
-        grouped = [keep.tile([P, HALF, PACK], BF16, name="grouped%d" % h, align_bytes=64) for h in range(2)]
+        def sum_tile(n, tags):
+            return keep.tile([P, T], F32, name="sum%d" % n, tag=tags[2 + n], align_bytes=64)
+
+        y1 = products("y1", TAGS1, lambda t: w1[:, 2 * P * t : 2 * P * (t + 1)].bitcast(FP4X4), s1, gw, gs)
+        grouped = keep.tile([P, S, PACK], BF16, name="grouped", align_bytes=64)
 
         def add1(n):
             t = ORDER[n]
             if n < 3:
-                nc.gpsimd.tensor_tensor(res[t][:], res[t][:], z1[n % 2][:], ADD)
+                total = sum_tile(n, TAGS1)
+                nc.gpsimd.tensor_tensor(total[:], res[t][:], z1[n % 3][:], ADD)
+                res[t] = total
                 rb = keep.tile([P, T], BF16, name="rb%d" % t, tag="win" if n == 0 else "rb%d" % t)
                 nc.scalar.copy(rb[:], res[t][:])
-                for h in range(2):
-                    nc.scalar.activation(grouped[h][:, :, t], rb[:].indirect(half_of(idx2, h)), COPY)
+                for piece in HALVES:
+                    nc.scalar.activation(grouped[:, piece, t], rb[:].indirect(entries(idx2, piece)), COPY)
             else:
                 last = keep.tile([P, T], F32, name="last", tag="win")
-                nc.vector.tensor_tensor(last[:], res[t][:], z1[n % 2][:], ADD)
+                nc.vector.tensor_tensor(last[:], res[t][:], z1[n % 3][:], ADD)
                 res[t] = last
 
+        held = {}
+
         def second_weights():
-            w2_raw = keep.tile([P, K], U32, name="w2_raw", tag="g1_0", align_bytes=64)
-            s2_raw = keep.tile([P, K], U8, name="s2_raw", tag="g1_1", align_bytes=64)
-            nc.sync.dma_start(out=w2_raw[:].bitcast(I32), in_=w2_words[0].rearrange("p n d -> p (n d)").bitcast(I32))
-            load_scale_rows(s2_raw, w2_scales[0])
-            nc.gpsimd.tensor_copy(as_planes(w2[:]), by_plane(w2_raw[:]))
-            nc.gpsimd.tensor_copy(as_planes(s2[:]), by_plane(s2_raw[:]))
+            held["s2"] = keep.tile([P, K], U8, name="s2", tag="g1", align_bytes=64)
+            nc.gpsimd.tensor_copy(as_planes(held["s2"][:]), by_plane(s2_raw[:]))
+            held["w2"] = keep.tile([P, K], U32, name="w2", tag="res%d" % ORDER[2], align_bytes=64)
+            nc.gpsimd.tensor_copy(as_planes(held["w2"][:]), by_plane(w2_raw[:]))
+            z2.append(keep.tile([P, T], F32, name="z2_2", tag="z1_2"))
+            nc.gpsimd.memset(z2[2][:], 0.0)
 
-        layer(y1, lambda h: g1[h][:], z1, idx1, add1, second_weights)
-        codes = [keep.tile([P, HALF], U32, name="codes%d" % h, align_bytes=64) for h in range(2)]
-        scales = [keep.tile([P, HALF], U8, name="scales%d" % h, align_bytes=64) for h in range(2)]
-        for h in range(2):
-            nc.vector.tensor_copy(grouped[h][:, :, ORDER[3]], res[ORDER[3]][:].indirect(half_of(idx2, h)))
-            nc.vector.quantize_mx(out=codes[h][:].bitcast(FP8X4), scales=scales[h][:],
-                                  in_=grouped[h][:].rearrange("p s t -> p (s t)"))
+        layer(y1, "res%d" % ORDER[0], g1, z1, idx1, add1, second_weights)
+        codes = keep.tile([P, S], U32, name="codes", align_bytes=64)
+        scales = keep.tile([P, S], U8, name="scales", align_bytes=64)
+        for piece in HALVES:
+            nc.vector.tensor_copy(grouped[:, piece, ORDER[3]], res[ORDER[3]][:].indirect(entries(idx2, piece)))
+        for piece in PIECES:
+            nc.vector.quantize_mx(out=codes[:, piece].bitcast(FP8X4), scales=scales[:, piece],
+                                  in_=grouped[:, piece, :].rearrange("p s t -> p (s t)"))
 
-        y2 = products("y2", lambda t: w2[:, P * t : P * (t + 1)].bitcast(FP8X4), s2, codes, lambda h: scales[h][:])
+        y2 = products("y2", TAGS2, lambda t: held["w2"][:, P * t : P * (t + 1)].bitcast(FP8X4), held["s2"], codes, scales)
 
         def add2(n):
             t = ORDER[n]
             if n < 3:
-                nc.gpsimd.tensor_tensor(res[t][:], res[t][:], z2[n % 2][:], ADD)
-                nc.sync.dma_start(out=out_rows[t], in_=res[t][:])
+                total = sum_tile(n, TAGS2)
+                nc.gpsimd.tensor_tensor(total[:], res[t][:], z2[n % 3][:], ADD)
+                nc.sync.dma_start(out=out_rows[t], in_=total[:])
             else:
                 for c in range(4):
                     cols = slice(c * HALF, (c + 1) * HALF)
-                    nc.vector.tensor_tensor(res[t][:, cols], res[t][:, cols], z2[n % 2][:, cols], ADD)
-                    nc.sync.dma_start(out=out_rows[t][:, cols], in_=res[t][:, cols])
+                    nc.vector.tensor_tensor(res[t][:, cols], res[t][:, cols], z2[n % 3][:, cols], ADD)
+                    nc.scalar.dma_start(out=out_rows[t][:, cols], in_=res[t][:, cols])
 
-        layer(y2, lambda h: g2[:, h * HALF : (h + 1) * HALF], z2, idx2, add2, lambda: None)
+        layer(y2, TAGS1[2], g2, z2, idx2, add2, lambda: None)

@@ -5,7 +5,7 @@ import concourse.mybir as mybir
 K, T, S = 512, 2048, 1024
 P = 128
 PACK = 4
-HALF = 512
+BANK = 512
 FLOPS = 2 * 2 * K * K * S
 
 F32 = mybir.dt.float32
@@ -21,11 +21,16 @@ COPY = mybir.ActivationFunctionType.Copy
 MULT = mybir.AluOpType.mult
 ADD = mybir.AluOpType.add
 
-ORDER = (2, 0, 1, 3)
-HALVES = (slice(0, 512), slice(512, 1024))
-PIECES = (slice(0, 256), slice(256, 512), slice(512, 1024))
-TAGS1 = ("y0", "y1", "slot_a", "slot_b", "res%d" % ORDER[1])
-TAGS2 = ("y0", "y1", "slot_c", "slot_d", "slot_b")
+A, B, C, D = 0, 2, 3, 1
+P0, P1, P2 = slice(0, 256), slice(256, 512), slice(512, 1024)
+ALL = slice(0, 1024)
+TOKEN_HALVES = (slice(0, 1024), slice(1024, 2048))
+THIRD_CUTS = (slice(0, 1024), slice(1024, 1664), slice(1664, 2048))
+TAIL = (slice(0, 512), slice(512, 1152), slice(1152, 1792), slice(1792, 2048))
+
+
+def width(piece):
+    return piece.stop - piece.start
 
 
 def tile_moe_mod_silu_kernel(
@@ -35,7 +40,10 @@ def tile_moe_mod_silu_kernel(
     with ExitStack() as ctx:
         lists = ctx.enter_context(tc.tile_pool(name="lists", bufs=1))
         keep = ctx.enter_context(tc.tile_pool(name="keep", bufs=1))
-        psum = ctx.enter_context(tc.psum_pool(name="psum", bufs=4))
+        psum = ctx.enter_context(tc.psum_pool(name="psum", bufs=8))
+
+        def tile(name, cols, dtype, tag=None):
+            return keep.tile([P, cols], dtype, name=name, tag=tag or name, align_bytes=64)
 
         def entries(lst, piece):
             return lst[:, piece.start // 16 : piece.stop // 16]
@@ -48,146 +56,192 @@ def tile_moe_mod_silu_kernel(
                     in_=words[4 * q : 4 * (q + 1), :].partition_broadcast(8),
                 )
 
+        def planes_of(ap, e):
+            return ap.rearrange("p (m u e) -> p e u m", u=2, e=2)[:, e]
+
+        def as_two(ap):
+            return ap.rearrange("p (u m) -> p u m", u=2)
+
         idx1 = lists.tile([P, S // 16], U16, name="idx1")
         idx2 = lists.tile([P, S // 16], U16, name="idx2")
-        xs = keep.tile([P, T], U8, name="xs", align_bytes=64)
-        xw = keep.tile([P, T], U32, name="xw", align_bytes=64)
-        w1_raw = keep.tile([P, 2 * K], U8, name="w1_raw", align_bytes=64)
-        s1_raw = keep.tile([P, K], U8, name="s1_raw", tag="s1_raw", align_bytes=64)
-        s2_raw = keep.tile([P, K], U8, name="s2_raw", align_bytes=64)
-        w2_raw = keep.tile([P, K], U32, name="w2_raw", align_bytes=64)
-        g1 = keep.tile([P, S], F32, name="g1", tag="g1", align_bytes=64)
-        g2 = keep.tile([P, S], F32, name="g2")
-        res = {t: keep.tile([P, T], F32, name="res%d" % t, tag="res%d" % t, align_bytes=64) for t in ORDER}
-        z1 = {b: keep.tile([P, T], F32, name="z1_%d" % b, tag="z1_%d" % b) for b in (0, 2)}
-        z2 = [keep.tile([P, T], F32, name="z2_%d" % b) for b in range(2)]
+        xs = tile("xs", T, U8)
+        xw = tile("xw", T, U32)
+        w1_raw = tile("w1_raw", 2 * K, U8)
+        s1_raw = tile("s1_raw", K, U8)
+        w2_raw = tile("w2_raw", K, U32)
+        s2_raw = tile("s2_raw", K, U8)
+        g1 = tile("g1", S, F32)
+        g2 = tile("g2", S, F32)
+        xres = {t: tile("xr%d" % t, T, F32) for t in (C, D)}
+        xhalf = {t: [tile("xr%d_%d" % (t, h), T // 2, F32) for h in range(2)] for t in (A, B)}
 
-        nc.vector.memset(z1[2][:], 0.0)
-        nc.vector.memset(z1[0][:], 0.0)
-        nc.scalar.activation(z2[0][:], z1[2][:], SILU)
-        nc.scalar.copy(z2[1][:], z1[2][:])
+        zero = tile("zero", 16, F32)
+        nc.vector.memset(zero[:], 0.0)
+        zeros = zero[:, 0:1].to_broadcast([P, T])
+        z1 = {A: tile("z1a", T, F32), B: tile("z1b", T, F32)}
+        nc.vector.memset(z1[A][:], 0.0)
+        nc.scalar.activation(z1[B][:], zeros, SILU)
 
+        xr_rows = xr.rearrange("(p t) w -> t p w", t=PACK)
+        out_rows = out.rearrange("(p t) w -> t p w", t=PACK)
         nc.sync.dma_start(idx1[:], offs)
         load_scale_rows(xs, x_scales[0])
         nc.sync.dma_start(out=w1_raw[:].bitcast(I32), in_=w1_words[0].bitcast(I32))
         nc.sync.dma_start(out=xw[:].bitcast(I32), in_=x_words[0].rearrange("p t d -> p (t d)").bitcast(I32))
         load_scale_rows(s1_raw, w1_scales[0])
-        for h in range(2):
-            nc.sync.dma_start(out=g1[:, h * HALF : (h + 1) * HALF], in_=gate1[:, h * HALF : (h + 1) * HALF])
-        xr_rows = xr.rearrange("(p t) w -> t p w", t=PACK)
-        out_rows = out.rearrange("(p t) w -> t p w", t=PACK)
-        for t in ORDER:
-            nc.sync.dma_start(out=res[t][:], in_=xr_rows[t])
+        for piece in (slice(0, 512), P2):
+            nc.sync.dma_start(out=g1[:, piece], in_=gate1[:, piece])
+        for t in (A, B):
+            for half, cols in zip(xhalf[t], TOKEN_HALVES):
+                nc.sync.dma_start(out=half[:], in_=xr_rows[t][:, cols])
         nc.sync.dma_start(idx2[:], offs2)
-        load_scale_rows(s2_raw, w2_scales[0])
-        nc.sync.dma_start(out=g2[:], in_=gate2)
         nc.sync.dma_start(out=w2_raw[:].bitcast(I32), in_=w2_words[0].rearrange("p n d -> p (n d)").bitcast(I32))
+        load_scale_rows(s2_raw, w2_scales[0])
+        nc.sync.dma_start(out=xres[C][:], in_=xr_rows[C])
+        nc.sync.dma_start(out=xres[D][:], in_=xr_rows[D])
+        nc.sync.dma_start(out=g2[:], in_=gate2)
 
-        w1 = keep.tile([P, 2 * K], U8, name="w1", align_bytes=64)
-        s1 = keep.tile([P, K], U8, name="s1", align_bytes=64)
-
-        def by_plane(ap):
-            return ap.rearrange("p (m t) -> p t m", t=PACK)
-
-        def as_planes(ap):
-            return ap.rearrange("p (t m) -> p t m", t=PACK)
-
-        gs = keep.tile([P, S], U8, name="gs", align_bytes=64)
-        gw = keep.tile([P, S], U32, name="gw", align_bytes=64)
+        gs = tile("gs", S, U8)
+        gw = tile("gw", S, U32)
+        w1 = tile("w1", 2 * K, U8)
+        s1 = {t: tile("s1_%d" % t, P, U8) for t in (A, B)}
+        s1_odd = tile("s1_odd", 2 * P, U8)
         nc.vector.tensor_copy(gs[:], xs[:].indirect(idx1[:]))
-        nc.vector.tensor_copy(as_planes(w1[:].bitcast(U16)), by_plane(w1_raw[:].bitcast(U16)))
-        nc.gpsimd.tensor_copy(as_planes(s1[:]), by_plane(s1_raw[:]))
-        z1[1] = keep.tile([P, T], F32, name="z1_1", tag="s1_raw", align_bytes=64)
-        nc.gpsimd.memset(z1[1][:], 0.0)
-        for piece in PIECES:
+        nc.vector.tensor_copy(
+            w1[:].bitcast(U16).rearrange("p (e u m) -> p e u m", e=2, u=2),
+            w1_raw[:].bitcast(U16).rearrange("p (m u e) -> p e u m", u=2, e=2),
+        )
+        nc.vector.tensor_copy(gw[:, P0], xw[:].indirect(entries(idx1, P0)))
+        for t in (A, B):
+            nc.gpsimd.tensor_copy(s1[t][:], planes_of(s1_raw[:], 0)[:, t // 2])
+        for piece in (P1, P2):
             nc.vector.tensor_copy(gw[:, piece], xw[:].indirect(entries(idx1, piece)))
+        nc.vector.tensor_copy(as_two(s1_odd[:]), planes_of(s1_raw[:], 1))
 
-        def products(name, tags, lhs, lhs_scale, rhs, rhs_scale):
-            ys = []
-            for n, t in enumerate(ORDER):
-                y = keep.tile([P, S], F32, name="%s%d" % (name, t), tag=tags[n], align_bytes=64)
-                for piece in PIECES if n == 0 else HALVES:
-                    width = piece.stop - piece.start
-                    acc = psum.tile([P, HALF], F32, name="acc")
-                    nc.tensor.matmul_mx(
-                        out=acc[:, :width], lhsT=lhs(t), lhsT_scale=lhs_scale[:, t * P : (t + 1) * P],
-                        rhs=rhs[:, piece].bitcast(FP8X4), rhs_scale=rhs_scale[:, piece], start=True, stop=True,
-                    )
-                    nc.scalar.activation(y[:, piece], acc[:, :width], SILU)
-                ys.append(y)
-            return ys
+        def product(y, cols, lhs, lhs_scale, rhs, rhs_scale):
+            acc = psum.tile([P, BANK], F32, name="acc")
+            n = width(cols)
+            nc.tensor.matmul_mx(out=acc[:, :n], lhsT=lhs, lhsT_scale=lhs_scale, rhs=rhs, rhs_scale=rhs_scale, start=True, stop=True)
+            nc.scalar.activation(y[:, cols], acc[:, :n], SILU)
 
-        def layer(y, tag_last, gate, z, idx, add, after_adds):
-            for k, piece in enumerate(PIECES):
-                eng = nc.vector if k == 0 else nc.gpsimd
-                eng.tensor_tensor(y[0][:, piece], y[0][:, piece], gate[:, piece], MULT)
-                nc.vector.tensor_copy(z[0][:].indirect(entries(idx, piece)), y[0][:, piece])
-            nc.gpsimd.tensor_tensor(y[1][:], y[1][:], gate[:], MULT)
-            yg2 = keep.tile([P, S], F32, name="yg2", tag="yg2")
-            nc.gpsimd.tensor_tensor(yg2[:], y[2][:], gate[:], MULT)
-            nc.vector.tensor_copy(z[1][:].indirect(idx[:]), y[1][:])
-            add(0)
-            yg3 = keep.tile([P, S], F32, name="yg3", tag=tag_last, align_bytes=64)
-            nc.gpsimd.tensor_tensor(yg3[:], y[3][:], gate[:], MULT)
-            nc.vector.tensor_copy(z[2][:].indirect(idx[:]), yg2[:])
-            add(1)
-            add(2)
-            after_adds()
-            nc.vector.tensor_copy(z[0][:].indirect(idx[:]), yg3[:])
-            add(3)
+        def first_product(t, piece, parts):
+            e, u = t % 2, t // 2
+            y = tile("y1_%d_%d" % (t, piece.start), width(piece), F32)
+            for part in parts:
+                product(
+                    y, slice(part.start - piece.start, part.stop - piece.start),
+                    w1[:, 2 * P * (2 * e + u) : 2 * P * (2 * e + u + 1)].bitcast(FP4X4), s1_odd[:, u * P : (u + 1) * P] if e else s1[t][:],
+                    gw[:, part].bitcast(FP8X4), gs[:, part],
+                )
+            return y
 
-        def sum_tile(n, tags):
-            return keep.tile([P, T], F32, name="sum%d" % n, tag=tags[2 + n], align_bytes=64)
+        steps1 = [(A, piece, (piece,)) for piece in (P0, P1, P2)] + [(t, ALL, (slice(0, 512), P2)) for t in (B, C, D)]
+        ys = [first_product(t, piece, parts) for t, piece, parts in steps1]
+        z1[C] = tile("z1c", T, F32, tag="gw")
+        z1[D] = z1[A]
+        z2 = {A: tile("z2a", T, F32, tag="gs"), B: tile("z2b", T, F32), C: tile("z2c", T, F32)}
+        z2[D] = z2[A]
+        for z in (z1[C], z2[A]):
+            nc.scalar.copy(z[:], zeros)
+        for t in (B, C):
+            nc.sync.dma_start(out=z2[t][:], in_=z2[A][:])
 
-        y1 = products("y1", TAGS1, lambda t: w1[:, 2 * P * t : 2 * P * (t + 1)].bitcast(FP4X4), s1, gw, gs)
-        grouped = keep.tile([P, S, PACK], BF16, name="grouped", align_bytes=64)
+        def gated(y, gate, piece, name, tag=None):
+            dst = tile(name, width(piece), F32, tag=tag)
+            nc.gpsimd.tensor_tensor(dst[:], y[:], gate[:, piece], MULT)
+            return dst
 
-        def add1(n):
-            t = ORDER[n]
-            if n < 3:
-                total = sum_tile(n, TAGS1)
-                nc.gpsimd.tensor_tensor(total[:], res[t][:], z1[n % 3][:], ADD)
-                res[t] = total
-                rb = keep.tile([P, T], BF16, name="rb%d" % t, tag="win" if n == 0 else "rb%d" % t)
-                nc.scalar.copy(rb[:], res[t][:])
-                for piece in HALVES:
-                    nc.scalar.activation(grouped[:, piece, t], rb[:].indirect(entries(idx2, piece)), COPY)
-            else:
-                last = keep.tile([P, T], F32, name="last", tag="win")
-                nc.vector.tensor_tensor(last[:], res[t][:], z1[n % 3][:], ADD)
-                res[t] = last
+        ys = [gated(y, g1, piece, "g1_%d_%d" % (t, piece.start)) for y, (t, piece, parts) in zip(ys[:5], steps1)] + ys[5:]
+        for y, (t, piece, parts) in zip(ys[:5], steps1[:5]):
+            nc.vector.tensor_copy(z1[t][:].indirect(entries(idx1, piece)), y[:])
 
-        held = {}
+        grouped = {piece.start: keep.tile([P, width(piece), PACK], BF16, name="grouped%d" % piece.start, tag="grouped%d" % piece.start, align_bytes=64)
+                   for piece in (P0, P1, P2)}
+        res = {}
 
-        def second_weights():
-            held["s2"] = keep.tile([P, K], U8, name="s2", tag="g1", align_bytes=64)
-            nc.gpsimd.tensor_copy(as_planes(held["s2"][:]), by_plane(s2_raw[:]))
-            held["w2"] = keep.tile([P, K], U32, name="w2", tag="res%d" % ORDER[2], align_bytes=64)
-            nc.gpsimd.tensor_copy(as_planes(held["w2"][:]), by_plane(w2_raw[:]))
-            z2.append(keep.tile([P, T], F32, name="z2_2", tag="z1_2"))
-            nc.gpsimd.memset(z2[2][:], 0.0)
+        def rounded(t, tag, cuts):
+            rb = tile("rb%d" % t, T, BF16, tag=tag)
+            for cols in cuts:
+                nc.scalar.copy(rb[:, cols], res[t][:, cols])
+            return rb
 
-        layer(y1, "res%d" % ORDER[0], g1, z1, idx1, add1, second_weights)
-        codes = keep.tile([P, S], U32, name="codes", align_bytes=64)
-        scales = keep.tile([P, S], U8, name="scales", align_bytes=64)
-        for piece in HALVES:
-            nc.vector.tensor_copy(grouped[:, piece, ORDER[3]], res[ORDER[3]][:].indirect(entries(idx2, piece)))
-        for piece in PIECES:
-            nc.vector.quantize_mx(out=codes[:, piece].bitcast(FP8X4), scales=scales[:, piece],
-                                  in_=grouped[:, piece, :].rearrange("p s t -> p (s t)"))
+        def scalar_gather(rb, t, piece):
+            nc.scalar.activation(grouped[piece.start][:, :, t], rb[:].indirect(entries(idx2, piece)), COPY)
 
-        y2 = products("y2", TAGS2, lambda t: held["w2"][:, P * t : P * (t + 1)].bitcast(FP8X4), held["s2"], codes, scales)
+        def first_sum(t, tag, rb_tag, cuts):
+            res[t] = tile("res%d" % t, T, F32, tag=tag)
+            for cols in cuts:
+                h = cols.start // (T // 2)
+                src = xres[t][:, cols] if t in xres else xhalf[t][h][:, cols.start - h * (T // 2) : cols.stop - h * (T // 2)]
+                nc.gpsimd.tensor_tensor(res[t][:, cols], src, z1[t][:, cols], ADD)
+            rb = rounded(t, rb_tag, cuts)
+            for piece in (P0, P1, P2):
+                scalar_gather(rb, t, piece)
 
-        def add2(n):
-            t = ORDER[n]
-            if n < 3:
-                total = sum_tile(n, TAGS2)
-                nc.gpsimd.tensor_tensor(total[:], res[t][:], z2[n % 3][:], ADD)
-                nc.sync.dma_start(out=out_rows[t], in_=total[:])
-            else:
-                for c in range(4):
-                    cols = slice(c * HALF, (c + 1) * HALF)
-                    nc.vector.tensor_tensor(res[t][:, cols], res[t][:, cols], z2[n % 3][:, cols], ADD)
-                    nc.scalar.dma_start(out=out_rows[t][:, cols], in_=res[t][:, cols])
+        def permuted(raw, dtype, name, tag):
+            dst = tile(name, K, dtype, tag=tag)
+            nc.vector.tensor_copy(dst[:].rearrange("p (t m) -> p t m", t=PACK), raw[:].rearrange("p (m t) -> p t m", t=PACK))
+            return dst
 
-        layer(y2, TAGS1[2], g2, z2, idx2, add2, lambda: None)
+        first_sum(A, "y1_%d_0" % B, "rb_a", THIRD_CUTS)
+        last = gated(ys[5], g1, ALL, "g1_last", "xr%d_0" % A)
+        nc.vector.tensor_copy(z1[D][:].indirect(idx1[:]), last[:])
+        first_sum(B, "xr%d_1" % A, "rb_b", THIRD_CUTS)
+        first_sum(C, "rb_a", "rb_c", THIRD_CUTS)
+        res[D] = tile("res%d" % D, T, F32, tag="xr%d" % C)
+        for cols in TOKEN_HALVES:
+            nc.vector.tensor_tensor(res[D][:, cols], xres[D][:, cols], z1[D][:, cols], ADD)
+
+        codes, scales = {}, {}
+
+        def quantise(piece, tag):
+            codes[piece.start] = tile("codes%d" % piece.start, width(piece), U32, tag=tag)
+            scales[piece.start] = tile("scales%d" % piece.start, width(piece), U8)
+            nc.vector.quantize_mx(out=codes[piece.start][:].bitcast(FP8X4), scales=scales[piece.start][:],
+                                  in_=grouped[piece.start][:].rearrange("p s t -> p (s t)"))
+
+        nc.vector.tensor_copy(grouped[0][:, :, D], res[D][:].indirect(entries(idx2, P0)))
+        w2 = permuted(w2_raw, U32, "w2", "xr%d" % D)
+        s2 = permuted(s2_raw, U8, "s2", "z1a")
+        quantise(P0, None)
+        for piece in (P1, P2):
+            nc.vector.tensor_copy(grouped[piece.start][:, :, D], res[D][:].indirect(entries(idx2, piece)))
+        quantise(P1, None)
+
+        def second_product(t, piece, parts):
+            y = tile("y2_%d_%d" % (t, piece.start), width(piece), F32)
+            for part in parts:
+                product(
+                    y, slice(part.start - piece.start, part.stop - piece.start),
+                    w2[:, t * P : (t + 1) * P].bitcast(FP8X4), s2[:, t * P : (t + 1) * P],
+                    codes[part.start][:].bitcast(FP8X4), scales[part.start][:],
+                )
+            return t, piece, y
+
+        def second_gated(steps):
+            return [(t, piece, gated(y, g2, piece, "g2_%d_%d" % (t, piece.start))) for t, piece, y in steps]
+
+        def scatter2(t, piece, y):
+            nc.vector.tensor_copy(z2[t][:].indirect(entries(idx2, piece)), y[:])
+
+        early = second_gated([second_product(t, piece, (piece,)) for piece in (P0, P1) for t in (A, B)])
+        scatter2(*early[0])
+        quantise(P2, "y2_%d_0" % A)
+        late = [second_product(t, P2, (P2,)) for t in (A, B)] + [second_product(t, ALL, (P0, P1, P2)) for t in (C, D)]
+        late = second_gated(late)
+        for step in early[1:] + late[:3]:
+            scatter2(*step)
+
+        def second_sum(t, tag, cuts):
+            total = tile("total%d" % t, T, F32, tag=tag)
+            for cols in cuts:
+                nc.gpsimd.tensor_tensor(total[:, cols], res[t][:, cols], z2[t][:, cols], ADD)
+                nc.sync.dma_start(out=out_rows[t][:, cols], in_=total[:, cols])
+
+        second_sum(A, "y2_%d_0" % C, TOKEN_HALVES)
+        scatter2(*late[3])
+        second_sum(B, "y1_%d_0" % B, TOKEN_HALVES)
+        second_sum(C, "xr%d_1" % A, THIRD_CUTS)
+        for cols in TAIL:
+            nc.vector.tensor_tensor(res[D][:, cols], res[D][:, cols], z2[D][:, cols], ADD)
+            nc.scalar.dma_start(out=out_rows[D][:, cols], in_=res[D][:, cols])

@@ -25,7 +25,8 @@ A, B, C, D = 0, 2, 3, 1
 P0, P1, P2 = slice(0, 256), slice(256, 512), slice(512, 1024)
 ALL = slice(0, 1024)
 TOKEN_HALVES = (slice(0, 1024), slice(1024, 2048))
-THIRD_CUTS = (slice(0, 1024), slice(1024, 1664), slice(1664, 2048))
+THIRD_CUTS = (slice(0, 1408), slice(1408, 2048))
+WHOLE = (slice(0, 2048),)
 TAIL = (slice(0, 512), slice(512, 1152), slice(1152, 1792), slice(1792, 2048))
 
 
@@ -56,12 +57,6 @@ def tile_moe_mod_silu_kernel(
                     in_=words[4 * q : 4 * (q + 1), :].partition_broadcast(8),
                 )
 
-        def planes_of(ap, e):
-            return ap.rearrange("p (m u e) -> p e u m", u=2, e=2)[:, e]
-
-        def as_two(ap):
-            return ap.rearrange("p (u m) -> p u m", u=2)
-
         idx1 = lists.tile([P, S // 16], U16, name="idx1")
         idx2 = lists.tile([P, S // 16], U16, name="idx2")
         xs = tile("xs", T, U8)
@@ -76,11 +71,16 @@ def tile_moe_mod_silu_kernel(
         xhalf = {t: [tile("xr%d_%d" % (t, h), T // 2, F32) for h in range(2)] for t in (A, B)}
 
         zero = tile("zero", 16, F32)
-        nc.vector.memset(zero[:], 0.0)
+        nc.gpsimd.memset(zero[:], 0.0)
         zeros = zero[:, 0:1].to_broadcast([P, T])
-        z1 = {A: tile("z1a", T, F32), B: tile("z1b", T, F32)}
-        nc.vector.memset(z1[A][:], 0.0)
-        nc.scalar.activation(z1[B][:], zeros, SILU)
+        z1 = {A: tile("z1a", T, F32), B: tile("z1b", T, F32), C: tile("z1c", T, F32)}
+        z1[D] = z1[A]
+        z2 = {A: tile("z2a", T, F32)}
+        z2[D] = z2[A]
+        for t in (A, B):
+            nc.gpsimd.memset(z1[t][:], 0.0)
+        nc.scalar.activation(z1[C][:], zeros, SILU)
+        nc.scalar.copy(z2[A][:], zeros)
 
         xr_rows = xr.rearrange("(p t) w -> t p w", t=PACK)
         out_rows = out.rearrange("(p t) w -> t p w", t=PACK)
@@ -104,19 +104,20 @@ def tile_moe_mod_silu_kernel(
         gs = tile("gs", S, U8)
         gw = tile("gw", S, U32)
         w1 = tile("w1", 2 * K, U8)
-        s1 = {t: tile("s1_%d" % t, P, U8) for t in (A, B)}
-        s1_odd = tile("s1_odd", 2 * P, U8)
+        s1_first = tile("s1_first", P, U8)
+        s1_rest = tile("s1_rest", 3 * P, U8)
+        s1 = {t: s1_rest[:, (t - 1) * P : t * P] if t else s1_first[:] for t in range(PACK)}
         nc.vector.tensor_copy(gs[:], xs[:].indirect(idx1[:]))
         nc.vector.tensor_copy(
             w1[:].bitcast(U16).rearrange("p (e u m) -> p e u m", e=2, u=2),
             w1_raw[:].bitcast(U16).rearrange("p (m u e) -> p e u m", u=2, e=2),
         )
         nc.vector.tensor_copy(gw[:, P0], xw[:].indirect(entries(idx1, P0)))
-        for t in (A, B):
-            nc.gpsimd.tensor_copy(s1[t][:], planes_of(s1_raw[:], 0)[:, t // 2])
+        s1_planes = s1_raw[:].rearrange("p (m t) -> p t m", t=PACK)
+        nc.gpsimd.tensor_copy(s1_first[:], s1_planes[:, 0])
+        nc.gpsimd.tensor_copy(s1_rest[:].rearrange("p (t m) -> p t m", t=3), s1_planes[:, 1:])
         for piece in (P1, P2):
             nc.vector.tensor_copy(gw[:, piece], xw[:].indirect(entries(idx1, piece)))
-        nc.vector.tensor_copy(as_two(s1_odd[:]), planes_of(s1_raw[:], 1))
 
         def product(y, cols, lhs, lhs_scale, rhs, rhs_scale):
             acc = psum.tile([P, BANK], F32, name="acc")
@@ -130,30 +131,25 @@ def tile_moe_mod_silu_kernel(
             for part in parts:
                 product(
                     y, slice(part.start - piece.start, part.stop - piece.start),
-                    w1[:, 2 * P * (2 * e + u) : 2 * P * (2 * e + u + 1)].bitcast(FP4X4), s1_odd[:, u * P : (u + 1) * P] if e else s1[t][:],
+                    w1[:, 2 * P * (2 * e + u) : 2 * P * (2 * e + u + 1)].bitcast(FP4X4), s1[t],
                     gw[:, part].bitcast(FP8X4), gs[:, part],
                 )
             return y
-
-        steps1 = [(A, piece, (piece,)) for piece in (P0, P1, P2)] + [(t, ALL, (slice(0, 512), P2)) for t in (B, C, D)]
-        ys = [first_product(t, piece, parts) for t, piece, parts in steps1]
-        z1[C] = tile("z1c", T, F32, tag="gw")
-        z1[D] = z1[A]
-        z2 = {A: tile("z2a", T, F32, tag="gs"), B: tile("z2b", T, F32), C: tile("z2c", T, F32)}
-        z2[D] = z2[A]
-        for z in (z1[C], z2[A]):
-            nc.scalar.copy(z[:], zeros)
-        for t in (B, C):
-            nc.sync.dma_start(out=z2[t][:], in_=z2[A][:])
 
         def gated(y, gate, piece, name, tag=None):
             dst = tile(name, width(piece), F32, tag=tag)
             nc.gpsimd.tensor_tensor(dst[:], y[:], gate[:, piece], MULT)
             return dst
 
-        ys = [gated(y, g1, piece, "g1_%d_%d" % (t, piece.start)) for y, (t, piece, parts) in zip(ys[:5], steps1)] + ys[5:]
-        for y, (t, piece, parts) in zip(ys[:5], steps1[:5]):
+        def scatter1(t, piece, y):
             nc.vector.tensor_copy(z1[t][:].indirect(entries(idx1, piece)), y[:])
+
+        halves = (slice(0, 512), P2)
+        steps1 = [(A, piece, first_product(A, piece, (piece,))) for piece in (P0, P1, P2)] + [(B, ALL, first_product(B, ALL, halves))]
+        steps1 = [(t, piece, gated(y, g1, piece, "g1_%d_%d" % (t, piece.start))) for t, piece, y in steps1]
+        third, fourth = [first_product(t, ALL, halves) for t in (C, D)]
+        for step in steps1 + [(C, ALL, gated(third, g1, ALL, "g1_third"))]:
+            scatter1(*step)
 
         grouped = {piece.start: keep.tile([P, width(piece), PACK], BF16, name="grouped%d" % piece.start, tag="grouped%d" % piece.start, align_bytes=64)
                    for piece in (P0, P1, P2)}
@@ -183,11 +179,12 @@ def tile_moe_mod_silu_kernel(
             nc.vector.tensor_copy(dst[:].rearrange("p (t m) -> p t m", t=PACK), raw[:].rearrange("p (m t) -> p t m", t=PACK))
             return dst
 
-        first_sum(A, "y1_%d_0" % B, "rb_a", THIRD_CUTS)
-        last = gated(ys[5], g1, ALL, "g1_last", "xr%d_0" % A)
-        nc.vector.tensor_copy(z1[D][:].indirect(idx1[:]), last[:])
-        first_sum(B, "xr%d_1" % A, "rb_b", THIRD_CUTS)
+        first_sum(A, "y1_%d_0" % B, "rb_a", TOKEN_HALVES)
+        scatter1(D, ALL, gated(fourth, g1, ALL, "g1_last", "xr%d_0" % A))
+        first_sum(B, "xr%d_1" % A, "rb_b", TOKEN_HALVES)
         first_sum(C, "rb_a", "rb_c", THIRD_CUTS)
+        z2[B] = tile("z2b", T, F32, tag="z1c")
+        nc.gpsimd.memset(z2[B][:], 0.0)
         res[D] = tile("res%d" % D, T, F32, tag="xr%d" % C)
         for cols in TOKEN_HALVES:
             nc.vector.tensor_tensor(res[D][:, cols], xres[D][:, cols], z1[D][:, cols], ADD)
@@ -206,7 +203,6 @@ def tile_moe_mod_silu_kernel(
         quantise(P0, None)
         for piece in (P1, P2):
             nc.vector.tensor_copy(grouped[piece.start][:, :, D], res[D][:].indirect(entries(idx2, piece)))
-        quantise(P1, None)
 
         def second_product(t, piece, parts):
             y = tile("y2_%d_%d" % (t, piece.start), width(piece), F32)
@@ -224,10 +220,14 @@ def tile_moe_mod_silu_kernel(
         def scatter2(t, piece, y):
             nc.vector.tensor_copy(z2[t][:].indirect(entries(idx2, piece)), y[:])
 
-        early = second_gated([second_product(t, piece, (piece,)) for piece in (P0, P1) for t in (A, B)])
+        early = second_gated([second_product(t, P0, (P0,)) for t in (A, B)])
         scatter2(*early[0])
-        quantise(P2, "y2_%d_0" % A)
+        quantise(P1, "y2_%d_0" % A)
+        quantise(P2, "y2_%d_0" % B)
+        early = early + second_gated([second_product(t, P1, (P1,)) for t in (A, B)])
         late = [second_product(t, P2, (P2,)) for t in (A, B)] + [second_product(t, ALL, (P0, P1, P2)) for t in (C, D)]
+        z2[C] = tile("z2c", T, F32, tag="y2_%d_0" % B)
+        nc.scalar.copy(z2[C][:], zeros)
         late = second_gated(late)
         for step in early[1:] + late[:3]:
             scatter2(*step)
@@ -238,9 +238,9 @@ def tile_moe_mod_silu_kernel(
                 nc.gpsimd.tensor_tensor(total[:, cols], res[t][:, cols], z2[t][:, cols], ADD)
                 nc.sync.dma_start(out=out_rows[t][:, cols], in_=total[:, cols])
 
-        second_sum(A, "y2_%d_0" % C, TOKEN_HALVES)
+        second_sum(A, "y2_%d_0" % C, WHOLE)
         scatter2(*late[3])
-        second_sum(B, "y1_%d_0" % B, TOKEN_HALVES)
+        second_sum(B, "y1_%d_0" % B, WHOLE)
         second_sum(C, "xr%d_1" % A, THIRD_CUTS)
         for cols in TAIL:
             nc.vector.tensor_tensor(res[D][:, cols], res[D][:, cols], z2[D][:, cols], ADD)

@@ -1,6 +1,7 @@
 from contextlib import ExitStack
 
 import concourse.mybir as mybir
+from concourse.masks import make_identity
 
 K, T, S = 512, 2048, 1024
 P = 128
@@ -27,7 +28,6 @@ ALL = slice(0, 1024)
 TOKEN_HALVES = (slice(0, 1024), slice(1024, 2048))
 THIRD_CUTS = (slice(0, 1408), slice(1408, 2048))
 WHOLE = (slice(0, 2048),)
-TAIL = (slice(0, 512), slice(512, 1152), slice(1152, 1792), slice(1792, 2048))
 
 
 def width(piece):
@@ -41,7 +41,8 @@ def tile_moe_mod_silu_kernel(
     with ExitStack() as ctx:
         lists = ctx.enter_context(tc.tile_pool(name="lists", bufs=1))
         keep = ctx.enter_context(tc.tile_pool(name="keep", bufs=1))
-        psum = ctx.enter_context(tc.psum_pool(name="psum", bufs=8))
+        psum = ctx.enter_context(tc.psum_pool(name="psum", bufs=4))
+        sums = ctx.enter_context(tc.psum_pool(name="sums", bufs=1))
 
         def tile(name, cols, dtype, tag=None):
             return keep.tile([P, cols], dtype, name=name, tag=tag or name, align_bytes=64)
@@ -67,16 +68,14 @@ def tile_moe_mod_silu_kernel(
         s2_raw = tile("s2_raw", K, U8)
         g1 = tile("g1", S, F32)
         g2 = tile("g2", S, F32)
-        xres = {t: tile("xr%d" % t, T, F32) for t in (C, D)}
-        xhalf = {t: [tile("xr%d_%d" % (t, h), T // 2, F32) for h in range(2)] for t in (A, B)}
+        xres = {t: tile("xr%d" % t, T, F32) for t in (A, B, C, D)}
 
         zero = tile("zero", 16, F32)
         nc.gpsimd.memset(zero[:], 0.0)
         zeros = zero[:, 0:1].to_broadcast([P, T])
         z1 = {A: tile("z1a", T, F32), B: tile("z1b", T, F32), C: tile("z1c", T, F32)}
-        z1[D] = z1[A]
+        z1[D] = z1[B]
         z2 = {A: tile("z2a", T, F32)}
-        z2[D] = z2[A]
         for t in (A, B):
             nc.gpsimd.memset(z1[t][:], 0.0)
         nc.scalar.activation(z1[C][:], zeros, SILU)
@@ -91,12 +90,11 @@ def tile_moe_mod_silu_kernel(
         load_scale_rows(s1_raw, w1_scales[0])
         for piece in (slice(0, 512), P2):
             nc.sync.dma_start(out=g1[:, piece], in_=gate1[:, piece])
-        for t in (A, B):
-            for half, cols in zip(xhalf[t], TOKEN_HALVES):
-                nc.sync.dma_start(out=half[:], in_=xr_rows[t][:, cols])
+        nc.sync.dma_start(out=xres[B][:], in_=xr_rows[B])
         nc.sync.dma_start(idx2[:], offs2)
         nc.sync.dma_start(out=w2_raw[:].bitcast(I32), in_=w2_words[0].rearrange("p n d -> p (n d)").bitcast(I32))
         load_scale_rows(s2_raw, w2_scales[0])
+        nc.sync.dma_start(out=xres[A][:], in_=xr_rows[A])
         nc.sync.dma_start(out=xres[C][:], in_=xr_rows[C])
         nc.sync.dma_start(out=xres[D][:], in_=xr_rows[D])
         nc.sync.dma_start(out=g2[:], in_=gate2)
@@ -116,11 +114,14 @@ def tile_moe_mod_silu_kernel(
         s1_planes = s1_raw[:].rearrange("p (m t) -> p t m", t=PACK)
         nc.gpsimd.tensor_copy(s1_first[:], s1_planes[:, 0])
         nc.gpsimd.tensor_copy(s1_rest[:].rearrange("p (t m) -> p t m", t=3), s1_planes[:, 1:])
+        ident = tile("ident", P, F32, tag="s1_raw")
+        ident16 = tile("ident16", P, BF16, tag="gs")
+        make_identity(nc, ident[:])
         for piece in (P1, P2):
             nc.vector.tensor_copy(gw[:, piece], xw[:].indirect(entries(idx1, piece)))
 
         def product(y, cols, lhs, lhs_scale, rhs, rhs_scale):
-            acc = psum.tile([P, BANK], F32, name="acc")
+            acc = psum.tile([P, BANK], F32, name="acc", tag="acc")
             n = width(cols)
             nc.tensor.matmul_mx(out=acc[:, :n], lhsT=lhs, lhsT_scale=lhs_scale, rhs=rhs, rhs_scale=rhs_scale, start=True, stop=True)
             nc.scalar.activation(y[:, cols], acc[:, :n], SILU)
@@ -146,10 +147,35 @@ def tile_moe_mod_silu_kernel(
 
         halves = (slice(0, 512), P2)
         steps1 = [(A, piece, first_product(A, piece, (piece,))) for piece in (P0, P1, P2)] + [(B, ALL, first_product(B, ALL, halves))]
-        steps1 = [(t, piece, gated(y, g1, piece, "g1_%d_%d" % (t, piece.start))) for t, piece, y in steps1]
+        nc.vector.tensor_tensor(steps1[0][2][:], steps1[0][2][:], g1[:, P0], MULT)
+        steps1 = steps1[:1] + [(t, piece, gated(y, g1, piece, "g1_%d_%d" % (t, piece.start))) for t, piece, y in steps1[1:]]
         third, fourth = [first_product(t, ALL, halves) for t in (C, D)]
-        for step in steps1 + [(C, ALL, gated(third, g1, ALL, "g1_third"))]:
+        nc.scalar.copy(ident16[:], ident[:])
+        z2[B] = tile("z2b", T, F32, tag="gw")
+        nc.scalar.copy(z2[B][:], zeros)
+        third, fourth = gated(third, g1, ALL, "g1_third"), gated(fourth, g1, ALL, "g1_fourth")
+        for step in steps1 + [(C, ALL, third)]:
             scatter1(*step)
+
+        def turned_onto(banks, src, first, last):
+            for c in range(T // P):
+                cols = slice(c * P, (c + 1) * P)
+                j = c % (BANK // P)
+                nc.tensor.matmul(banks[:, cols], lhsT=src[:, cols], rhs=ident[:], is_transpose=True,
+                                 start=first and j == 0, stop=last and j == BANK // P - 1)
+
+        def turned_back(banks, dst, dtype, identity, tag):
+            rows = tile(tag, T, dtype)
+            for b in range(T // BANK):
+                nc.scalar.copy(rows[:, b * BANK : (b + 1) * BANK], banks[:, b * BANK : (b + 1) * BANK])
+            for b in range(T // BANK):
+                back = psum.tile([P, BANK], dtype, name="back", tag="acc")
+                for j in range(BANK // P):
+                    nc.tensor.transpose(back[:, j * P : (j + 1) * P], rows[:, b * BANK + j * P : b * BANK + (j + 1) * P], identity[:])
+                nc.scalar.copy(dst[:, b * BANK : (b + 1) * BANK], back[:])
+
+        def sum_banks():
+            return sums.tile([P, T], F32, name="banks", tag="banks")
 
         grouped = {piece.start: keep.tile([P, width(piece), PACK], BF16, name="grouped%d" % piece.start, tag="grouped%d" % piece.start, align_bytes=64)
                    for piece in (P0, P1, P2)}
@@ -167,42 +193,55 @@ def tile_moe_mod_silu_kernel(
         def first_sum(t, tag, rb_tag, cuts):
             res[t] = tile("res%d" % t, T, F32, tag=tag)
             for cols in cuts:
-                h = cols.start // (T // 2)
-                src = xres[t][:, cols] if t in xres else xhalf[t][h][:, cols.start - h * (T // 2) : cols.stop - h * (T // 2)]
-                nc.gpsimd.tensor_tensor(res[t][:, cols], src, z1[t][:, cols], ADD)
+                nc.gpsimd.tensor_tensor(res[t][:, cols], xres[t][:, cols], z1[t][:, cols], ADD)
             rb = rounded(t, rb_tag, cuts)
             for piece in (P0, P1, P2):
                 scalar_gather(rb, t, piece)
 
         def permuted(raw, dtype, name, tag):
             dst = tile(name, K, dtype, tag=tag)
-            nc.vector.tensor_copy(dst[:].rearrange("p (t m) -> p t m", t=PACK), raw[:].rearrange("p (m t) -> p t m", t=PACK))
+            nc.gpsimd.tensor_copy(dst[:].rearrange("p (t m) -> p t m", t=PACK), raw[:].rearrange("p (m t) -> p t m", t=PACK))
             return dst
 
-        first_sum(A, "y1_%d_0" % B, "rb_a", TOKEN_HALVES)
-        scatter1(D, ALL, gated(fourth, g1, ALL, "g1_last", "xr%d_0" % A))
-        first_sum(B, "xr%d_1" % A, "rb_b", TOKEN_HALVES)
+        w2 = permuted(w2_raw, U32, "w2", "y1_%d_0" % C)
+        s2 = permuted(s2_raw, U8, "s2", "y1_%d_0" % D)
+        banks = sum_banks()
+        turned_onto(banks, xres[A], True, False)
+        turned_onto(banks, z1[A], False, True)
+        rb_first = tile("rb_a", T, BF16)
+        turned_back(banks, rb_first, BF16, ident16, "rows1")
+        for piece in (P0, P1, P2):
+            scalar_gather(rb_first, A, piece)
+        banks = sum_banks()
+        turned_onto(banks, xres[A], True, False)
+        turned_onto(banks, z1[A], False, False)
+        first_sum(B, "rows1", "rb_b", TOKEN_HALVES)
+        scatter1(D, ALL, fourth)
         first_sum(C, "rb_a", "rb_c", THIRD_CUTS)
-        z2[B] = tile("z2b", T, F32, tag="z1c")
-        nc.gpsimd.memset(z2[B][:], 0.0)
-        res[D] = tile("res%d" % D, T, F32, tag="xr%d" % C)
-        for cols in TOKEN_HALVES:
-            nc.vector.tensor_tensor(res[D][:, cols], xres[D][:, cols], z1[D][:, cols], ADD)
+        z2[C] = tile("z2c", T, F32, tag="z1c")
+        nc.gpsimd.memset(z2[C][:], 0.0)
+        res[D] = tile("res%d" % D, T, F32, tag="rb_b")
+        z2[D] = res[D]
+        nc.vector.tensor_tensor(res[D][:], xres[D][:], z1[D][:], ADD)
 
         codes, scales = {}, {}
 
-        def quantise(piece, tag):
-            codes[piece.start] = tile("codes%d" % piece.start, width(piece), U32, tag=tag)
+        def quantise(piece):
+            codes[piece.start] = tile("codes%d" % piece.start, width(piece), U32)
             scales[piece.start] = tile("scales%d" % piece.start, width(piece), U8)
             nc.vector.quantize_mx(out=codes[piece.start][:].bitcast(FP8X4), scales=scales[piece.start][:],
                                   in_=grouped[piece.start][:].rearrange("p s t -> p (s t)"))
 
-        nc.vector.tensor_copy(grouped[0][:, :, D], res[D][:].indirect(entries(idx2, P0)))
-        w2 = permuted(w2_raw, U32, "w2", "xr%d" % D)
-        s2 = permuted(s2_raw, U8, "s2", "z1a")
-        quantise(P0, None)
+        kept = tile("kept", S, F32)
+        for piece in (P0, P1):
+            nc.vector.tensor_copy(kept[:, piece], res[D][:].indirect(entries(idx2, piece)))
+        nc.vector.tensor_copy(grouped[P0.start][:, :, D], kept[:, P0])
+        quantise(P0)
+        nc.vector.tensor_copy(kept[:, P2], res[D][:].indirect(entries(idx2, P2)))
+        nc.vector.tensor_copy(grouped[P2.start][:, :, D], kept[:, P2])
+        nc.scalar.copy(grouped[P1.start][:, :, D], kept[:, P1])
         for piece in (P1, P2):
-            nc.vector.tensor_copy(grouped[piece.start][:, :, D], res[D][:].indirect(entries(idx2, piece)))
+            quantise(piece)
 
         def second_product(t, piece, parts):
             y = tile("y2_%d_%d" % (t, piece.start), width(piece), F32)
@@ -220,17 +259,15 @@ def tile_moe_mod_silu_kernel(
         def scatter2(t, piece, y):
             nc.vector.tensor_copy(z2[t][:].indirect(entries(idx2, piece)), y[:])
 
-        early = second_gated([second_product(t, P0, (P0,)) for t in (A, B)])
-        scatter2(*early[0])
-        quantise(P1, "y2_%d_0" % A)
-        quantise(P2, "y2_%d_0" % B)
-        early = early + second_gated([second_product(t, P1, (P1,)) for t in (A, B)])
-        late = [second_product(t, P2, (P2,)) for t in (A, B)] + [second_product(t, ALL, (P0, P1, P2)) for t in (C, D)]
-        z2[C] = tile("z2c", T, F32, tag="y2_%d_0" % B)
-        nc.scalar.copy(z2[C][:], zeros)
-        late = second_gated(late)
-        for step in early[1:] + late[:3]:
+        rest = slice(P1.start, S)
+        steps2 = [second_product(t, P0, (P0,)) for t in (A, B)] + [second_product(t, rest, (P1, P2)) for t in (A, B)]
+        steps2 = steps2 + [second_product(t, ALL, (P0, P1, P2)) for t in (C, D)]
+        nc.vector.tensor_tensor(steps2[0][2][:], steps2[0][2][:], g2[:, P0], MULT)
+        steps2 = steps2[:1] + second_gated(steps2[1:])
+        for step in steps2[:5]:
             scatter2(*step)
+        last = steps2[5][2]
+        nc.gpsimd.tensor_tensor(last[:], last[:], kept[:], ADD)
 
         def second_sum(t, tag, cuts):
             total = tile("total%d" % t, T, F32, tag=tag)
@@ -238,10 +275,12 @@ def tile_moe_mod_silu_kernel(
                 nc.gpsimd.tensor_tensor(total[:, cols], res[t][:, cols], z2[t][:, cols], ADD)
                 nc.sync.dma_start(out=out_rows[t][:, cols], in_=total[:, cols])
 
-        second_sum(A, "y2_%d_0" % C, WHOLE)
-        scatter2(*late[3])
-        second_sum(B, "y1_%d_0" % B, WHOLE)
-        second_sum(C, "xr%d_1" % A, THIRD_CUTS)
-        for cols in TAIL:
-            nc.vector.tensor_tensor(res[D][:, cols], res[D][:, cols], z2[D][:, cols], ADD)
+        turned_onto(banks, z2[A], False, True)
+        total = tile("total_a", T, F32)
+        turned_back(banks, total, F32, ident, "rows2")
+        nc.sync.dma_start(out=out_rows[A], in_=total[:])
+        second_sum(B, "y2_%d_0" % D, WHOLE)
+        scatter2(*steps2[5])
+        second_sum(C, "rows1", THIRD_CUTS)
+        for cols in TOKEN_HALVES:
             nc.scalar.dma_start(out=out_rows[D][:, cols], in_=res[D][:, cols])

@@ -161,13 +161,13 @@ def tile_moe_mod_silu_kernel(
             for c in range(T // P):
                 cols = slice(c * P, (c + 1) * P)
                 j = c % (BANK // P)
-                nc.tensor.matmul(banks[:, cols], lhsT=src[:, cols], rhs=ident[:], is_transpose=True,
+                nc.tensor.matmul(banks[c // (BANK // P)][:, j * P : (j + 1) * P], lhsT=src[:, cols], rhs=ident[:], is_transpose=True,
                                  start=first and j == 0, stop=last and j == BANK // P - 1)
 
         def turned_back(banks, dst, dtype, identity, tag):
             rows = tile(tag, T, dtype)
             for b in range(T // BANK):
-                nc.scalar.copy(rows[:, b * BANK : (b + 1) * BANK], banks[:, b * BANK : (b + 1) * BANK])
+                nc.scalar.copy(rows[:, b * BANK : (b + 1) * BANK], banks[b][:])
             for b in range(T // BANK):
                 back = psum.tile([P, BANK], dtype, name="back", tag="acc")
                 for j in range(BANK // P):
@@ -175,7 +175,7 @@ def tile_moe_mod_silu_kernel(
                 nc.scalar.copy(dst[:, b * BANK : (b + 1) * BANK], back[:])
 
         def sum_banks():
-            return sums.tile([P, T], F32, name="banks", tag="banks")
+            return [sums.tile([P, BANK], F32, name="sum%d" % b, tag="sum%d" % b) for b in range(T // BANK)]
 
         grouped = {piece.start: keep.tile([P, width(piece), PACK], BF16, name="grouped%d" % piece.start, tag="grouped%d" % piece.start, align_bytes=64)
                    for piece in (P0, P1, P2)}
@@ -220,7 +220,7 @@ def tile_moe_mod_silu_kernel(
         first_sum(C, "rb_a", "rb_c", THIRD_CUTS)
         z2[C] = tile("z2c", T, F32, tag="z1c")
         nc.gpsimd.memset(z2[C][:], 0.0)
-        res[D] = tile("res%d" % D, T, F32, tag="rb_b")
+        res[D] = tile("res%d" % D, T, F32, tag="xr%d" % C)
         z2[D] = res[D]
         nc.vector.tensor_tensor(res[D][:], xres[D][:], z1[D][:], ADD)
 
@@ -232,14 +232,14 @@ def tile_moe_mod_silu_kernel(
             nc.vector.quantize_mx(out=codes[piece.start][:].bitcast(FP8X4), scales=scales[piece.start][:],
                                   in_=grouped[piece.start][:].rearrange("p s t -> p (s t)"))
 
-        kept = tile("kept", S, F32)
-        for piece in (P0, P1):
+        kept = tile("kept", S, F32, tag="rb_b")
+        for piece in (P0, P1, P2):
             nc.vector.tensor_copy(kept[:, piece], res[D][:].indirect(entries(idx2, piece)))
-        nc.vector.tensor_copy(grouped[P0.start][:, :, D], kept[:, P0])
+        for piece in (P0, P1):
+            nc.scalar.copy(grouped[piece.start][:, :, D], kept[:, piece])
+        nc.scalar.copy(grouped[P2.start][:, :256, D], kept[:, 512:768])
         quantise(P0)
-        nc.vector.tensor_copy(kept[:, P2], res[D][:].indirect(entries(idx2, P2)))
-        nc.vector.tensor_copy(grouped[P2.start][:, :, D], kept[:, P2])
-        nc.scalar.copy(grouped[P1.start][:, :, D], kept[:, P1])
+        nc.vector.tensor_copy(grouped[P2.start][:, 256:, D], kept[:, 768:])
         for piece in (P1, P2):
             quantise(piece)
 
@@ -273,14 +273,14 @@ def tile_moe_mod_silu_kernel(
             total = tile("total%d" % t, T, F32, tag=tag)
             for cols in cuts:
                 nc.gpsimd.tensor_tensor(total[:, cols], res[t][:, cols], z2[t][:, cols], ADD)
-                nc.sync.dma_start(out=out_rows[t][:, cols], in_=total[:, cols])
+                nc.scalar.dma_start(out=out_rows[t][:, cols], in_=total[:, cols])
 
         turned_onto(banks, z2[A], False, True)
         total = tile("total_a", T, F32)
         turned_back(banks, total, F32, ident, "rows2")
-        nc.sync.dma_start(out=out_rows[A], in_=total[:])
+        nc.scalar.dma_start(out=out_rows[A], in_=total[:])
         second_sum(B, "y2_%d_0" % D, WHOLE)
         scatter2(*steps2[5])
         second_sum(C, "rows1", THIRD_CUTS)
         for cols in TOKEN_HALVES:
-            nc.scalar.dma_start(out=out_rows[D][:, cols], in_=res[D][:, cols])
+            nc.sync.dma_start(out=out_rows[D][:, cols], in_=res[D][:, cols])

@@ -235,9 +235,9 @@ def tile_moe_mod_silu_kernel(
         kept = tile("kept", S, F32, tag="rb_b")
         for piece in (P0, P1, P2):
             nc.vector.tensor_copy(kept[:, piece], res[D][:].indirect(entries(idx2, piece)))
-        for piece in (P0, P1):
-            nc.scalar.copy(grouped[piece.start][:, :, D], kept[:, piece])
+        nc.scalar.copy(grouped[P1.start][:, :, D], kept[:, P1])
         nc.scalar.copy(grouped[P2.start][:, :256, D], kept[:, 512:768])
+        nc.vector.tensor_copy(grouped[P0.start][:, :, D], kept[:, P0])
         quantise(P0)
         nc.vector.tensor_copy(grouped[P2.start][:, 256:, D], kept[:, 768:])
         for piece in (P1, P2):
@@ -262,8 +262,9 @@ def tile_moe_mod_silu_kernel(
         rest = slice(P1.start, S)
         steps2 = [second_product(t, P0, (P0,)) for t in (A, B)] + [second_product(t, rest, (P1, P2)) for t in (A, B)]
         steps2 = steps2 + [second_product(t, ALL, (P0, P1, P2)) for t in (C, D)]
-        nc.vector.tensor_tensor(steps2[0][2][:], steps2[0][2][:], g2[:, P0], MULT)
-        steps2 = steps2[:1] + second_gated(steps2[1:])
+        opening2 = tile("opening2", width(P0), F32)
+        nc.vector.tensor_tensor(opening2[:], steps2[0][2][:], g2[:, P0], MULT)
+        steps2 = [(A, P0, opening2), (B, P0, gated(steps2[1][2], g2, P0, "follower2", "y2_%d_0" % A))] + second_gated(steps2[2:])
         for step in steps2[:5]:
             scatter2(*step)
         last = steps2[5][2]

@@ -102,18 +102,17 @@ def tile_moe_mod_silu_kernel(
         gs = tile("gs", S, U8)
         gw = tile("gw", S, U32)
         w1 = tile("w1", 2 * K, U8)
-        s1_first = tile("s1_first", P, U8)
-        s1_rest = tile("s1_rest", 3 * P, U8)
-        s1 = {t: s1_rest[:, (t - 1) * P : t * P] if t else s1_first[:] for t in range(PACK)}
+        s1_pairs = [tile("s1_%d" % e, 2 * P, U8) for e in range(2)]
+        s1 = {t: s1_pairs[t % 2][:, t // 2 * P : (t // 2 + 1) * P] for t in range(PACK)}
         nc.vector.tensor_copy(gs[:], xs[:].indirect(idx1[:]))
         nc.vector.tensor_copy(
             w1[:].bitcast(U16).rearrange("p (e u m) -> p e u m", e=2, u=2),
             w1_raw[:].bitcast(U16).rearrange("p (m u e) -> p e u m", u=2, e=2),
         )
         nc.vector.tensor_copy(gw[:, P0], xw[:].indirect(entries(idx1, P0)))
-        s1_planes = s1_raw[:].rearrange("p (m t) -> p t m", t=PACK)
-        nc.gpsimd.tensor_copy(s1_first[:], s1_planes[:, 0])
-        nc.gpsimd.tensor_copy(s1_rest[:].rearrange("p (t m) -> p t m", t=3), s1_planes[:, 1:])
+        s1_planes = s1_raw[:].rearrange("p (m u e) -> p e u m", u=2, e=2)
+        for e in range(2):
+            nc.gpsimd.tensor_copy(s1_pairs[e][:].rearrange("p (u m) -> p u m", u=2), s1_planes[:, e])
         ident = tile("ident", P, F32, tag="s1_raw")
         ident16 = tile("ident16", P, BF16, tag="gs")
         make_identity(nc, ident[:])
@@ -146,9 +145,12 @@ def tile_moe_mod_silu_kernel(
             nc.vector.tensor_copy(z1[t][:].indirect(entries(idx1, piece)), y[:])
 
         halves = (slice(0, 512), P2)
-        steps1 = [(A, piece, first_product(A, piece, (piece,))) for piece in (P0, P1, P2)] + [(B, ALL, first_product(B, ALL, halves))]
-        nc.vector.tensor_tensor(steps1[0][2][:], steps1[0][2][:], g1[:, P0], MULT)
-        steps1 = steps1[:1] + [(t, piece, gated(y, g1, piece, "g1_%d_%d" % (t, piece.start))) for t, piece, y in steps1[1:]]
+        steps1 = [(t, piece, first_product(t, piece, parts)) for t, piece, parts in
+                  ((A, P0, (P0,)), (B, P0, (P0,)), (A, slice(256, S), (P1, P2)), (B, slice(256, S), (P1, P2)))]
+        opening1 = tile("opening1", width(P0), F32)
+        nc.vector.tensor_tensor(opening1[:], steps1[0][2][:], g1[:, P0], MULT)
+        steps1 = [(A, P0, opening1), (B, P0, gated(steps1[1][2], g1, P0, "follower1", "y1_%d_0" % A))] + [
+            (t, piece, gated(y, g1, piece, "g1_%d_%d" % (t, piece.start))) for t, piece, y in steps1[2:]]
         third, fourth = [first_product(t, ALL, halves) for t in (C, D)]
         nc.scalar.copy(ident16[:], ident[:])
         z2[B] = tile("z2b", T, F32, tag="gw")
@@ -215,9 +217,9 @@ def tile_moe_mod_silu_kernel(
         banks = sum_banks()
         turned_onto(banks, xres[A], True, False)
         turned_onto(banks, z1[A], False, False)
-        first_sum(B, "rows1", "rb_b", TOKEN_HALVES)
+        first_sum(B, "w2_raw", "rb_a", TOKEN_HALVES)
         scatter1(D, ALL, fourth)
-        first_sum(C, "rb_a", "rb_c", THIRD_CUTS)
+        first_sum(C, "z1a", "rb_c", THIRD_CUTS)
         z2[C] = tile("z2c", T, F32, tag="z1c")
         nc.gpsimd.memset(z2[C][:], 0.0)
         res[D] = tile("res%d" % D, T, F32, tag="xr%d" % C)
@@ -232,7 +234,7 @@ def tile_moe_mod_silu_kernel(
             nc.vector.quantize_mx(out=codes[piece.start][:].bitcast(FP8X4), scales=scales[piece.start][:],
                                   in_=grouped[piece.start][:].rearrange("p s t -> p (s t)"))
 
-        kept = tile("kept", S, F32, tag="rb_b")
+        kept = tile("kept", S, F32, tag="rb_a")
         for piece in (P0, P1, P2):
             nc.vector.tensor_copy(kept[:, piece], res[D][:].indirect(entries(idx2, piece)))
         nc.scalar.copy(grouped[P1.start][:, :, D], kept[:, P1])
@@ -282,6 +284,6 @@ def tile_moe_mod_silu_kernel(
         nc.scalar.dma_start(out=out_rows[A], in_=total[:])
         second_sum(B, "y2_%d_0" % D, WHOLE)
         scatter2(*steps2[5])
-        second_sum(C, "rows1", THIRD_CUTS)
+        second_sum(C, "w2_raw", THIRD_CUTS)
         for cols in TOKEN_HALVES:
             nc.sync.dma_start(out=out_rows[D][:, cols], in_=res[D][:, cols])

@@ -27,7 +27,7 @@ P0, P1, P2 = slice(0, 256), slice(256, 512), slice(512, 1024)
 ALL = slice(0, 1024)
 TOKEN_HALVES = (slice(0, 1024), slice(1024, 2048))
 THIRD_CUTS = (slice(0, 1408), slice(1408, 2048))
-WHOLE = (slice(0, 2048),)
+SECOND = (slice(0, 256), slice(256, 768), slice(768, 1024))
 
 
 def width(piece):
@@ -153,18 +153,19 @@ def tile_moe_mod_silu_kernel(
             (t, piece, gated(y, g1, piece, "g1_%d_%d" % (t, piece.start))) for t, piece, y in steps1[2:]]
         third, fourth = [first_product(t, ALL, halves) for t in (C, D)]
         nc.scalar.copy(ident16[:], ident[:])
-        z2[B] = tile("z2b", T, F32, tag="gw")
-        nc.scalar.copy(z2[B][:], zeros)
+        z2[D] = tile("z2d", T, F32, tag="gw")
+        z2[C] = tile("z2c", T, F32, tag="w1")
+        for t in (D, C):
+            nc.scalar.copy(z2[t][:], zeros)
         third, fourth = gated(third, g1, ALL, "g1_third"), gated(fourth, g1, ALL, "g1_fourth")
         for step in steps1 + [(C, ALL, third)]:
             scatter1(*step)
 
-        def turned_onto(banks, src, first, last):
-            for c in range(T // P):
-                cols = slice(c * P, (c + 1) * P)
-                j = c % (BANK // P)
-                nc.tensor.matmul(banks[c // (BANK // P)][:, j * P : (j + 1) * P], lhsT=src[:, cols], rhs=ident[:], is_transpose=True,
-                                 start=first and j == 0, stop=last and j == BANK // P - 1)
+        def turned_onto(banks, src, first, last, which=range(T // BANK)):
+            for b in which:
+                for j in range(BANK // P):
+                    nc.tensor.matmul(banks[b][:, j * P : (j + 1) * P], lhsT=src[:, b * BANK + j * P : b * BANK + (j + 1) * P], rhs=ident[:],
+                                     is_transpose=True, start=first and j == 0, stop=last and j == BANK // P - 1)
 
         def turned_back(banks, dst, dtype, identity, tag):
             rows = tile(tag, T, dtype)
@@ -180,7 +181,7 @@ def tile_moe_mod_silu_kernel(
             return [sums.tile([P, BANK], F32, name="sum%d" % b, tag="sum%d" % b) for b in range(T // BANK)]
 
         grouped = {piece.start: keep.tile([P, width(piece), PACK], BF16, name="grouped%d" % piece.start, tag="grouped%d" % piece.start, align_bytes=64)
-                   for piece in (P0, P1, P2)}
+                   for piece in SECOND}
         res = {}
 
         def rounded(t, tag, cuts):
@@ -197,7 +198,7 @@ def tile_moe_mod_silu_kernel(
             for cols in cuts:
                 nc.gpsimd.tensor_tensor(res[t][:, cols], xres[t][:, cols], z1[t][:, cols], ADD)
             rb = rounded(t, rb_tag, cuts)
-            for piece in (P0, P1, P2):
+            for piece in SECOND:
                 scalar_gather(rb, t, piece)
 
         def permuted(raw, dtype, name, tag):
@@ -206,25 +207,34 @@ def tile_moe_mod_silu_kernel(
             return dst
 
         w2 = permuted(w2_raw, U32, "w2", "y1_%d_0" % C)
-        s2 = permuted(s2_raw, U8, "s2", "y1_%d_0" % D)
+        s2_planes = s2_raw[:].rearrange("p (m t) -> p t m", t=PACK)
+        s2_early = tile("s2_early", C * P, U8, tag="y1_%d_0" % D)
+        nc.gpsimd.tensor_copy(s2_early[:].rearrange("p (t m) -> p t m", t=C), s2_planes[:, :C])
+        s2 = {t: s2_early[:, t * P : (t + 1) * P] for t in range(C)}
         banks = sum_banks()
         turned_onto(banks, xres[A], True, False)
         turned_onto(banks, z1[A], False, True)
         rb_first = tile("rb_a", T, BF16)
         turned_back(banks, rb_first, BF16, ident16, "rows1")
-        for piece in (P0, P1, P2):
+        for piece in SECOND:
             scalar_gather(rb_first, A, piece)
         banks = sum_banks()
-        turned_onto(banks, xres[A], True, False)
-        turned_onto(banks, z1[A], False, False)
+        for b in range(T // BANK):
+            turned_onto(banks, xres[A], True, False, (b,))
+            turned_onto(banks, z1[A], False, False, (b,))
         first_sum(B, "w2_raw", "rb_a", TOKEN_HALVES)
         scatter1(D, ALL, fourth)
-        first_sum(C, "z1a", "rb_c", THIRD_CUTS)
-        z2[C] = tile("z2c", T, F32, tag="z1c")
-        nc.gpsimd.memset(z2[C][:], 0.0)
-        res[D] = tile("res%d" % D, T, F32, tag="xr%d" % C)
-        z2[D] = res[D]
-        nc.vector.tensor_tensor(res[D][:], xres[D][:], z1[D][:], ADD)
+        rb_third = tile("rb_c", T, BF16, tag="xr%d" % A)
+        nc.gpsimd.tensor_tensor(rb_third[:], xres[C][:], z1[C][:], ADD)
+        for piece in SECOND:
+            scalar_gather(rb_third, C, piece)
+        s2[C] = tile("s2_late", P, U8, tag="z1a")[:]
+        nc.gpsimd.tensor_copy(s2[C], s2_planes[:, C])
+        z2[B] = res[B]
+        rb_last = tile("rb_d", T, BF16, tag="s2_raw")
+        nc.vector.tensor_tensor(rb_last[:], xres[D][:], z1[D][:], ADD)
+        for piece in SECOND:
+            scalar_gather(rb_last, D, piece)
 
         codes, scales = {}, {}
 
@@ -234,15 +244,9 @@ def tile_moe_mod_silu_kernel(
             nc.vector.quantize_mx(out=codes[piece.start][:].bitcast(FP8X4), scales=scales[piece.start][:],
                                   in_=grouped[piece.start][:].rearrange("p s t -> p (s t)"))
 
-        kept = tile("kept", S, F32, tag="rb_a")
-        for piece in (P0, P1, P2):
-            nc.vector.tensor_copy(kept[:, piece], res[D][:].indirect(entries(idx2, piece)))
-        nc.scalar.copy(grouped[P1.start][:, :, D], kept[:, P1])
-        nc.scalar.copy(grouped[P2.start][:, :256, D], kept[:, 512:768])
-        nc.vector.tensor_copy(grouped[P0.start][:, :, D], kept[:, P0])
-        quantise(P0)
-        nc.vector.tensor_copy(grouped[P2.start][:, 256:, D], kept[:, 768:])
-        for piece in (P1, P2):
+        kept = tile("kept", S, F32, tag="xr%d" % A)
+        nc.vector.tensor_copy(kept[:], res[B][:].indirect(idx2[:]))
+        for piece in SECOND:
             quantise(piece)
 
         def second_product(t, piece, parts):
@@ -250,7 +254,7 @@ def tile_moe_mod_silu_kernel(
             for part in parts:
                 product(
                     y, slice(part.start - piece.start, part.stop - piece.start),
-                    w2[:, t * P : (t + 1) * P].bitcast(FP8X4), s2[:, t * P : (t + 1) * P],
+                    w2[:, t * P : (t + 1) * P].bitcast(FP8X4), s2[t],
                     codes[part.start][:].bitcast(FP8X4), scales[part.start][:],
                 )
             return t, piece, y
@@ -262,28 +266,33 @@ def tile_moe_mod_silu_kernel(
             nc.vector.tensor_copy(z2[t][:].indirect(entries(idx2, piece)), y[:])
 
         rest = slice(P1.start, S)
-        steps2 = [second_product(t, P0, (P0,)) for t in (A, B)] + [second_product(t, rest, (P1, P2)) for t in (A, B)]
-        steps2 = steps2 + [second_product(t, ALL, (P0, P1, P2)) for t in (C, D)]
+        steps2 = [second_product(t, P0, SECOND[:1]) for t in (A, D)] + [second_product(t, rest, SECOND[1:]) for t in (A, D)]
+        steps2 = steps2 + [second_product(t, ALL, SECOND) for t in (C, B)]
         opening2 = tile("opening2", width(P0), F32)
         nc.vector.tensor_tensor(opening2[:], steps2[0][2][:], g2[:, P0], MULT)
-        steps2 = [(A, P0, opening2), (B, P0, gated(steps2[1][2], g2, P0, "follower2", "y2_%d_0" % A))] + second_gated(steps2[2:])
+        steps2 = [(A, P0, opening2), (D, P0, gated(steps2[1][2], g2, P0, "follower2", "y2_%d_0" % A))] + second_gated(steps2[2:])
         for step in steps2[:5]:
             scatter2(*step)
         last = steps2[5][2]
         nc.gpsimd.tensor_tensor(last[:], last[:], kept[:], ADD)
-
-        def second_sum(t, tag, cuts):
-            total = tile("total%d" % t, T, F32, tag=tag)
-            for cols in cuts:
-                nc.gpsimd.tensor_tensor(total[:, cols], res[t][:, cols], z2[t][:, cols], ADD)
-                nc.scalar.dma_start(out=out_rows[t][:, cols], in_=total[:, cols])
+        res[C] = tile("res%d" % C, T, F32, tag="y2_%d_0" % B)
+        nc.gpsimd.tensor_tensor(res[C][:], xres[C][:], z1[C][:], ADD)
 
         turned_onto(banks, z2[A], False, True)
         total = tile("total_a", T, F32)
         turned_back(banks, total, F32, ident, "rows2")
         nc.scalar.dma_start(out=out_rows[A], in_=total[:])
-        second_sum(B, "y2_%d_0" % D, WHOLE)
+        banks = sum_banks()
+        turned_onto(banks, xres[D], True, False)
+        turned_onto(banks, z1[D], False, False)
+        turned_onto(banks, z2[D], False, True)
+        total = tile("total_d", T, F32, tag="xr%d" % B)
+        turned_back(banks, total, F32, ident, "rows2")
+        nc.scalar.dma_start(out=out_rows[D], in_=total[:])
         scatter2(*steps2[5])
-        second_sum(C, "w2_raw", THIRD_CUTS)
+        total = tile("total_c", T, F32, tag="rows2")
+        for cols in THIRD_CUTS:
+            nc.gpsimd.tensor_tensor(total[:, cols], res[C][:, cols], z2[C][:, cols], ADD)
+            nc.scalar.dma_start(out=out_rows[C][:, cols], in_=total[:, cols])
         for cols in TOKEN_HALVES:
-            nc.sync.dma_start(out=out_rows[D][:, cols], in_=res[D][:, cols])
+            nc.sync.dma_start(out=out_rows[B][:, cols], in_=res[B][:, cols])

@@ -23,11 +23,12 @@ MULT = mybir.AluOpType.mult
 ADD = mybir.AluOpType.add
 
 A, B, C, D = 0, 2, 3, 1
-P0, P1, P2 = slice(0, 256), slice(256, 512), slice(512, 1024)
+P0, P1, P2 = slice(0, 256), slice(256, 768), slice(768, 1024)
 ALL = slice(0, 1024)
 TOKEN_HALVES = (slice(0, 1024), slice(1024, 2048))
 THIRD_CUTS = (slice(0, 1408), slice(1408, 2048))
-SECOND = (slice(0, 256), slice(256, 768), slice(768, 1024))
+SECOND = (P0, P1, P2)
+HALVES = (slice(0, 512), slice(512, 1024))
 
 
 def width(piece):
@@ -88,7 +89,7 @@ def tile_moe_mod_silu_kernel(
         nc.sync.dma_start(out=w1_raw[:].bitcast(I32), in_=w1_words[0].bitcast(I32))
         nc.sync.dma_start(out=xw[:].bitcast(I32), in_=x_words[0].rearrange("p t d -> p (t d)").bitcast(I32))
         load_scale_rows(s1_raw, w1_scales[0])
-        for piece in (slice(0, 512), P2):
+        for piece in HALVES:
             nc.sync.dma_start(out=g1[:, piece], in_=gate1[:, piece])
         nc.sync.dma_start(out=xres[B][:], in_=xr_rows[B])
         nc.sync.dma_start(idx2[:], offs2)
@@ -144,14 +145,13 @@ def tile_moe_mod_silu_kernel(
         def scatter1(t, piece, y):
             nc.vector.tensor_copy(z1[t][:].indirect(entries(idx1, piece)), y[:])
 
-        halves = (slice(0, 512), P2)
         steps1 = [(t, piece, first_product(t, piece, parts)) for t, piece, parts in
                   ((A, P0, (P0,)), (B, P0, (P0,)), (A, slice(256, S), (P1, P2)), (B, slice(256, S), (P1, P2)))]
         opening1 = tile("opening1", width(P0), F32)
         nc.vector.tensor_tensor(opening1[:], steps1[0][2][:], g1[:, P0], MULT)
         steps1 = [(A, P0, opening1), (B, P0, gated(steps1[1][2], g1, P0, "follower1", "y1_%d_0" % A))] + [
             (t, piece, gated(y, g1, piece, "g1_%d_%d" % (t, piece.start))) for t, piece, y in steps1[2:]]
-        third, fourth = [first_product(t, ALL, halves) for t in (C, D)]
+        third, fourth = [first_product(t, ALL, HALVES) for t in (C, D)]
         nc.scalar.copy(ident16[:], ident[:])
         z2[D] = tile("z2d", T, F32, tag="gw")
         z2[C] = tile("z2c", T, F32, tag="w1")

@@ -29,6 +29,7 @@ TOKEN_HALVES = (slice(0, 1024), slice(1024, 2048))
 THIRD_CUTS = (slice(0, 1408), slice(1408, 2048))
 SECOND = (P0, P1, P2)
 HALVES = (slice(0, 512), slice(512, 1024))
+HELD = (slice(0, 512), slice(512, 1024), slice(1024, 1408))
 
 
 def width(piece):
@@ -42,7 +43,7 @@ def tile_moe_mod_silu_kernel(
     with ExitStack() as ctx:
         lists = ctx.enter_context(tc.tile_pool(name="lists", bufs=1))
         keep = ctx.enter_context(tc.tile_pool(name="keep", bufs=1))
-        psum = ctx.enter_context(tc.psum_pool(name="psum", bufs=4))
+        psum = ctx.enter_context(tc.psum_pool(name="psum", bufs=1))
         sums = ctx.enter_context(tc.psum_pool(name="sums", bufs=1))
 
         def tile(name, cols, dtype, tag=None):
@@ -76,11 +77,11 @@ def tile_moe_mod_silu_kernel(
         zeros = zero[:, 0:1].to_broadcast([P, T])
         z1 = {A: tile("z1a", T, F32), B: tile("z1b", T, F32), C: tile("z1c", T, F32)}
         z1[D] = z1[B]
-        z2 = {A: tile("z2a", T, F32)}
+        z2 = {B: tile("z2b", T, F32)}
         for t in (A, B):
             nc.gpsimd.memset(z1[t][:], 0.0)
         nc.scalar.activation(z1[C][:], zeros, SILU)
-        nc.scalar.copy(z2[A][:], zeros)
+        nc.scalar.copy(z2[B][:], zeros)
 
         xr_rows = xr.rearrange("(p t) w -> t p w", t=PACK)
         out_rows = out.rearrange("(p t) w -> t p w", t=PACK)
@@ -91,13 +92,13 @@ def tile_moe_mod_silu_kernel(
         load_scale_rows(s1_raw, w1_scales[0])
         for piece in HALVES:
             nc.sync.dma_start(out=g1[:, piece], in_=gate1[:, piece])
-        nc.sync.dma_start(out=xres[B][:], in_=xr_rows[B])
+        nc.sync.dma_start(out=xres[D][:], in_=xr_rows[D])
         nc.sync.dma_start(idx2[:], offs2)
         nc.sync.dma_start(out=w2_raw[:].bitcast(I32), in_=w2_words[0].rearrange("p n d -> p (n d)").bitcast(I32))
         load_scale_rows(s2_raw, w2_scales[0])
         nc.sync.dma_start(out=xres[A][:], in_=xr_rows[A])
+        nc.sync.dma_start(out=xres[B][:], in_=xr_rows[B])
         nc.sync.dma_start(out=xres[C][:], in_=xr_rows[C])
-        nc.sync.dma_start(out=xres[D][:], in_=xr_rows[D])
         nc.sync.dma_start(out=g2[:], in_=gate2)
 
         gs = tile("gs", S, U8)
@@ -115,13 +116,15 @@ def tile_moe_mod_silu_kernel(
         for e in range(2):
             nc.gpsimd.tensor_copy(s1_pairs[e][:].rearrange("p (u m) -> p u m", u=2), s1_planes[:, e])
         ident = tile("ident", P, F32, tag="s1_raw")
-        ident16 = tile("ident16", P, BF16, tag="gs")
         make_identity(nc, ident[:])
         for piece in (P1, P2):
             nc.vector.tensor_copy(gw[:, piece], xw[:].indirect(entries(idx1, piece)))
 
+        turns = []
+
         def product(y, cols, lhs, lhs_scale, rhs, rhs_scale):
-            acc = psum.tile([P, BANK], F32, name="acc", tag="acc")
+            acc = psum.tile([P, BANK], F32, name="acc", tag="acc%d" % (len(turns) % 4))
+            turns.append(cols)
             n = width(cols)
             nc.tensor.matmul_mx(out=acc[:, :n], lhsT=lhs, lhsT_scale=lhs_scale, rhs=rhs, rhs_scale=rhs_scale, start=True, stop=True)
             nc.scalar.activation(y[:, cols], acc[:, :n], SILU)
@@ -152,11 +155,8 @@ def tile_moe_mod_silu_kernel(
         steps1 = [(A, P0, opening1), (B, P0, gated(steps1[1][2], g1, P0, "follower1", "y1_%d_0" % A))] + [
             (t, piece, gated(y, g1, piece, "g1_%d_%d" % (t, piece.start))) for t, piece, y in steps1[2:]]
         third, fourth = [first_product(t, ALL, HALVES) for t in (C, D)]
-        nc.scalar.copy(ident16[:], ident[:])
         z2[D] = tile("z2d", T, F32, tag="gw")
-        z2[C] = tile("z2c", T, F32, tag="w1")
-        for t in (D, C):
-            nc.scalar.copy(z2[t][:], zeros)
+        nc.scalar.copy(z2[D][:], zeros)
         third, fourth = gated(third, g1, ALL, "g1_third"), gated(fourth, g1, ALL, "g1_fourth")
         for step in steps1 + [(C, ALL, third)]:
             scatter1(*step)
@@ -167,37 +167,30 @@ def tile_moe_mod_silu_kernel(
                     nc.tensor.matmul(banks[b][:, j * P : (j + 1) * P], lhsT=src[:, b * BANK + j * P : b * BANK + (j + 1) * P], rhs=ident[:],
                                      is_transpose=True, start=first and j == 0, stop=last and j == BANK // P - 1)
 
-        def turned_back(banks, dst, dtype, identity, tag):
-            rows = tile(tag, T, dtype)
+        def turned_back(banks, dst, tag):
+            rows = tile(tag, T, F32)
             for b in range(T // BANK):
                 nc.scalar.copy(rows[:, b * BANK : (b + 1) * BANK], banks[b][:])
+            backs = []
             for b in range(T // BANK):
-                back = psum.tile([P, BANK], dtype, name="back", tag="acc")
+                back = psum.tile([P, BANK], F32, name="back", tag="acc%d" % b)
                 for j in range(BANK // P):
-                    nc.tensor.transpose(back[:, j * P : (j + 1) * P], rows[:, b * BANK + j * P : b * BANK + (j + 1) * P], identity[:])
+                    nc.tensor.transpose(back[:, j * P : (j + 1) * P], rows[:, b * BANK + j * P : b * BANK + (j + 1) * P], ident[:])
                 nc.scalar.copy(dst[:, b * BANK : (b + 1) * BANK], back[:])
+                backs.append(back)
+            return backs
 
         def sum_banks():
             return [sums.tile([P, BANK], F32, name="sum%d" % b, tag="sum%d" % b) for b in range(T // BANK)]
 
         grouped = {piece.start: keep.tile([P, width(piece), PACK], BF16, name="grouped%d" % piece.start, tag="grouped%d" % piece.start, align_bytes=64)
                    for piece in SECOND}
-        res = {}
-
-        def rounded(t, tag, cuts):
-            rb = tile("rb%d" % t, T, BF16, tag=tag)
-            for cols in cuts:
-                nc.scalar.copy(rb[:, cols], res[t][:, cols])
-            return rb
-
         def scalar_gather(rb, t, piece):
             nc.scalar.activation(grouped[piece.start][:, :, t], rb[:].indirect(entries(idx2, piece)), COPY)
 
-        def first_sum(t, tag, rb_tag, cuts):
-            res[t] = tile("res%d" % t, T, F32, tag=tag)
-            for cols in cuts:
-                nc.gpsimd.tensor_tensor(res[t][:, cols], xres[t][:, cols], z1[t][:, cols], ADD)
-            rb = rounded(t, rb_tag, cuts)
+        def first_sum(t, tag):
+            rb = tile("rb%d" % t, T, BF16, tag=tag)
+            nc.gpsimd.tensor_tensor(rb[:], xres[t][:], z1[t][:], ADD)
             for piece in SECOND:
                 scalar_gather(rb, t, piece)
 
@@ -207,45 +200,55 @@ def tile_moe_mod_silu_kernel(
             return dst
 
         w2 = permuted(w2_raw, U32, "w2", "y1_%d_0" % C)
-        s2_planes = s2_raw[:].rearrange("p (m t) -> p t m", t=PACK)
-        s2_early = tile("s2_early", C * P, U8, tag="y1_%d_0" % D)
-        nc.gpsimd.tensor_copy(s2_early[:].rearrange("p (t m) -> p t m", t=C), s2_planes[:, :C])
-        s2 = {t: s2_early[:, t * P : (t + 1) * P] for t in range(C)}
+        s2_all = permuted(s2_raw, U8, "s2", "y1_%d_0" % D)
+        s2 = {t: s2_all[:, t * P : (t + 1) * P] for t in range(PACK)}
+        z2[C] = tile("z2c", T, F32, tag="s2_raw")
+        nc.gpsimd.memset(z2[C][:], 0.0)
+        held_rows = tile("held_rows", T, F32)
+        for b, cols in enumerate(HELD):
+            turned = psum.tile([P, BANK], F32, name="turned", tag="acc%d" % b)
+            for j in range(width(cols) // P):
+                nc.tensor.transpose(turned[:, j * P : (j + 1) * P], xres[D][:, cols.start + j * P : cols.start + (j + 1) * P], ident[:])
+            nc.scalar.copy(held_rows[:, cols], turned[:, : width(cols)])
         banks = sum_banks()
         turned_onto(banks, xres[A], True, False)
         turned_onto(banks, z1[A], False, True)
+        res_a = tile("res_a", T, F32)
         rb_first = tile("rb_a", T, BF16)
-        turned_back(banks, rb_first, BF16, ident16, "rows1")
+        backs = turned_back(banks, rb_first, "rows1")
         for piece in SECOND:
             scalar_gather(rb_first, A, piece)
+        for b, back in enumerate(backs):
+            nc.scalar.copy(res_a[:, b * BANK : (b + 1) * BANK], back[:])
         banks = sum_banks()
-        for b in range(T // BANK):
-            turned_onto(banks, xres[A], True, False, (b,))
-            turned_onto(banks, z1[A], False, False, (b,))
-        first_sum(B, "w2_raw", "rb_a", TOKEN_HALVES)
+        turned_onto(banks, z1[B], True, False)
+        turned_onto(banks, xres[B], False, False)
+        held = []
+        for b, cols in enumerate(HELD):
+            held.append(psum.tile([P, BANK], F32, name="held", tag="acc%d" % b))
+            for j in range(width(cols) // P):
+                nc.tensor.transpose(held[b][:, j * P : (j + 1) * P], held_rows[:, cols.start + j * P : cols.start + (j + 1) * P], ident[:])
+        first_sum(B, "rows1")
         scatter1(D, ALL, fourth)
-        rb_third = tile("rb_c", T, BF16, tag="xr%d" % A)
-        nc.gpsimd.tensor_tensor(rb_third[:], xres[C][:], z1[C][:], ADD)
-        for piece in SECOND:
-            scalar_gather(rb_third, C, piece)
-        s2[C] = tile("s2_late", P, U8, tag="z1a")[:]
-        nc.gpsimd.tensor_copy(s2[C], s2_planes[:, C])
-        z2[B] = res[B]
-        rb_last = tile("rb_d", T, BF16, tag="s2_raw")
-        nc.vector.tensor_tensor(rb_last[:], xres[D][:], z1[D][:], ADD)
+        first_sum(C, "xr%d" % B)
+        z2[A] = res_a
+        rb_last = tile("rb_d", T, BF16, tag="held_rows")
+        for b, cols in enumerate(HELD):
+            nc.vector.tensor_tensor(rb_last[:, cols], held[b][:, : width(cols)], z1[D][:, cols], ADD)
+        rest = slice(HELD[-1].stop, T)
+        nc.gpsimd.tensor_tensor(rb_last[:, rest], xres[D][:, rest], z1[D][:, rest], ADD)
         for piece in SECOND:
             scalar_gather(rb_last, D, piece)
 
-        codes, scales = {}, {}
+        codes = tile("codes", S, U32)
+        scales = tile("scales", S, U8)
 
         def quantise(piece):
-            codes[piece.start] = tile("codes%d" % piece.start, width(piece), U32)
-            scales[piece.start] = tile("scales%d" % piece.start, width(piece), U8)
-            nc.vector.quantize_mx(out=codes[piece.start][:].bitcast(FP8X4), scales=scales[piece.start][:],
+            nc.vector.quantize_mx(out=codes[:, piece].bitcast(FP8X4), scales=scales[:, piece],
                                   in_=grouped[piece.start][:].rearrange("p s t -> p (s t)"))
 
-        kept = tile("kept", S, F32, tag="xr%d" % A)
-        nc.vector.tensor_copy(kept[:], res[B][:].indirect(idx2[:]))
+        kept = tile("kept", S, F32, tag="xr%d" % B)
+        nc.vector.tensor_copy(kept[:], res_a[:].indirect(idx2[:]))
         for piece in SECOND:
             quantise(piece)
 
@@ -255,7 +258,7 @@ def tile_moe_mod_silu_kernel(
                 product(
                     y, slice(part.start - piece.start, part.stop - piece.start),
                     w2[:, t * P : (t + 1) * P].bitcast(FP8X4), s2[t],
-                    codes[part.start][:].bitcast(FP8X4), scales[part.start][:],
+                    codes[:, part].bitcast(FP8X4), scales[:, part],
                 )
             return t, piece, y
 
@@ -266,33 +269,33 @@ def tile_moe_mod_silu_kernel(
             nc.vector.tensor_copy(z2[t][:].indirect(entries(idx2, piece)), y[:])
 
         rest = slice(P1.start, S)
-        steps2 = [second_product(t, P0, SECOND[:1]) for t in (A, D)] + [second_product(t, rest, SECOND[1:]) for t in (A, D)]
-        steps2 = steps2 + [second_product(t, ALL, SECOND) for t in (C, B)]
+        steps2 = [second_product(t, P0, SECOND[:1]) for t in (B, D)] + [second_product(t, rest, SECOND[1:]) for t in (B, D)]
+        steps2 = steps2 + [second_product(t, ALL, HALVES) for t in (C, A)]
         opening2 = tile("opening2", width(P0), F32)
         nc.vector.tensor_tensor(opening2[:], steps2[0][2][:], g2[:, P0], MULT)
-        steps2 = [(A, P0, opening2), (D, P0, gated(steps2[1][2], g2, P0, "follower2", "y2_%d_0" % A))] + second_gated(steps2[2:])
+        steps2 = [(B, P0, opening2), (D, P0, gated(steps2[1][2], g2, P0, "follower2", "y2_%d_0" % B))] + second_gated(steps2[2:])
         for step in steps2[:5]:
             scatter2(*step)
         last = steps2[5][2]
         nc.gpsimd.tensor_tensor(last[:], last[:], kept[:], ADD)
-        res[C] = tile("res%d" % C, T, F32, tag="y2_%d_0" % B)
-        nc.gpsimd.tensor_tensor(res[C][:], xres[C][:], z1[C][:], ADD)
+        res_c = tile("res_c", T, F32, tag="y2_%d_0" % A)
+        nc.gpsimd.tensor_tensor(res_c[:], xres[C][:], z1[C][:], ADD)
 
-        turned_onto(banks, z2[A], False, True)
-        total = tile("total_a", T, F32)
-        turned_back(banks, total, F32, ident, "rows2")
-        nc.scalar.dma_start(out=out_rows[A], in_=total[:])
+        turned_onto(banks, z2[B], False, True)
+        total = tile("total_b", T, F32, tag="xr%d" % A)
+        turned_back(banks, total, "rows2")
+        nc.scalar.dma_start(out=out_rows[B], in_=total[:])
         banks = sum_banks()
         turned_onto(banks, xres[D], True, False)
         turned_onto(banks, z1[D], False, False)
         turned_onto(banks, z2[D], False, True)
-        total = tile("total_d", T, F32, tag="xr%d" % B)
-        turned_back(banks, total, F32, ident, "rows2")
+        total = tile("total_d", T, F32, tag="rows1")
+        turned_back(banks, total, "rows2")
         nc.scalar.dma_start(out=out_rows[D], in_=total[:])
         scatter2(*steps2[5])
         total = tile("total_c", T, F32, tag="rows2")
         for cols in THIRD_CUTS:
-            nc.gpsimd.tensor_tensor(total[:, cols], res[C][:, cols], z2[C][:, cols], ADD)
+            nc.gpsimd.tensor_tensor(total[:, cols], res_c[:, cols], z2[C][:, cols], ADD)
             nc.scalar.dma_start(out=out_rows[C][:, cols], in_=total[:, cols])
         for cols in TOKEN_HALVES:
-            nc.sync.dma_start(out=out_rows[B][:, cols], in_=res[B][:, cols])
+            nc.sync.dma_start(out=out_rows[A][:, cols], in_=res_a[:, cols])

@@ -29,7 +29,7 @@ TOKEN_HALVES = (slice(0, 1024), slice(1024, 2048))
 THIRD_CUTS = (slice(0, 1408), slice(1408, 2048))
 SECOND = (P0, P1, P2)
 HALVES = (slice(0, 512), slice(512, 1024))
-HELD = (slice(0, 512), slice(512, 1024), slice(1024, 1408))
+HELD = (slice(0, 512), slice(512, 1024), slice(1024, 1536))
 
 
 def width(piece):
@@ -77,11 +77,12 @@ def tile_moe_mod_silu_kernel(
         zeros = zero[:, 0:1].to_broadcast([P, T])
         z1 = {A: tile("z1a", T, F32), B: tile("z1b", T, F32), C: tile("z1c", T, F32)}
         z1[D] = z1[B]
-        z2 = {B: tile("z2b", T, F32)}
-        for t in (A, B):
-            nc.gpsimd.memset(z1[t][:], 0.0)
-        nc.scalar.activation(z1[C][:], zeros, SILU)
-        nc.scalar.copy(z2[B][:], zeros)
+        z2 = {}
+        nc.gpsimd.memset(z1[A][:], 0.0)
+        ident = tile("ident", P, F32)
+        make_identity(nc, ident[:])
+        nc.scalar.activation(z1[B][:], zeros, SILU)
+        nc.scalar.copy(z1[C][:], zeros)
 
         xr_rows = xr.rearrange("(p t) w -> t p w", t=PACK)
         out_rows = out.rearrange("(p t) w -> t p w", t=PACK)
@@ -115,8 +116,6 @@ def tile_moe_mod_silu_kernel(
         s1_planes = s1_raw[:].rearrange("p (m u e) -> p e u m", u=2, e=2)
         for e in range(2):
             nc.gpsimd.tensor_copy(s1_pairs[e][:].rearrange("p (u m) -> p u m", u=2), s1_planes[:, e])
-        ident = tile("ident", P, F32, tag="s1_raw")
-        make_identity(nc, ident[:])
         for piece in (P1, P2):
             nc.vector.tensor_copy(gw[:, piece], xw[:].indirect(entries(idx1, piece)))
 
@@ -202,8 +201,8 @@ def tile_moe_mod_silu_kernel(
         w2 = permuted(w2_raw, U32, "w2", "y1_%d_0" % C)
         s2_all = permuted(s2_raw, U8, "s2", "y1_%d_0" % D)
         s2 = {t: s2_all[:, t * P : (t + 1) * P] for t in range(PACK)}
-        z2[C] = tile("z2c", T, F32, tag="s2_raw")
-        nc.gpsimd.memset(z2[C][:], 0.0)
+        z2[B] = tile("z2b", T, F32, tag="s2_raw")
+        nc.gpsimd.memset(z2[B][:], 0.0)
         held_rows = tile("held_rows", T, F32)
         for b, cols in enumerate(HELD):
             turned = psum.tile([P, BANK], F32, name="turned", tag="acc%d" % b)
@@ -271,6 +270,8 @@ def tile_moe_mod_silu_kernel(
         rest = slice(P1.start, S)
         steps2 = [second_product(t, P0, SECOND[:1]) for t in (B, D)] + [second_product(t, rest, SECOND[1:]) for t in (B, D)]
         steps2 = steps2 + [second_product(t, ALL, HALVES) for t in (C, A)]
+        z2[C] = tile("z2c", T, F32, tag="scales")
+        nc.scalar.copy(z2[C][:], zeros)
         opening2 = tile("opening2", width(P0), F32)
         nc.vector.tensor_tensor(opening2[:], steps2[0][2][:], g2[:, P0], MULT)
         steps2 = [(B, P0, opening2), (D, P0, gated(steps2[1][2], g2, P0, "follower2", "y2_%d_0" % B))] + second_gated(steps2[2:])

@@ -29,7 +29,7 @@ TOKEN_HALVES = (slice(0, 1024), slice(1024, 2048))
 THIRD_CUTS = (slice(0, 1408), slice(1408, 2048))
 SECOND = (P0, P1, P2)
 HALVES = (slice(0, 512), slice(512, 1024))
-HELD = (slice(0, 512), slice(512, 1024), slice(1024, 1536))
+HELD = (slice(0, 512), slice(512, 1024), slice(1024, 1408))
 
 
 def width(piece):
@@ -182,16 +182,15 @@ def tile_moe_mod_silu_kernel(
         def sum_banks():
             return [sums.tile([P, BANK], F32, name="sum%d" % b, tag="sum%d" % b) for b in range(T // BANK)]
 
-        grouped = {piece.start: keep.tile([P, width(piece), PACK], BF16, name="grouped%d" % piece.start, tag="grouped%d" % piece.start, align_bytes=64)
-                   for piece in SECOND}
+        grouped = keep.tile([P, S, PACK], BF16, name="grouped", align_bytes=64)
+
         def scalar_gather(rb, t, piece):
-            nc.scalar.activation(grouped[piece.start][:, :, t], rb[:].indirect(entries(idx2, piece)), COPY)
+            nc.scalar.activation(grouped[:, piece, t], rb[:].indirect(entries(idx2, piece)), COPY)
 
         def first_sum(t, tag):
             rb = tile("rb%d" % t, T, BF16, tag=tag)
             nc.gpsimd.tensor_tensor(rb[:], xres[t][:], z1[t][:], ADD)
-            for piece in SECOND:
-                scalar_gather(rb, t, piece)
+            scalar_gather(rb, t, ALL)
 
         def permuted(raw, dtype, name, tag):
             dst = tile(name, K, dtype, tag=tag)
@@ -215,8 +214,7 @@ def tile_moe_mod_silu_kernel(
         res_a = tile("res_a", T, F32)
         rb_first = tile("rb_a", T, BF16)
         backs = turned_back(banks, rb_first, "rows1")
-        for piece in SECOND:
-            scalar_gather(rb_first, A, piece)
+        scalar_gather(rb_first, A, ALL)
         for b, back in enumerate(backs):
             nc.scalar.copy(res_a[:, b * BANK : (b + 1) * BANK], back[:])
         banks = sum_banks()
@@ -244,7 +242,7 @@ def tile_moe_mod_silu_kernel(
 
         def quantise(piece):
             nc.vector.quantize_mx(out=codes[:, piece].bitcast(FP8X4), scales=scales[:, piece],
-                                  in_=grouped[piece.start][:].rearrange("p s t -> p (s t)"))
+                                  in_=grouped[:, piece, :].rearrange("p s t -> p (s t)"))
 
         kept = tile("kept", S, F32, tag="xr%d" % B)
         nc.vector.tensor_copy(kept[:], res_a[:].indirect(idx2[:]))

@@ -52,9 +52,9 @@ def tile_moe_mod_silu_kernel(
         def entries(lst, piece):
             return lst[:, piece.start // 16 : piece.stop // 16]
 
-        def load_scale_rows(plane, rows):
+        def load_scale_rows(plane, rows, quadrants=range(4)):
             words = rows.bitcast(I32)
-            for q in range(4):
+            for q in quadrants:
                 nc.sync.dma_start(
                     out=plane[32 * q : 32 * (q + 1), :].bitcast(I32),
                     in_=words[4 * q : 4 * (q + 1), :].partition_broadcast(8),
@@ -73,25 +73,28 @@ def tile_moe_mod_silu_kernel(
         xres = {t: tile("xr%d" % t, T, F32) for t in (A, B, C, D)}
 
         zero = tile("zero", 16, F32)
-        nc.gpsimd.memset(zero[:], 0.0)
+        ident = tile("ident", P, F32)
+        nc.vector.memset(xs[:].bitcast(I32), 0)
+        nc.vector.memset(zero[:], 0.0)
+        nc.vector.memset(ident[:], 0.0)
         zeros = zero[:, 0:1].to_broadcast([P, T])
-        z1 = {A: tile("z1a", T, F32), B: tile("z1b", T, F32), C: tile("z1c", T, F32)}
+        z1 = {A: tile("z1a", T, F32), B: tile("z1b", T, F32)}
         z1[D] = z1[B]
         z2 = {}
-        nc.gpsimd.memset(z1[A][:], 0.0)
-        ident = tile("ident", P, F32)
-        make_identity(nc, ident[:])
+        nc.vector.memset(z1[A][:], 0.0)
+        make_identity(nc, ident[:], nomemset=True)
+        for q in range(4):
+            nc.scalar.dma_start(out=xs[32 * q : 32 * q + 4, :].bitcast(I32), in_=x_scales[0].bitcast(I32)[4 * q : 4 * (q + 1), :])
         nc.scalar.activation(z1[B][:], zeros, SILU)
-        nc.scalar.copy(z1[C][:], zeros)
 
         xr_rows = xr.rearrange("(p t) w -> t p w", t=PACK)
         out_rows = out.rearrange("(p t) w -> t p w", t=PACK)
         nc.sync.dma_start(idx1[:], offs)
-        load_scale_rows(xs, x_scales[0])
         nc.sync.dma_start(out=w1_raw[:].bitcast(I32), in_=w1_words[0].bitcast(I32))
+        load_scale_rows(s1_raw, w1_scales[0], (0,))
         nc.sync.dma_start(out=xw[:].bitcast(I32), in_=x_words[0].rearrange("p t d -> p (t d)").bitcast(I32))
-        load_scale_rows(s1_raw, w1_scales[0])
-        for piece in HALVES:
+        load_scale_rows(s1_raw, w1_scales[0], (1, 2, 3))
+        for piece in (P0, slice(P1.start, S)):
             nc.sync.dma_start(out=g1[:, piece], in_=gate1[:, piece])
         nc.sync.dma_start(out=xres[D][:], in_=xr_rows[D])
         nc.sync.dma_start(idx2[:], offs2)
@@ -107,15 +110,17 @@ def tile_moe_mod_silu_kernel(
         w1 = tile("w1", 2 * K, U8)
         s1_pairs = [tile("s1_%d" % e, 2 * P, U8) for e in range(2)]
         s1 = {t: s1_pairs[t % 2][:, t // 2 * P : (t // 2 + 1) * P] for t in range(PACK)}
-        nc.vector.tensor_copy(gs[:], xs[:].indirect(idx1[:]))
         nc.vector.tensor_copy(
             w1[:].bitcast(U16).rearrange("p (e u m) -> p e u m", e=2, u=2),
             w1_raw[:].bitcast(U16).rearrange("p (m u e) -> p e u m", u=2, e=2),
         )
+        nc.vector.tensor_copy(gs[:], xs[:].indirect(idx1[:]))
         nc.vector.tensor_copy(gw[:, P0], xw[:].indirect(entries(idx1, P0)))
         s1_planes = s1_raw[:].rearrange("p (m u e) -> p e u m", u=2, e=2)
         for e in range(2):
             nc.gpsimd.tensor_copy(s1_pairs[e][:].rearrange("p (u m) -> p u m", u=2), s1_planes[:, e])
+        z1[C] = tile("z1c", T, F32, tag="s1_raw")
+        nc.gpsimd.memset(z1[C][:], 0.0)
         for piece in (P1, P2):
             nc.vector.tensor_copy(gw[:, piece], xw[:].indirect(entries(idx1, piece)))
 

@@ -52,9 +52,9 @@ def tile_moe_mod_silu_kernel(
         def entries(lst, piece):
             return lst[:, piece.start // 16 : piece.stop // 16]
 
-        def load_scale_rows(plane, rows, quadrants=range(4)):
+        def load_scale_rows(plane, rows):
             words = rows.bitcast(I32)
-            for q in quadrants:
+            for q in range(4):
                 nc.sync.dma_start(
                     out=plane[32 * q : 32 * (q + 1), :].bitcast(I32),
                     in_=words[4 * q : 4 * (q + 1), :].partition_broadcast(8),
@@ -83,18 +83,17 @@ def tile_moe_mod_silu_kernel(
         z2 = {}
         nc.vector.memset(z1[A][:], 0.0)
         make_identity(nc, ident[:], nomemset=True)
-        for q in range(4):
-            nc.scalar.dma_start(out=xs[32 * q : 32 * q + 4, :].bitcast(I32), in_=x_scales[0].bitcast(I32)[4 * q : 4 * (q + 1), :])
         nc.scalar.activation(z1[B][:], zeros, SILU)
 
         xr_rows = xr.rearrange("(p t) w -> t p w", t=PACK)
         out_rows = out.rearrange("(p t) w -> t p w", t=PACK)
         nc.sync.dma_start(idx1[:], offs)
         nc.sync.dma_start(out=w1_raw[:].bitcast(I32), in_=w1_words[0].bitcast(I32))
-        load_scale_rows(s1_raw, w1_scales[0], (0,))
+        for q in range(4):
+            nc.sync.dma_start(out=xs[32 * q : 32 * q + 4, :].bitcast(I32), in_=x_scales[0].bitcast(I32)[4 * q : 4 * (q + 1), :])
         nc.sync.dma_start(out=xw[:].bitcast(I32), in_=x_words[0].rearrange("p t d -> p (t d)").bitcast(I32))
-        load_scale_rows(s1_raw, w1_scales[0], (1, 2, 3))
-        for piece in (P0, slice(P1.start, S)):
+        load_scale_rows(s1_raw, w1_scales[0])
+        for piece in HALVES:
             nc.sync.dma_start(out=g1[:, piece], in_=gate1[:, piece])
         nc.sync.dma_start(out=xres[D][:], in_=xr_rows[D])
         nc.sync.dma_start(idx2[:], offs2)

@@ -60,6 +60,11 @@ def tile_moe_mod_silu_kernel(
                     in_=words[4 * q : 4 * (q + 1), :].partition_broadcast(8),
                 )
 
+        def load_live_rows(plane, rows):
+            words = rows.bitcast(I32)
+            for q in range(4):
+                nc.sync.dma_start(out=plane[32 * q : 32 * q + 4, :].bitcast(I32), in_=words[4 * q : 4 * (q + 1), :])
+
         idx1 = lists.tile([P, S // 16], U16, name="idx1")
         idx2 = lists.tile([P, S // 16], U16, name="idx2")
         xs = tile("xs", T, U8)
@@ -77,6 +82,7 @@ def tile_moe_mod_silu_kernel(
         nc.vector.memset(xs[:].bitcast(I32), 0)
         nc.vector.memset(zero[:], 0.0)
         nc.vector.memset(ident[:], 0.0)
+        nc.vector.memset(s1_raw[:].bitcast(I32), 0)
         zeros = zero[:, 0:1].to_broadcast([P, T])
         z1 = {A: tile("z1a", T, F32), B: tile("z1b", T, F32)}
         z1[D] = z1[B]
@@ -89,10 +95,9 @@ def tile_moe_mod_silu_kernel(
         out_rows = out.rearrange("(p t) w -> t p w", t=PACK)
         nc.sync.dma_start(idx1[:], offs)
         nc.sync.dma_start(out=w1_raw[:].bitcast(I32), in_=w1_words[0].bitcast(I32))
-        for q in range(4):
-            nc.sync.dma_start(out=xs[32 * q : 32 * q + 4, :].bitcast(I32), in_=x_scales[0].bitcast(I32)[4 * q : 4 * (q + 1), :])
+        load_live_rows(xs, x_scales[0])
         nc.sync.dma_start(out=xw[:].bitcast(I32), in_=x_words[0].rearrange("p t d -> p (t d)").bitcast(I32))
-        load_scale_rows(s1_raw, w1_scales[0])
+        load_live_rows(s1_raw, w1_scales[0])
         for piece in HALVES:
             nc.sync.dma_start(out=g1[:, piece], in_=gate1[:, piece])
         nc.sync.dma_start(out=xres[D][:], in_=xr_rows[D])

@@ -22,14 +22,10 @@ COPY = mybir.ActivationFunctionType.Copy
 MULT = mybir.AluOpType.mult
 ADD = mybir.AluOpType.add
 
-A, B, C, D = 0, 2, 3, 1
-P0, P1, P2 = slice(0, 256), slice(256, 768), slice(768, 1024)
-ALL = slice(0, 1024)
-TOKEN_HALVES = (slice(0, 1024), slice(1024, 2048))
-THIRD_CUTS = (slice(0, 1408), slice(1408, 2048))
-SECOND = (P0, P1, P2)
-HALVES = (slice(0, 512), slice(512, 1024))
-HELD = (slice(0, 512), slice(512, 1024), slice(1024, 1408))
+A, B, C, D = 0, 2, 1, 3
+Q = [slice(256 * q, 256 * (q + 1)) for q in range(4)]
+H = [slice(0, 512), slice(512, 1024)]
+TH = [slice(0, 1024), slice(1024, 2048)]
 
 
 def width(piece):
@@ -44,21 +40,12 @@ def tile_moe_mod_silu_kernel(
         lists = ctx.enter_context(tc.tile_pool(name="lists", bufs=1))
         keep = ctx.enter_context(tc.tile_pool(name="keep", bufs=1))
         psum = ctx.enter_context(tc.psum_pool(name="psum", bufs=1))
-        sums = ctx.enter_context(tc.psum_pool(name="sums", bufs=1))
 
         def tile(name, cols, dtype, tag=None):
             return keep.tile([P, cols], dtype, name=name, tag=tag or name, align_bytes=64)
 
         def entries(lst, piece):
             return lst[:, piece.start // 16 : piece.stop // 16]
-
-        def load_scale_rows(plane, rows):
-            words = rows.bitcast(I32)
-            for q in range(4):
-                nc.sync.dma_start(
-                    out=plane[32 * q : 32 * (q + 1), :].bitcast(I32),
-                    in_=words[4 * q : 4 * (q + 1), :].partition_broadcast(8),
-                )
 
         def load_live_rows(plane, rows):
             words = rows.bitcast(I32)
@@ -75,7 +62,9 @@ def tile_moe_mod_silu_kernel(
         s2_raw = tile("s2_raw", K, U8)
         g1 = tile("g1", S, F32)
         g2 = tile("g2", S, F32)
-        xres = {t: tile("xr%d" % t, T, F32) for t in (A, B, C, D)}
+        g2_rows = tile("g2_rows", P, F32)
+        xr_a = tile("xr_a", T, F32)
+        res = {A: tile("res_a", T, F32), C: tile("res_c", T, F32)}
 
         zero = tile("zero", 16, F32)
         ident = tile("ident", P, F32)
@@ -83,13 +72,13 @@ def tile_moe_mod_silu_kernel(
         nc.vector.memset(zero[:], 0.0)
         nc.vector.memset(ident[:], 0.0)
         nc.vector.memset(s1_raw[:].bitcast(I32), 0)
+        nc.vector.memset(s2_raw[:].bitcast(I32), 0)
         zeros = zero[:, 0:1].to_broadcast([P, T])
-        z1 = {A: tile("z1a", T, F32), B: tile("z1b", T, F32)}
-        z1[D] = z1[B]
-        z2 = {}
+        z1 = {t: tile("z1_%d" % t, T, F32) for t in (A, B, D)}
         nc.vector.memset(z1[A][:], 0.0)
         make_identity(nc, ident[:], nomemset=True)
         nc.scalar.activation(z1[B][:], zeros, SILU)
+        nc.scalar.copy(z1[D][:], zeros)
 
         xr_rows = xr.rearrange("(p t) w -> t p w", t=PACK)
         out_rows = out.rearrange("(p t) w -> t p w", t=PACK)
@@ -98,15 +87,14 @@ def tile_moe_mod_silu_kernel(
         load_live_rows(xs, x_scales[0])
         nc.sync.dma_start(out=xw[:].bitcast(I32), in_=x_words[0].rearrange("p t d -> p (t d)").bitcast(I32))
         load_live_rows(s1_raw, w1_scales[0])
-        for piece in HALVES:
+        for piece in H:
             nc.sync.dma_start(out=g1[:, piece], in_=gate1[:, piece])
-        nc.sync.dma_start(out=xres[D][:], in_=xr_rows[D])
-        nc.sync.dma_start(idx2[:], offs2)
         nc.sync.dma_start(out=w2_raw[:].bitcast(I32), in_=w2_words[0].rearrange("p n d -> p (n d)").bitcast(I32))
-        load_scale_rows(s2_raw, w2_scales[0])
-        nc.sync.dma_start(out=xres[A][:], in_=xr_rows[A])
-        nc.sync.dma_start(out=xres[B][:], in_=xr_rows[B])
-        nc.sync.dma_start(out=xres[C][:], in_=xr_rows[C])
+        load_live_rows(s2_raw, w2_scales[0])
+        nc.sync.dma_start(idx2[:], offs2)
+        nc.sync.dma_start(out=xr_a[:], in_=xr_rows[A])
+        nc.sync.dma_start(out=g2_rows[:], in_=gate2[0:16, :].rearrange("a (m j) -> (a m) j", j=P))
+        nc.sync.dma_start(out=res[C][:], in_=xr_rows[C])
         nc.sync.dma_start(out=g2[:], in_=gate2)
 
         gs = tile("gs", S, U8)
@@ -118,192 +106,197 @@ def tile_moe_mod_silu_kernel(
             w1[:].bitcast(U16).rearrange("p (e u m) -> p e u m", e=2, u=2),
             w1_raw[:].bitcast(U16).rearrange("p (m u e) -> p e u m", u=2, e=2),
         )
-        nc.vector.tensor_copy(gs[:], xs[:].indirect(idx1[:]))
-        nc.vector.tensor_copy(gw[:, P0], xw[:].indirect(entries(idx1, P0)))
+        z1[C] = tile("z1_c", T, F32, tag="w1_raw")
+        nc.gpsimd.memset(z1[C][:], 0.0)
+        nc.vector.tensor_copy(gs[:, H[0]], xs[:].indirect(entries(idx1, H[0])))
+        nc.vector.tensor_copy(gw[:, Q[0]], xw[:].indirect(entries(idx1, Q[0])))
         s1_planes = s1_raw[:].rearrange("p (m u e) -> p e u m", u=2, e=2)
         for e in range(2):
             nc.gpsimd.tensor_copy(s1_pairs[e][:].rearrange("p (u m) -> p u m", u=2), s1_planes[:, e])
-        z1[C] = tile("z1c", T, F32, tag="s1_raw")
-        nc.gpsimd.memset(z1[C][:], 0.0)
-        for piece in (P1, P2):
-            nc.vector.tensor_copy(gw[:, piece], xw[:].indirect(entries(idx1, piece)))
+        nc.vector.tensor_copy(gw[:, Q[1]], xw[:].indirect(entries(idx1, Q[1])))
+        nc.vector.tensor_copy(gs[:, H[1]], xs[:].indirect(entries(idx1, H[1])))
+        nc.vector.tensor_copy(gw[:, H[1]], xw[:].indirect(entries(idx1, H[1])))
 
         turns = []
 
-        def product(y, cols, lhs, lhs_scale, rhs, rhs_scale):
-            acc = psum.tile([P, BANK], F32, name="acc", tag="acc%d" % (len(turns) % 4))
-            turns.append(cols)
-            n = width(cols)
+        def product(y, lhs, lhs_scale, rhs, rhs_scale, n):
+            acc = psum.tile([P, BANK], F32, name="acc", tag="acc%d" % (len(turns) % 6))
+            turns.append(n)
             nc.tensor.matmul_mx(out=acc[:, :n], lhsT=lhs, lhsT_scale=lhs_scale, rhs=rhs, rhs_scale=rhs_scale, start=True, stop=True)
-            nc.scalar.activation(y[:, cols], acc[:, :n], SILU)
+            nc.scalar.activation(y, acc[:, :n], SILU)
 
-        def first_product(t, piece, parts):
+        y1 = {t: tile("y1_%d" % t, S, F32) for t in (A, B, C, D)}
+
+        raw = {(B, 0): tile("raw_b", 256, F32), (C, 0): tile("raw_c", BANK, F32), (D, BANK): tile("raw_d", BANK, F32)}
+
+        def first(t, piece):
             e, u = t % 2, t // 2
-            y = tile("y1_%d_%d" % (t, piece.start), width(piece), F32)
-            for part in parts:
-                product(
-                    y, slice(part.start - piece.start, part.stop - piece.start),
-                    w1[:, 2 * P * (2 * e + u) : 2 * P * (2 * e + u + 1)].bitcast(FP4X4), s1[t],
-                    gw[:, part].bitcast(FP8X4), gs[:, part],
-                )
-            return y
+            product(raw[t, piece.start][:] if (t, piece.start) in raw else y1[t][:, piece], w1[:, 2 * P * (2 * e + u) : 2 * P * (2 * e + u + 1)].bitcast(FP4X4), s1[t],
+                    gw[:, piece].bitcast(FP8X4), gs[:, piece], width(piece))
 
-        def gated(y, gate, piece, name, tag=None):
-            dst = tile(name, width(piece), F32, tag=tag)
-            nc.gpsimd.tensor_tensor(dst[:], y[:], gate[:, piece], MULT)
-            return dst
+        def pool_gate1(t, piece):
+            src = raw[t, piece.start][:] if (t, piece.start) in raw else y1[t][:, piece]
+            nc.gpsimd.tensor_tensor(y1[t][:, piece], src, g1[:, piece], MULT)
 
-        def scatter1(t, piece, y):
-            nc.vector.tensor_copy(z1[t][:].indirect(entries(idx1, piece)), y[:])
+        def forth(engine, t, piece):
+            scatter(engine, z1[t], idx1, piece, y1[t][:, piece])
 
-        steps1 = [(t, piece, first_product(t, piece, parts)) for t, piece, parts in
-                  ((A, P0, (P0,)), (B, P0, (P0,)), (A, slice(256, S), (P1, P2)), (B, slice(256, S), (P1, P2)))]
-        opening1 = tile("opening1", width(P0), F32)
-        nc.vector.tensor_tensor(opening1[:], steps1[0][2][:], g1[:, P0], MULT)
-        steps1 = [(A, P0, opening1), (B, P0, gated(steps1[1][2], g1, P0, "follower1", "y1_%d_0" % A))] + [
-            (t, piece, gated(y, g1, piece, "g1_%d_%d" % (t, piece.start))) for t, piece, y in steps1[2:]]
-        third, fourth = [first_product(t, ALL, HALVES) for t in (C, D)]
-        z2[D] = tile("z2d", T, F32, tag="gw")
-        nc.scalar.copy(z2[D][:], zeros)
-        third, fourth = gated(third, g1, ALL, "g1_third"), gated(fourth, g1, ALL, "g1_fourth")
-        for step in steps1 + [(C, ALL, third)]:
-            scatter1(*step)
+        def scatter(engine, window, lst, piece, src):
+            if engine == "vector":
+                nc.vector.tensor_copy(window[:].indirect(entries(lst, piece)), src)
+            else:
+                nc.scalar.activation(window[:].indirect(entries(lst, piece)), src, COPY)
 
-        def turned_onto(banks, src, first, last, which=range(T // BANK)):
-            for b in which:
+        def gate_columns():
+            cols = tile("gate_cols", S // P, F32)
+            turned = psum.tile([P, P], F32, name="turned", tag="gate0")
+            nc.tensor.transpose(turned[:], g2_rows[:], ident[:])
+            nc.scalar.copy(cols[:], turned[:, 0 : S // P])
+            return cols
+
+        def gate_banks(cols):
+            banks = []
+            for h in range(2):
+                bank = psum.tile([P, BANK], F32, name="gate_bank", tag="gate%d" % h)
                 for j in range(BANK // P):
-                    nc.tensor.matmul(banks[b][:, j * P : (j + 1) * P], lhsT=src[:, b * BANK + j * P : b * BANK + (j + 1) * P], rhs=ident[:],
-                                     is_transpose=True, start=first and j == 0, stop=last and j == BANK // P - 1)
-
-        def turned_back(banks, dst, tag):
-            rows = tile(tag, T, F32)
-            for b in range(T // BANK):
-                nc.scalar.copy(rows[:, b * BANK : (b + 1) * BANK], banks[b][:])
-            backs = []
-            for b in range(T // BANK):
-                back = psum.tile([P, BANK], F32, name="back", tag="acc%d" % b)
-                for j in range(BANK // P):
-                    nc.tensor.transpose(back[:, j * P : (j + 1) * P], rows[:, b * BANK + j * P : b * BANK + (j + 1) * P], ident[:])
-                nc.scalar.copy(dst[:, b * BANK : (b + 1) * BANK], back[:])
-                backs.append(back)
-            return backs
-
-        def sum_banks():
-            return [sums.tile([P, BANK], F32, name="sum%d" % b, tag="sum%d" % b) for b in range(T // BANK)]
-
-        grouped = keep.tile([P, S, PACK], BF16, name="grouped", align_bytes=64)
-
-        def scalar_gather(rb, t, piece):
-            nc.scalar.activation(grouped[:, piece, t], rb[:].indirect(entries(idx2, piece)), COPY)
-
-        def first_sum(t, tag):
-            rb = tile("rb%d" % t, T, BF16, tag=tag)
-            nc.gpsimd.tensor_tensor(rb[:], xres[t][:], z1[t][:], ADD)
-            scalar_gather(rb, t, ALL)
+                    nc.tensor.transpose(bank[:, j * P : (j + 1) * P], cols[:, 4 * h + j : 4 * h + j + 1].to_broadcast([P, P]), ident[:])
+                banks.append(bank)
+            return banks
 
         def permuted(raw, dtype, name, tag):
             dst = tile(name, K, dtype, tag=tag)
             nc.gpsimd.tensor_copy(dst[:].rearrange("p (t m) -> p t m", t=PACK), raw[:].rearrange("p (m t) -> p t m", t=PACK))
             return dst
 
-        w2 = permuted(w2_raw, U32, "w2", "y1_%d_0" % C)
-        s2_all = permuted(s2_raw, U8, "s2", "y1_%d_0" % D)
-        s2 = {t: s2_all[:, t * P : (t + 1) * P] for t in range(PACK)}
-        z2[B] = tile("z2b", T, F32, tag="s2_raw")
-        nc.gpsimd.memset(z2[B][:], 0.0)
-        held_rows = tile("held_rows", T, F32)
-        for b, cols in enumerate(HELD):
-            turned = psum.tile([P, BANK], F32, name="turned", tag="acc%d" % b)
-            for j in range(width(cols) // P):
-                nc.tensor.transpose(turned[:, j * P : (j + 1) * P], xres[D][:, cols.start + j * P : cols.start + (j + 1) * P], ident[:])
-            nc.scalar.copy(held_rows[:, cols], turned[:, : width(cols)])
-        banks = sum_banks()
-        turned_onto(banks, xres[A], True, False)
-        turned_onto(banks, z1[A], False, True)
-        res_a = tile("res_a", T, F32)
-        rb_first = tile("rb_a", T, BF16)
-        backs = turned_back(banks, rb_first, "rows1")
-        scalar_gather(rb_first, A, ALL)
-        for b, back in enumerate(backs):
-            nc.scalar.copy(res_a[:, b * BANK : (b + 1) * BANK], back[:])
-        banks = sum_banks()
-        turned_onto(banks, z1[B], True, False)
-        turned_onto(banks, xres[B], False, False)
-        held = []
-        for b, cols in enumerate(HELD):
-            held.append(psum.tile([P, BANK], F32, name="held", tag="acc%d" % b))
-            for j in range(width(cols) // P):
-                nc.tensor.transpose(held[b][:, j * P : (j + 1) * P], held_rows[:, cols.start + j * P : cols.start + (j + 1) * P], ident[:])
-        first_sum(B, "rows1")
-        scatter1(D, ALL, fourth)
-        first_sum(C, "xr%d" % B)
-        z2[A] = res_a
-        rb_last = tile("rb_d", T, BF16, tag="held_rows")
-        for b, cols in enumerate(HELD):
-            nc.vector.tensor_tensor(rb_last[:, cols], held[b][:, : width(cols)], z1[D][:, cols], ADD)
-        rest = slice(HELD[-1].stop, T)
-        nc.gpsimd.tensor_tensor(rb_last[:, rest], xres[D][:, rest], z1[D][:, rest], ADD)
-        for piece in SECOND:
-            scalar_gather(rb_last, D, piece)
+        for t, piece in ((B, Q[0]), (A, Q[0]), (B, Q[1]), (A, Q[1])):
+            first(t, piece)
+            pool_gate1(t, piece)
+        forth("scalar", B, Q[0])
+        raw[A, BANK] = tile("raw_a", BANK, F32, tag="raw_b")
+        for t, piece in ((A, H[1]), (B, H[1])):
+            first(t, piece)
+            pool_gate1(t, piece)
+        forth("vector", A, Q[0])
+        forth("vector", A, Q[1])
+        forth("scalar", B, Q[1])
+        first(C, H[0])
+        first(D, H[0])
+        pool_gate1(C, H[0])
+        pool_gate1(D, H[0])
+        first(C, H[1])
+        forth("scalar", B, Q[2])
+        first(D, H[1])
+        pool_gate1(C, H[1])
+        pool_gate1(D, H[1])
+        g2_banks = gate_banks(gate_columns())
+        forth("vector", A, H[1])
+        forth("scalar", B, Q[3])
+        forth("vector", C, H[0])
+        forth("vector", C, H[1])
+        res[B] = tile("res_b", T, F32, tag="raw_c")
+        nc.sync.dma_start(out=res[B][:], in_=xr_rows[B])
+        nc.gpsimd.tensor_tensor(res[A][:], xr_a[:], z1[A][:], ADD)
+        res[D] = tile("res_d", T, F32, tag="raw_d")
+        nc.sync.dma_start(out=res[D][:], in_=xr_rows[D])
+        forth("scalar", D, slice(0, 384))
+        forth("scalar", D, slice(384, 640))
+        forth("scalar", D, slice(640, 1024))
+        for t in (B, C, D):
+            nc.vector.tensor_tensor(res[t][:], res[t][:], z1[t][:], ADD)
+        w2 = permuted(w2_raw, U32, "w2", "z1_%d" % D)
+        s2_all = permuted(s2_raw, U8, "s2", "w2_raw")
 
+        PIECES = (Q[0], Q[1], H[1])
+        kept_first = keep.tile([P, 2, PACK, 256], F32, name="kept_first", tag="xr_a", align_bytes=64)
+        kept_rest = keep.tile([P, PACK, BANK], F32, name="kept_rest", tag="z1_%d" % A, align_bytes=64)
+        kept = [kept_first[:, 0], kept_first[:, 1], kept_rest[:]]
+        grouped = [keep.tile([P, width(p), PACK], BF16, name="grouped%d" % p.start, align_bytes=64) for p in PIECES]
         codes = tile("codes", S, U32)
         scales = tile("scales", S, U8)
 
-        def quantise(piece):
-            nc.vector.quantize_mx(out=codes[:, piece].bitcast(FP8X4), scales=scales[:, piece],
-                                  in_=grouped[:, piece, :].rearrange("p s t -> p (s t)"))
+        def gather(engine, t, k):
+            src = res[t][:].indirect(entries(idx2, PIECES[k]))
+            if engine == "vector":
+                nc.vector.tensor_copy(kept[k][:, t, :], src)
+            else:
+                nc.scalar.activation(kept[k][:, t, :], src, COPY)
 
-        kept = tile("kept", S, F32, tag="xr%d" % B)
-        nc.vector.tensor_copy(kept[:], res_a[:].indirect(idx2[:]))
-        for piece in SECOND:
-            quantise(piece)
+        def weave(k):
+            nc.vector.tensor_copy(grouped[k][:].rearrange("p (c i) t -> p c t i", i=4), kept[k].rearrange("p t (c i) -> p c t i", i=4))
 
-        def second_product(t, piece, parts):
-            y = tile("y2_%d_%d" % (t, piece.start), width(piece), F32)
-            for part in parts:
-                product(
-                    y, slice(part.start - piece.start, part.stop - piece.start),
-                    w2[:, t * P : (t + 1) * P].bitcast(FP8X4), s2[t],
-                    codes[:, part].bitcast(FP8X4), scales[:, part],
-                )
-            return t, piece, y
+        def quantise(k):
+            nc.vector.quantize_mx(out=codes[:, PIECES[k]].bitcast(FP8X4), scales=scales[:, PIECES[k]], in_=grouped[k][:].rearrange("p s t -> p (s t)"))
 
-        def second_gated(steps):
-            return [(t, piece, gated(y, g2, piece, "g2_%d_%d" % (t, piece.start))) for t, piece, y in steps]
+        y2 = {t: tile("y2_%d" % t, S, F32) for t in (A, B, C, D)}
 
-        def scatter2(t, piece, y):
-            nc.vector.tensor_copy(z2[t][:].indirect(entries(idx2, piece)), y[:])
+        def second(t, piece):
+            product(y2[t][:, piece], w2[:, t * P : (t + 1) * P].bitcast(FP8X4), s2_all[:, t * P : (t + 1) * P],
+                    codes[:, piece].bitcast(FP8X4), scales[:, piece], width(piece))
 
-        rest = slice(P1.start, S)
-        steps2 = [second_product(t, P0, SECOND[:1]) for t in (B, D)] + [second_product(t, rest, SECOND[1:]) for t in (B, D)]
-        steps2 = steps2 + [second_product(t, ALL, HALVES) for t in (C, A)]
-        z2[C] = tile("z2c", T, F32, tag="scales")
-        nc.scalar.copy(z2[C][:], zeros)
-        opening2 = tile("opening2", width(P0), F32)
-        nc.vector.tensor_tensor(opening2[:], steps2[0][2][:], g2[:, P0], MULT)
-        steps2 = [(B, P0, opening2), (D, P0, gated(steps2[1][2], g2, P0, "follower2", "y2_%d_0" % B))] + second_gated(steps2[2:])
-        for step in steps2[:5]:
-            scatter2(*step)
-        last = steps2[5][2]
-        nc.gpsimd.tensor_tensor(last[:], last[:], kept[:], ADD)
-        res_c = tile("res_c", T, F32, tag="y2_%d_0" % A)
-        nc.gpsimd.tensor_tensor(res_c[:], xres[C][:], z1[C][:], ADD)
+        def vector_gate(t, piece):
+            at = piece.start % BANK
+            nc.vector.tensor_tensor(y2[t][:, piece], y2[t][:, piece], g2_banks[piece.start // BANK][:, at : at + width(piece)], MULT)
 
-        turned_onto(banks, z2[B], False, True)
-        total = tile("total_b", T, F32, tag="xr%d" % A)
-        turned_back(banks, total, "rows2")
-        nc.scalar.dma_start(out=out_rows[B], in_=total[:])
-        banks = sum_banks()
-        turned_onto(banks, xres[D], True, False)
-        turned_onto(banks, z1[D], False, False)
-        turned_onto(banks, z2[D], False, True)
-        total = tile("total_d", T, F32, tag="rows1")
-        turned_back(banks, total, "rows2")
-        nc.scalar.dma_start(out=out_rows[D], in_=total[:])
-        scatter2(*steps2[5])
-        total = tile("total_c", T, F32, tag="rows2")
-        for cols in THIRD_CUTS:
-            nc.gpsimd.tensor_tensor(total[:, cols], res_c[:, cols], z2[C][:, cols], ADD)
-            nc.scalar.dma_start(out=out_rows[C][:, cols], in_=total[:, cols])
-        for cols in TOKEN_HALVES:
-            nc.sync.dma_start(out=out_rows[A][:, cols], in_=res_a[:, cols])
+        def pool_gate(t, piece):
+            nc.gpsimd.tensor_tensor(y2[t][:, piece], y2[t][:, piece], g2[:, piece], MULT)
+
+        def pool_add(t, k):
+            nc.gpsimd.tensor_tensor(y2[t][:, PIECES[k]], y2[t][:, PIECES[k]], kept[k][:, t, :], ADD)
+
+        def back(engine, t, piece):
+            scatter(engine, res[t], idx2, piece, y2[t][:, piece])
+
+        def fused(t, k):
+            nc.vector.tensor_tensor(res[t][:].indirect(entries(idx2, PIECES[k])), y2[t][:, PIECES[k]], kept[k][:, t, :], ADD)
+
+        for t, k in ((A, 0), (A, 1), (A, 2), (B, 0), (B, 1), (C, 0), (C, 1), (B, 2), (C, 2), (D, 2)):
+            gather("scalar", t, k)
+        gather("vector", D, 0)
+        gather("vector", D, 1)
+        weave(0)
+        weave(1)
+        quantise(0)
+        quantise(1)
+        for t, piece in ((B, Q[0]), (A, Q[0]), (B, Q[1]), (A, Q[1]), (D, H[0])):
+            second(t, piece)
+        weave(2)
+        vector_gate(B, Q[0])
+        quantise(2)
+        vector_gate(A, Q[0])
+        vector_gate(B, Q[1])
+        vector_gate(A, Q[1])
+        vector_gate(D, H[0])
+        for t, k in ((B, 0), (A, 0), (B, 1), (A, 1), (D, 0), (D, 1)):
+            pool_add(t, k)
+        second(B, H[1])
+        second(A, H[1])
+        back("scalar", B, Q[0])
+        back("vector", A, Q[0])
+        second(D, H[1])
+        back("scalar", B, Q[1])
+        vector_gate(B, H[1])
+        vector_gate(A, H[1])
+        pool_add(B, 2)
+        pool_add(A, 2)
+        back("vector", A, Q[1])
+        second(C, H[0])
+        second(C, H[1])
+        back("scalar", D, Q[0])
+        pool_gate(D, H[1])
+        pool_gate(C, H[0])
+        pool_add(D, 2)
+        back("scalar", B, Q[2])
+        back("scalar", D, Q[1])
+        back("scalar", B, Q[3])
+        back("vector", A, H[1])
+        for t in (A, B):
+            nc.sync.dma_start(out=out_rows[t], in_=res[t][:])
+        back("scalar", D, Q[2])
+        back("scalar", D, Q[3])
+        vector_gate(C, H[1])
+        fused(C, 0)
+        fused(C, 1)
+        fused(C, 2)
+        for t in (D, C):
+            for cols in TH:
+                nc.sync.dma_start(out=out_rows[t][:, cols], in_=res[t][:, cols])

@@ -25,6 +25,8 @@ ADD = mybir.AluOpType.add
 A, B, C, D = 0, 2, 1, 3
 Q = [slice(256 * q, 256 * (q + 1)) for q in range(4)]
 H = [slice(0, 512), slice(512, 1024)]
+REST = slice(256, 1024)
+THIRDS = [slice(0, 256), slice(256, 640), slice(640, 1024)]
 TH = [slice(0, 1024), slice(1024, 2048)]
 
 
@@ -61,10 +63,10 @@ def tile_moe_mod_silu_kernel(
         w2_raw = tile("w2_raw", K, U32)
         s2_raw = tile("s2_raw", K, U8)
         g1 = tile("g1", S, F32)
-        g2 = tile("g2", S, F32)
+        g2 = tile("g2", BANK, F32)
         g2_rows = tile("g2_rows", P, F32)
         xr_a = tile("xr_a", T, F32)
-        res = {A: tile("res_a", T, F32), C: tile("res_c", T, F32)}
+        res = {A: tile("res_a", T, F32)}
 
         zero = tile("zero", 16, F32)
         ident = tile("ident", P, F32)
@@ -87,15 +89,14 @@ def tile_moe_mod_silu_kernel(
         load_live_rows(xs, x_scales[0])
         nc.sync.dma_start(out=xw[:].bitcast(I32), in_=x_words[0].rearrange("p t d -> p (t d)").bitcast(I32))
         load_live_rows(s1_raw, w1_scales[0])
-        for piece in H:
-            nc.sync.dma_start(out=g1[:, piece], in_=gate1[:, piece])
+        nc.sync.dma_start(out=g1[:, Q[0]], in_=gate1[:, Q[0]])
         nc.sync.dma_start(out=w2_raw[:].bitcast(I32), in_=w2_words[0].rearrange("p n d -> p (n d)").bitcast(I32))
+        nc.sync.dma_start(out=g1[:, REST], in_=gate1[:, REST])
         load_live_rows(s2_raw, w2_scales[0])
         nc.sync.dma_start(idx2[:], offs2)
         nc.sync.dma_start(out=xr_a[:], in_=xr_rows[A])
         nc.sync.dma_start(out=g2_rows[:], in_=gate2[0:16, :].rearrange("a (m j) -> (a m) j", j=P))
-        nc.sync.dma_start(out=res[C][:], in_=xr_rows[C])
-        nc.sync.dma_start(out=g2[:], in_=gate2)
+        nc.sync.dma_start(out=g2[:], in_=gate2[:, H[0]])
 
         gs = tile("gs", S, U8)
         gw = tile("gw", S, U32)
@@ -108,13 +109,19 @@ def tile_moe_mod_silu_kernel(
         )
         z1[C] = tile("z1_c", T, F32, tag="w1_raw")
         nc.gpsimd.memset(z1[C][:], 0.0)
-        nc.vector.tensor_copy(gs[:, H[0]], xs[:].indirect(entries(idx1, H[0])))
+        nc.vector.tensor_copy(gs[:], xs[:].indirect(idx1[:]))
         nc.vector.tensor_copy(gw[:, Q[0]], xw[:].indirect(entries(idx1, Q[0])))
         s1_planes = s1_raw[:].rearrange("p (m u e) -> p e u m", u=2, e=2)
         for e in range(2):
             nc.gpsimd.tensor_copy(s1_pairs[e][:].rearrange("p (u m) -> p u m", u=2), s1_planes[:, e])
+
+        def permuted(raw, dtype, name, tag):
+            dst = tile(name, K, dtype, tag=tag)
+            nc.gpsimd.tensor_copy(dst[:].rearrange("p (t m) -> p t m", t=PACK), raw[:].rearrange("p (m t) -> p t m", t=PACK))
+            return dst
+
+        w2 = permuted(w2_raw, U32, "w2", "w2")
         nc.vector.tensor_copy(gw[:, Q[1]], xw[:].indirect(entries(idx1, Q[1])))
-        nc.vector.tensor_copy(gs[:, H[1]], xs[:].indirect(entries(idx1, H[1])))
         nc.vector.tensor_copy(gw[:, H[1]], xw[:].indirect(entries(idx1, H[1])))
 
         turns = []
@@ -125,178 +132,171 @@ def tile_moe_mod_silu_kernel(
             nc.tensor.matmul_mx(out=acc[:, :n], lhsT=lhs, lhsT_scale=lhs_scale, rhs=rhs, rhs_scale=rhs_scale, start=True, stop=True)
             nc.scalar.activation(y, acc[:, :n], SILU)
 
+        raw1 = {t: tile("raw1_%d" % t, S, F32) for t in (A, B, C, D)}
         y1 = {t: tile("y1_%d" % t, S, F32) for t in (A, B, C, D)}
-
-        raw = {(B, 0): tile("raw_b", 256, F32), (C, 0): tile("raw_c", BANK, F32), (D, BANK): tile("raw_d", BANK, F32)}
 
         def first(t, piece):
             e, u = t % 2, t // 2
-            product(raw[t, piece.start][:] if (t, piece.start) in raw else y1[t][:, piece], w1[:, 2 * P * (2 * e + u) : 2 * P * (2 * e + u + 1)].bitcast(FP4X4), s1[t],
+            product(raw1[t][:, piece], w1[:, 2 * P * (2 * e + u) : 2 * P * (2 * e + u + 1)].bitcast(FP4X4), s1[t],
                     gw[:, piece].bitcast(FP8X4), gs[:, piece], width(piece))
 
-        def pool_gate1(t, piece):
-            src = raw[t, piece.start][:] if (t, piece.start) in raw else y1[t][:, piece]
-            nc.gpsimd.tensor_tensor(y1[t][:, piece], src, g1[:, piece], MULT)
-
-        def forth(engine, t, piece):
-            scatter(engine, z1[t], idx1, piece, y1[t][:, piece])
+        def gate1_on(engine, t, piece):
+            engine.tensor_tensor(y1[t][:, piece], raw1[t][:, piece], g1[:, piece], MULT)
 
         def scatter(engine, window, lst, piece, src):
-            if engine == "vector":
+            if engine is nc.vector:
                 nc.vector.tensor_copy(window[:].indirect(entries(lst, piece)), src)
             else:
                 nc.scalar.activation(window[:].indirect(entries(lst, piece)), src, COPY)
 
-        def gate_columns():
-            cols = tile("gate_cols", S // P, F32)
-            turned = psum.tile([P, P], F32, name="turned", tag="gate0")
-            nc.tensor.transpose(turned[:], g2_rows[:], ident[:])
-            nc.scalar.copy(cols[:], turned[:, 0 : S // P])
-            return cols
+        def forth(engine, t, piece):
+            scatter(engine, z1[t], idx1, piece, y1[t][:, piece])
 
-        def gate_banks(cols):
-            banks = []
-            for h in range(2):
-                bank = psum.tile([P, BANK], F32, name="gate_bank", tag="gate%d" % h)
-                for j in range(BANK // P):
-                    nc.tensor.transpose(bank[:, j * P : (j + 1) * P], cols[:, 4 * h + j : 4 * h + j + 1].to_broadcast([P, P]), ident[:])
-                banks.append(bank)
-            return banks
+        for t in (A, D, B, C):
+            first(t, Q[0])
+        gate1_on(nc.vector, A, Q[0])
+        for t in (B, C):
+            gate1_on(nc.gpsimd, t, Q[0])
+        for piece in (Q[1], H[1]):
+            first(A, piece)
+        forth(nc.scalar, B, Q[0])
+        forth(nc.vector, A, Q[0])
+        forth(nc.vector, C, Q[0])
+        for t in (B, C, D):
+            for piece in (Q[1], H[1]):
+                first(t, piece)
+        gate1_on(nc.gpsimd, A, REST)
+        gate1_on(nc.gpsimd, D, Q[0])
+        for t in (B, C, D):
+            gate1_on(nc.gpsimd, t, REST)
+        forth(nc.vector, A, REST)
+        forth(nc.vector, C, REST)
 
-        def permuted(raw, dtype, name, tag):
-            dst = tile(name, K, dtype, tag=tag)
-            nc.gpsimd.tensor_copy(dst[:].rearrange("p (t m) -> p t m", t=PACK), raw[:].rearrange("p (m t) -> p t m", t=PACK))
-            return dst
+        gate_cols = tile("gate_cols", S // P, F32)
+        turned = psum.tile([P, P], F32, name="turned", tag="gate0")
+        nc.tensor.transpose(turned[:], g2_rows[:], ident[:])
+        nc.scalar.copy(gate_cols[:], turned[:, 0 : S // P])
+        g2_banks = []
+        for h in range(2):
+            bank = psum.tile([P, BANK], F32, name="gate_bank", tag="gate%d" % h)
+            for j in range(BANK // P):
+                nc.tensor.transpose(bank[:, j * P : (j + 1) * P], gate_cols[:, 4 * h + j : 4 * h + j + 1].to_broadcast([P, P]), ident[:])
+            g2_banks.append(bank)
 
-        for t, piece in ((B, Q[0]), (A, Q[0]), (B, Q[1]), (A, Q[1])):
-            first(t, piece)
-            pool_gate1(t, piece)
-        forth("scalar", B, Q[0])
-        raw[A, BANK] = tile("raw_a", BANK, F32, tag="raw_b")
-        for t, piece in ((A, H[1]), (B, H[1])):
-            first(t, piece)
-            pool_gate1(t, piece)
-        forth("vector", A, Q[0])
-        forth("vector", A, Q[1])
-        forth("scalar", B, Q[1])
-        first(C, H[0])
-        first(D, H[0])
-        pool_gate1(C, H[0])
-        pool_gate1(D, H[0])
-        first(C, H[1])
-        forth("scalar", B, Q[2])
-        first(D, H[1])
-        pool_gate1(C, H[1])
-        pool_gate1(D, H[1])
-        g2_banks = gate_banks(gate_columns())
-        forth("vector", A, H[1])
-        forth("scalar", B, Q[3])
-        forth("vector", C, H[0])
-        forth("vector", C, H[1])
-        res[B] = tile("res_b", T, F32, tag="raw_c")
-        nc.sync.dma_start(out=res[B][:], in_=xr_rows[B])
+        forth(nc.scalar, D, THIRDS[0])
+        for piece in THIRDS[1:]:
+            forth(nc.scalar, B, piece)
+            forth(nc.scalar, D, piece)
+        for t in (B, C, D):
+            res[t] = tile("res_%d" % t, T, F32, tag="raw1_%d" % t)
+            nc.sync.dma_start(out=res[t][:], in_=xr_rows[t])
         nc.gpsimd.tensor_tensor(res[A][:], xr_a[:], z1[A][:], ADD)
-        res[D] = tile("res_d", T, F32, tag="raw_d")
-        nc.sync.dma_start(out=res[D][:], in_=xr_rows[D])
-        forth("scalar", D, slice(0, 384))
-        forth("scalar", D, slice(384, 640))
-        forth("scalar", D, slice(640, 1024))
         for t in (B, C, D):
             nc.vector.tensor_tensor(res[t][:], res[t][:], z1[t][:], ADD)
-        w2 = permuted(w2_raw, U32, "w2", "z1_%d" % D)
-        s2_all = permuted(s2_raw, U8, "s2", "w2_raw")
+
+        s2_all = permuted(s2_raw, U8, "s2", "z1_%d" % D)
 
         PIECES = (Q[0], Q[1], H[1])
-        kept_first = keep.tile([P, 2, PACK, 256], F32, name="kept_first", tag="xr_a", align_bytes=64)
-        kept_rest = keep.tile([P, PACK, BANK], F32, name="kept_rest", tag="z1_%d" % A, align_bytes=64)
-        kept = [kept_first[:, 0], kept_first[:, 1], kept_rest[:]]
-        grouped = [keep.tile([P, width(p), PACK], BF16, name="grouped%d" % p.start, align_bytes=64) for p in PIECES]
+        kept = [keep.tile([P, PACK, BANK], F32, name="kept%d" % h, tag=tag, align_bytes=64) for h, tag in enumerate(("xr_a", "w1_raw"))]
         codes = tile("codes", S, U32)
         scales = tile("scales", S, U8)
 
-        def gather(engine, t, k):
-            src = res[t][:].indirect(entries(idx2, PIECES[k]))
-            if engine == "vector":
-                nc.vector.tensor_copy(kept[k][:, t, :], src)
-            else:
-                nc.scalar.activation(kept[k][:, t, :], src, COPY)
+        def kept_at(t, piece):
+            at = piece.start % BANK
+            return kept[piece.start // BANK][:, t, at : at + width(piece)]
 
-        def weave(k):
-            nc.vector.tensor_copy(grouped[k][:].rearrange("p (c i) t -> p c t i", i=4), kept[k].rearrange("p t (c i) -> p c t i", i=4))
+        def gather(engine, t, piece):
+            src = res[t][:].indirect(entries(idx2, piece))
+            if engine is nc.vector:
+                nc.vector.tensor_copy(kept_at(t, piece), src)
+            else:
+                nc.scalar.activation(kept_at(t, piece), src, COPY)
+
+        grouped = {}
+
+        def weave(k, tag):
+            at = PIECES[k].start % BANK
+            planes = kept[PIECES[k].start // BANK][:, :, at : at + width(PIECES[k])]
+            if tag is None:
+                grouped[k] = kept[1][:, D, :].bitcast(BF16).rearrange("p (s t) -> p s t", t=PACK)
+            else:
+                grouped[k] = keep.tile([P, width(PIECES[k]), PACK], BF16, name="grouped%d" % k, tag=tag, align_bytes=64)[:]
+            nc.vector.tensor_copy(grouped[k].rearrange("p (c i) t -> p c t i", i=4), planes.rearrange("p t (c i) -> p c t i", i=4))
 
         def quantise(k):
-            nc.vector.quantize_mx(out=codes[:, PIECES[k]].bitcast(FP8X4), scales=scales[:, PIECES[k]], in_=grouped[k][:].rearrange("p s t -> p (s t)"))
+            nc.vector.quantize_mx(out=codes[:, PIECES[k]].bitcast(FP8X4), scales=scales[:, PIECES[k]], in_=grouped[k].rearrange("p s t -> p (s t)"))
 
         y2 = {t: tile("y2_%d" % t, S, F32) for t in (A, B, C, D)}
+        raw2 = {}
 
         def second(t, piece):
-            product(y2[t][:, piece], w2[:, t * P : (t + 1) * P].bitcast(FP8X4), s2_all[:, t * P : (t + 1) * P],
+            raw2[t, piece.start] = tile("raw2_%d_%d" % (t, piece.start), width(piece), F32)
+            product(raw2[t, piece.start][:], w2[:, t * P : (t + 1) * P].bitcast(FP8X4), s2_all[:, t * P : (t + 1) * P],
                     codes[:, piece].bitcast(FP8X4), scales[:, piece], width(piece))
 
         def vector_gate(t, piece):
             at = piece.start % BANK
-            nc.vector.tensor_tensor(y2[t][:, piece], y2[t][:, piece], g2_banks[piece.start // BANK][:, at : at + width(piece)], MULT)
+            nc.vector.tensor_tensor(y2[t][:, piece], raw2[t, piece.start][:], g2_banks[piece.start // BANK][:, at : at + width(piece)], MULT)
 
-        def pool_gate(t, piece):
-            nc.gpsimd.tensor_tensor(y2[t][:, piece], y2[t][:, piece], g2[:, piece], MULT)
-
-        def pool_add(t, k):
-            nc.gpsimd.tensor_tensor(y2[t][:, PIECES[k]], y2[t][:, PIECES[k]], kept[k][:, t, :], ADD)
+        def add_on(engine, t, piece):
+            engine.tensor_tensor(y2[t][:, piece], y2[t][:, piece], kept_at(t, piece), ADD)
 
         def back(engine, t, piece):
             scatter(engine, res[t], idx2, piece, y2[t][:, piece])
 
-        def fused(t, k):
-            nc.vector.tensor_tensor(res[t][:].indirect(entries(idx2, PIECES[k])), y2[t][:, PIECES[k]], kept[k][:, t, :], ADD)
+        def fused(t, piece):
+            nc.vector.tensor_tensor(res[t][:].indirect(entries(idx2, piece)), y2[t][:, piece], kept_at(t, piece), ADD)
 
-        for t, k in ((A, 0), (A, 1), (A, 2), (B, 0), (B, 1), (C, 0), (C, 1), (B, 2), (C, 2), (D, 2)):
-            gather("scalar", t, k)
-        gather("vector", D, 0)
-        gather("vector", D, 1)
-        weave(0)
-        weave(1)
+        for t, piece in ((A, H[0]), (B, H[0]), (C, H[0]), (A, H[1]), (B, H[1]), (C, H[1])):
+            gather(nc.scalar, t, piece)
+        gather(nc.vector, D, H[0])
+        weave(0, "grouped0")
+        weave(1, None)
         quantise(0)
         quantise(1)
-        for t, piece in ((B, Q[0]), (A, Q[0]), (B, Q[1]), (A, Q[1]), (D, H[0])):
+        gather(nc.vector, D, H[1])
+        FIRST = ((B, Q[0]), (D, H[0]), (A, H[0]), (B, Q[1]))
+        for t, piece in FIRST:
             second(t, piece)
-        weave(2)
-        vector_gate(B, Q[0])
-        quantise(2)
-        vector_gate(A, Q[0])
-        vector_gate(B, Q[1])
-        vector_gate(A, Q[1])
-        vector_gate(D, H[0])
-        for t, k in ((B, 0), (A, 0), (B, 1), (A, 1), (D, 0), (D, 1)):
-            pool_add(t, k)
-        second(B, H[1])
-        second(A, H[1])
-        back("scalar", B, Q[0])
-        back("vector", A, Q[0])
-        second(D, H[1])
-        back("scalar", B, Q[1])
-        vector_gate(B, H[1])
-        vector_gate(A, H[1])
-        pool_add(B, 2)
-        pool_add(A, 2)
-        back("vector", A, Q[1])
         second(C, H[0])
-        second(C, H[1])
-        back("scalar", D, Q[0])
-        pool_gate(D, H[1])
-        pool_gate(C, H[0])
-        pool_add(D, 2)
-        back("scalar", B, Q[2])
-        back("scalar", D, Q[1])
-        back("scalar", B, Q[3])
-        back("vector", A, H[1])
-        for t in (A, B):
-            nc.sync.dma_start(out=out_rows[t], in_=res[t][:])
-        back("scalar", D, Q[2])
-        back("scalar", D, Q[3])
+        for t, piece in FIRST:
+            vector_gate(t, piece)
+        weave(2, "raw2_%d_0" % D)
+        add_on(nc.gpsimd, B, Q[0])
+        add_on(nc.gpsimd, D, Q[0])
+        add_on(nc.vector, A, Q[0])
+        quantise(2)
+        back(nc.scalar, B, Q[0])
+        back(nc.scalar, D, Q[0])
+        back(nc.vector, A, Q[0])
+        for t in (A, B, D, C):
+            second(t, H[1])
+        late = keep.tile([P, 3, 256], F32, name="late", tag="raw2_%d_0" % D, align_bytes=64)
+        for j, t in enumerate((B, A, D)):
+            nc.gpsimd.tensor_tensor(late[:, j, :], y2[t][:, Q[1]], kept_at(t, Q[1]), ADD)
+        vector_gate(A, H[1])
+        gated_b = tile("gated_b", BANK, F32)
+        nc.vector.tensor_tensor(gated_b[:], raw2[B, BANK][:], g2_banks[1][:], MULT)
+        scatter(nc.vector, res[A], idx2, Q[1], late[:, 1, :])
+        vector_gate(D, H[1])
         vector_gate(C, H[1])
-        fused(C, 0)
-        fused(C, 1)
-        fused(C, 2)
-        for t in (D, C):
-            for cols in TH:
-                nc.sync.dma_start(out=out_rows[t][:, cols], in_=res[t][:, cols])
+        add_on(nc.gpsimd, A, H[1])
+        for q in (2, 3):
+            nc.gpsimd.tensor_tensor(y2[B][:, Q[q]], gated_b[:, Q[q - 2]], kept_at(B, Q[q]), ADD)
+            add_on(nc.gpsimd, D, Q[q])
+        gated_c = tile("gated_c", BANK, F32, tag="gated_b")
+        nc.gpsimd.tensor_tensor(gated_c[:], raw2[C, 0][:], g2[:], MULT)
+        back(nc.vector, A, H[1])
+        nc.sync.dma_start(out=out_rows[A], in_=res[A][:])
+        scatter(nc.scalar, res[B], idx2, Q[1], late[:, 0, :])
+        scatter(nc.scalar, res[D], idx2, Q[1], late[:, 2, :])
+        for q in (2, 3):
+            for t in (B, D):
+                back(nc.scalar, t, Q[q])
+        nc.sync.dma_start(out=out_rows[B], in_=res[B][:])
+        nc.vector.tensor_tensor(res[C][:].indirect(entries(idx2, H[0])), gated_c[:], kept_at(C, H[0]), ADD)
+        fused(C, H[1])
+        for cols in TH:
+            nc.scalar.dma_start(out=out_rows[D][:, cols], in_=res[D][:, cols])
+        for cols in TH:
+            nc.sync.dma_start(out=out_rows[C][:, cols], in_=res[C][:, cols])

@@ -22,7 +22,7 @@ COPY = mybir.ActivationFunctionType.Copy
 MULT = mybir.AluOpType.mult
 ADD = mybir.AluOpType.add
 
-A, B, C, D = 0, 2, 1, 3
+A, B, C, D = 0, 1, 2, 3
 Q = [slice(256 * q, 256 * (q + 1)) for q in range(4)]
 H = [slice(0, 512), slice(512, 1024)]
 REST = slice(256, 1024)
@@ -63,7 +63,7 @@ def tile_moe_mod_silu_kernel(
         w2_raw = tile("w2_raw", K, U32)
         s2_raw = tile("s2_raw", K, U8)
         g1 = tile("g1", S, F32)
-        g2 = tile("g2", BANK, F32)
+        g2 = tile("g2", S, F32)
         g2_rows = tile("g2_rows", P, F32)
         xr_a = tile("xr_a", T, F32)
         res = {A: tile("res_a", T, F32)}
@@ -96,7 +96,7 @@ def tile_moe_mod_silu_kernel(
         nc.sync.dma_start(idx2[:], offs2)
         nc.sync.dma_start(out=xr_a[:], in_=xr_rows[A])
         nc.sync.dma_start(out=g2_rows[:], in_=gate2[0:16, :].rearrange("a (m j) -> (a m) j", j=P))
-        nc.sync.dma_start(out=g2[:], in_=gate2[:, H[0]])
+        nc.sync.dma_start(out=g2[:], in_=gate2)
 
         gs = tile("gs", S, U8)
         gw = tile("gw", S, U32)
@@ -135,10 +135,16 @@ def tile_moe_mod_silu_kernel(
         raw1 = {t: tile("raw1_%d" % t, S, F32) for t in (A, B, C, D)}
         y1 = {t: tile("y1_%d" % t, S, F32) for t in (A, B, C, D)}
 
-        def first(t, piece):
+        def w1_of(t):
             e, u = t % 2, t // 2
-            product(raw1[t][:, piece], w1[:, 2 * P * (2 * e + u) : 2 * P * (2 * e + u + 1)].bitcast(FP4X4), s1[t],
-                    gw[:, piece].bitcast(FP8X4), gs[:, piece], width(piece))
+            return w1[:, 2 * P * (2 * e + u) : 2 * P * (2 * e + u + 1)].bitcast(FP4X4)
+
+        def first(t, piece, bank, dst=None):
+            acc = psum.tile([P, BANK], F32, name="acc", tag="acc%d" % bank)
+            n = width(piece)
+            nc.tensor.matmul_mx(out=acc[:, :n], lhsT=w1_of(t), lhsT_scale=s1[t], rhs=gw[:, piece].bitcast(FP8X4), rhs_scale=gs[:, piece],
+                                start=True, stop=True)
+            nc.scalar.activation(raw1[t][:, piece] if dst is None else dst, acc[:, :n], SILU)
 
         def gate1_on(engine, t, piece):
             engine.tensor_tensor(y1[t][:, piece], raw1[t][:, piece], g1[:, piece], MULT)
@@ -152,23 +158,28 @@ def tile_moe_mod_silu_kernel(
         def forth(engine, t, piece):
             scatter(engine, z1[t], idx1, piece, y1[t][:, piece])
 
-        for t in (A, D, B, C):
-            first(t, Q[0])
-        gate1_on(nc.vector, A, Q[0])
-        for t in (B, C):
-            gate1_on(nc.gpsimd, t, Q[0])
-        for piece in (Q[1], H[1]):
-            first(A, piece)
-        forth(nc.scalar, B, Q[0])
-        forth(nc.vector, A, Q[0])
-        forth(nc.vector, C, Q[0])
-        for t in (B, C, D):
-            for piece in (Q[1], H[1]):
-                first(t, piece)
-        gate1_on(nc.gpsimd, A, REST)
-        gate1_on(nc.gpsimd, D, Q[0])
-        for t in (B, C, D):
-            gate1_on(nc.gpsimd, t, REST)
+        def first_pair(pair, engine, name):
+            raw = keep.tile([P, 2, 256], F32, name=name + "_raw", align_bytes=64)
+            for j, t in enumerate(pair):
+                first(t, Q[0], t, raw[:, j, :])
+            gated = keep.tile([P, 2, 256], F32, name=name, align_bytes=64)
+            engine.tensor_tensor(gated[:], raw[:], g1[:, Q[0]].unsqueeze(1).to_broadcast([P, 2, 256]), MULT)
+            return gated
+
+        lead_v = first_pair((A, C), nc.vector, "lead_v")
+        lead_s = first_pair((B, D), nc.gpsimd, "lead_s")
+        first(A, Q[1], A)
+        first(A, H[1], C)
+        scatter(nc.vector, z1[A], idx1, Q[0], lead_v[:, 0, :])
+        scatter(nc.vector, z1[C], idx1, Q[0], lead_v[:, 1, :])
+        first(B, Q[1], B)
+        first(B, H[1], D)
+        scatter(nc.scalar, z1[B], idx1, Q[0], lead_s[:, 0, :])
+        for t in (C, D):
+            first(t, Q[1], t % 2)
+            first(t, H[1], 2 + t % 2)
+        for t, piece in ((A, REST), (B, THIRDS[1]), (C, REST), (D, THIRDS[1]), (B, THIRDS[2]), (D, THIRDS[2])):
+            gate1_on(nc.gpsimd, t, piece)
         forth(nc.vector, A, REST)
         forth(nc.vector, C, REST)
 
@@ -183,27 +194,33 @@ def tile_moe_mod_silu_kernel(
                 nc.tensor.transpose(bank[:, j * P : (j + 1) * P], gate_cols[:, 4 * h + j : 4 * h + j + 1].to_broadcast([P, P]), ident[:])
             g2_banks.append(bank)
 
-        forth(nc.scalar, D, THIRDS[0])
+        scatter(nc.scalar, z1[D], idx1, Q[0], lead_s[:, 1, :])
         for piece in THIRDS[1:]:
             forth(nc.scalar, B, piece)
             forth(nc.scalar, D, piece)
-        for t in (B, C, D):
+        for t in (C, B, D):
             res[t] = tile("res_%d" % t, T, F32, tag="raw1_%d" % t)
             nc.sync.dma_start(out=res[t][:], in_=xr_rows[t])
         nc.gpsimd.tensor_tensor(res[A][:], xr_a[:], z1[A][:], ADD)
-        for t in (B, C, D):
+        for t in (C, B):
             nc.vector.tensor_tensor(res[t][:], res[t][:], z1[t][:], ADD)
+        xr_d = res[D]
+        res[D] = tile("res_d", T, F32)
+        nc.vector.tensor_tensor(res[D][:], xr_d[:], z1[D][:], ADD)
 
-        s2_all = permuted(s2_raw, U8, "s2", "z1_%d" % D)
+        s2_all = permuted(s2_raw, U8, "s2", "raw1_%d" % D)
 
         PIECES = (Q[0], Q[1], H[1])
-        kept = [keep.tile([P, PACK, BANK], F32, name="kept%d" % h, tag=tag, align_bytes=64) for h, tag in enumerate(("xr_a", "w1_raw"))]
+        kept_first = keep.tile([P, 2, PACK, 256], F32, name="kept_first", tag="xr_a", align_bytes=64)
+        kept_rest = keep.tile([P, PACK, BANK], F32, name="kept_rest", tag="z1_%d" % D, align_bytes=64)
+        kept = [kept_first[:, 0], kept_first[:, 1], kept_rest[:]]
         codes = tile("codes", S, U32)
         scales = tile("scales", S, U8)
 
         def kept_at(t, piece):
-            at = piece.start % BANK
-            return kept[piece.start // BANK][:, t, at : at + width(piece)]
+            if piece.start < BANK:
+                return kept[piece.start // 256][:, t, :]
+            return kept_rest[:, t, piece.start - BANK : piece.stop - BANK]
 
         def gather(engine, t, piece):
             src = res[t][:].indirect(entries(idx2, piece))
@@ -215,10 +232,9 @@ def tile_moe_mod_silu_kernel(
         grouped = {}
 
         def weave(k, tag):
-            at = PIECES[k].start % BANK
-            planes = kept[PIECES[k].start // BANK][:, :, at : at + width(PIECES[k])]
+            planes = kept[k]
             if tag is None:
-                grouped[k] = kept[1][:, D, :].bitcast(BF16).rearrange("p (s t) -> p s t", t=PACK)
+                grouped[k] = kept_rest[:, D, :].bitcast(BF16).rearrange("p (s t) -> p s t", t=PACK)
             else:
                 grouped[k] = keep.tile([P, width(PIECES[k]), PACK], BF16, name="grouped%d" % k, tag=tag, align_bytes=64)[:]
             nc.vector.tensor_copy(grouped[k].rearrange("p (c i) t -> p c t i", i=4), planes.rearrange("p t (c i) -> p c t i", i=4))
@@ -226,7 +242,7 @@ def tile_moe_mod_silu_kernel(
         def quantise(k):
             nc.vector.quantize_mx(out=codes[:, PIECES[k]].bitcast(FP8X4), scales=scales[:, PIECES[k]], in_=grouped[k].rearrange("p s t -> p (s t)"))
 
-        y2 = {t: tile("y2_%d" % t, S, F32) for t in (A, B, C, D)}
+        y2 = {t: tile("y2_%d" % t, S, F32) for t in (A, B, D)}
         raw2 = {}
 
         def second(t, piece):
@@ -244,14 +260,12 @@ def tile_moe_mod_silu_kernel(
         def back(engine, t, piece):
             scatter(engine, res[t], idx2, piece, y2[t][:, piece])
 
-        def fused(t, piece):
-            nc.vector.tensor_tensor(res[t][:].indirect(entries(idx2, piece)), y2[t][:, piece], kept_at(t, piece), ADD)
-
-        for t, piece in ((A, H[0]), (B, H[0]), (C, H[0]), (A, H[1]), (B, H[1]), (C, H[1])):
+        for t, piece in ((A, Q[0]), (A, Q[1]), (C, Q[0]), (C, Q[1]), (B, Q[0]), (B, Q[1]), (A, H[1]), (C, H[1]), (B, H[1])):
             gather(nc.scalar, t, piece)
-        gather(nc.vector, D, H[0])
-        weave(0, "grouped0")
-        weave(1, None)
+        gather(nc.vector, D, Q[0])
+        gather(nc.vector, D, Q[1])
+        weave(0, None)
+        weave(1, "grouped1")
         quantise(0)
         quantise(1)
         gather(nc.vector, D, H[1])
@@ -269,33 +283,43 @@ def tile_moe_mod_silu_kernel(
         back(nc.scalar, B, Q[0])
         back(nc.scalar, D, Q[0])
         back(nc.vector, A, Q[0])
-        for t in (A, B, D, C):
+        for t in (A, B, D):
             second(t, H[1])
-        late = keep.tile([P, 3, 256], F32, name="late", tag="raw2_%d_0" % D, align_bytes=64)
-        for j, t in enumerate((B, A, D)):
-            nc.gpsimd.tensor_tensor(late[:, j, :], y2[t][:, Q[1]], kept_at(t, Q[1]), ADD)
-        vector_gate(A, H[1])
-        gated_b = tile("gated_b", BANK, F32)
-        nc.vector.tensor_tensor(gated_b[:], raw2[B, BANK][:], g2_banks[1][:], MULT)
-        scatter(nc.vector, res[A], idx2, Q[1], late[:, 1, :])
-        vector_gate(D, H[1])
-        vector_gate(C, H[1])
-        add_on(nc.gpsimd, A, H[1])
-        for q in (2, 3):
-            nc.gpsimd.tensor_tensor(y2[B][:, Q[q]], gated_b[:, Q[q - 2]], kept_at(B, Q[q]), ADD)
-            add_on(nc.gpsimd, D, Q[q])
-        gated_c = tile("gated_c", BANK, F32, tag="gated_b")
-        nc.gpsimd.tensor_tensor(gated_c[:], raw2[C, 0][:], g2[:], MULT)
-        back(nc.vector, A, H[1])
+        early = tile("early", BANK + 256, F32, tag="raw2_%d_0" % D)
+        early_c, early_b = early[:, 0:BANK], early[:, BANK:]
+        nc.gpsimd.tensor_tensor(early_c, raw2[C, 0][:], g2[:, H[0]], MULT)
+        nc.gpsimd.tensor_tensor(early_b, y2[B][:, Q[1]], kept_at(B, Q[1]), ADD)
+        scatter(nc.scalar, res[B], idx2, Q[1], early_b)
+        second(C, H[1])
+        for t in (A, B, D):
+            vector_gate(t, H[1])
+        late_a = tile("late_a", 256, F32, tag="raw2_%d_%d" % (A, BANK))
+        late = tile("late", width(REST) + BANK, F32, tag="raw2_%d_%d" % (B, BANK))
+        late_d, last_a = late[:, 0 : width(REST)], late[:, width(REST) :]
+
+        def add_d(piece):
+            nc.gpsimd.tensor_tensor(late_d[:, piece.start - 256 : piece.stop - 256], y2[D][:, piece], kept_at(D, piece), ADD)
+
+        nc.gpsimd.tensor_tensor(late_a[:], y2[A][:, Q[1]], kept_at(A, Q[1]), ADD)
+        add_on(nc.gpsimd, B, Q[2])
+        nc.gpsimd.tensor_tensor(last_a, y2[A][:, H[1]], kept_at(A, H[1]), ADD)
+        add_d(Q[1])
+        add_d(slice(BANK, 640))
+        scatter(nc.vector, res[A], idx2, Q[1], late_a[:])
+        scatter(nc.vector, res[A], idx2, H[1], last_a)
+        gated_c = tile("gated_c", S, F32, tag="raw2_%d_%d" % (A, BANK))
+        nc.gpsimd.tensor_tensor(gated_c[:, H[0]].rearrange("p (q s) -> p q s", q=2), early_c.rearrange("p (q s) -> p q s", q=2), kept_first[:, :, C, :], ADD)
+        add_on(nc.gpsimd, B, Q[3])
+        add_d(THIRDS[2])
+        nc.gpsimd.tensor_tensor(gated_c[:, H[1]], raw2[C, BANK][:], g2[:, H[1]], MULT)
         nc.sync.dma_start(out=out_rows[A], in_=res[A][:])
-        scatter(nc.scalar, res[B], idx2, Q[1], late[:, 0, :])
-        scatter(nc.scalar, res[D], idx2, Q[1], late[:, 2, :])
-        for q in (2, 3):
-            for t in (B, D):
-                back(nc.scalar, t, Q[q])
+        back(nc.scalar, B, Q[2])
+        scatter(nc.scalar, res[D], idx2, THIRDS[1], late_d[:, 0:384])
+        back(nc.scalar, B, Q[3])
+        scatter(nc.scalar, res[D], idx2, THIRDS[2], late_d[:, 384:768])
         nc.sync.dma_start(out=out_rows[B], in_=res[B][:])
-        nc.vector.tensor_tensor(res[C][:].indirect(entries(idx2, H[0])), gated_c[:], kept_at(C, H[0]), ADD)
-        fused(C, H[1])
+        scatter(nc.vector, res[C], idx2, H[0], gated_c[:, H[0]])
+        nc.vector.tensor_tensor(res[C][:].indirect(entries(idx2, H[1])), gated_c[:, H[1]], kept_at(C, H[1]), ADD)
         for cols in TH:
             nc.scalar.dma_start(out=out_rows[D][:, cols], in_=res[D][:, cols])
         for cols in TH:

@@ -163,7 +163,11 @@ def tile_moe_mod_silu_kernel(
             for j, t in enumerate(pair):
                 first(t, Q[0], t, raw[:, j, :])
             gated = keep.tile([P, 2, 256], F32, name=name, align_bytes=64)
-            engine.tensor_tensor(gated[:], raw[:], g1[:, Q[0]].unsqueeze(1).to_broadcast([P, 2, 256]), MULT)
+            if engine is nc.vector:
+                for j in range(2):
+                    engine.tensor_tensor(gated[:, j, :], raw[:, j, :], g1[:, Q[0]], MULT)
+            else:
+                engine.tensor_tensor(gated[:], raw[:], g1[:, Q[0]].unsqueeze(1).to_broadcast([P, 2, 256]), MULT)
             return gated
 
         lead_v = first_pair((A, C), nc.vector, "lead_v")
@@ -174,10 +178,11 @@ def tile_moe_mod_silu_kernel(
         scatter(nc.vector, z1[C], idx1, Q[0], lead_v[:, 1, :])
         first(B, Q[1], B)
         first(B, H[1], D)
+        first(C, Q[1], A)
+        first(C, H[1], C)
         scatter(nc.scalar, z1[B], idx1, Q[0], lead_s[:, 0, :])
-        for t in (C, D):
-            first(t, Q[1], t % 2)
-            first(t, H[1], 2 + t % 2)
+        first(D, Q[1], B)
+        first(D, H[1], D)
         for t, piece in ((A, REST), (B, THIRDS[1]), (C, REST), (D, THIRDS[1]), (B, THIRDS[2]), (D, THIRDS[2])):
             gate1_on(nc.gpsimd, t, piece)
         forth(nc.vector, A, REST)

@@ -273,7 +273,8 @@ def tile_moe_mod_silu_kernel(
         weave(1, "grouped1")
         quantise(0)
         quantise(1)
-        gather(nc.vector, D, H[1])
+        gather(nc.vector, D, Q[2])
+        gather(nc.scalar, D, Q[3])
         FIRST = ((B, Q[0]), (D, H[0]), (A, H[0]), (B, Q[1]))
         for t, piece in FIRST:
             second(t, piece)

@@ -250,14 +250,14 @@ def tile_moe_mod_silu_kernel(
         y2 = {t: tile("y2_%d" % t, S, F32) for t in (A, B, D)}
         raw2 = {}
 
-        def second(t, piece):
-            raw2[t, piece.start] = tile("raw2_%d_%d" % (t, piece.start), width(piece), F32)
-            product(raw2[t, piece.start][:], w2[:, t * P : (t + 1) * P].bitcast(FP8X4), s2_all[:, t * P : (t + 1) * P],
+        def second(t, piece, dst=None):
+            raw2[t, piece.start] = tile("raw2_%d_%d" % (t, piece.start), width(piece), F32)[:] if dst is None else dst
+            product(raw2[t, piece.start], w2[:, t * P : (t + 1) * P].bitcast(FP8X4), s2_all[:, t * P : (t + 1) * P],
                     codes[:, piece].bitcast(FP8X4), scales[:, piece], width(piece))
 
         def vector_gate(t, piece):
             at = piece.start % BANK
-            nc.vector.tensor_tensor(y2[t][:, piece], raw2[t, piece.start][:], g2_banks[piece.start // BANK][:, at : at + width(piece)], MULT)
+            nc.vector.tensor_tensor(y2[t][:, piece], raw2[t, piece.start], g2_banks[piece.start // BANK][:, at : at + width(piece)], MULT)
 
         def add_on(engine, t, piece):
             engine.tensor_tensor(y2[t][:, piece], y2[t][:, piece], kept_at(t, piece), ADD)
@@ -274,12 +274,14 @@ def tile_moe_mod_silu_kernel(
         quantise(0)
         quantise(1)
         gather(nc.vector, D, Q[2])
-        gather(nc.scalar, D, Q[3])
         FIRST = ((B, Q[0]), (D, H[0]), (A, H[0]), (B, Q[1]))
-        for t, piece in FIRST:
+        second(B, Q[0], kept_at(D, Q[3]))
+        vector_gate(B, Q[0])
+        for t, piece in FIRST[1:]:
             second(t, piece)
+        gather(nc.scalar, D, Q[3])
         second(C, H[0])
-        for t, piece in FIRST:
+        for t, piece in FIRST[1:]:
             vector_gate(t, piece)
         weave(2, "raw2_%d_0" % D)
         add_on(nc.gpsimd, B, Q[0])
@@ -293,7 +295,7 @@ def tile_moe_mod_silu_kernel(
             second(t, H[1])
         early = tile("early", BANK + 256, F32, tag="raw2_%d_0" % D)
         early_c, early_b = early[:, 0:BANK], early[:, BANK:]
-        nc.gpsimd.tensor_tensor(early_c, raw2[C, 0][:], g2[:, H[0]], MULT)
+        nc.gpsimd.tensor_tensor(early_c, raw2[C, 0], g2[:, H[0]], MULT)
         nc.gpsimd.tensor_tensor(early_b, y2[B][:, Q[1]], kept_at(B, Q[1]), ADD)
         scatter(nc.scalar, res[B], idx2, Q[1], early_b)
         second(C, H[1])
@@ -317,7 +319,7 @@ def tile_moe_mod_silu_kernel(
         nc.gpsimd.tensor_tensor(gated_c[:, H[0]].rearrange("p (q s) -> p q s", q=2), early_c.rearrange("p (q s) -> p q s", q=2), kept_first[:, :, C, :], ADD)
         add_on(nc.gpsimd, B, Q[3])
         add_d(THIRDS[2])
-        nc.gpsimd.tensor_tensor(gated_c[:, H[1]], raw2[C, BANK][:], g2[:, H[1]], MULT)
+        nc.gpsimd.tensor_tensor(gated_c[:, H[1]], raw2[C, BANK], g2[:, H[1]], MULT)
         nc.sync.dma_start(out=out_rows[A], in_=res[A][:])
         back(nc.scalar, B, Q[2])
         scatter(nc.scalar, res[D], idx2, THIRDS[1], late_d[:, 0:384])

@@ -28,6 +28,7 @@ H = [slice(0, 512), slice(512, 1024)]
 REST = slice(256, 1024)
 THIRDS = [slice(0, 256), slice(256, 640), slice(640, 1024)]
 TH = [slice(0, 1024), slice(1024, 2048)]
+A_POOL, A_VECTOR = slice(0, 1792), slice(1792, 2048)
 
 
 def width(piece):
@@ -65,7 +66,7 @@ def tile_moe_mod_silu_kernel(
         g1 = tile("g1", S, F32)
         g2 = tile("g2", S, F32)
         g2_rows = tile("g2_rows", P, F32)
-        xr_a = tile("xr_a", T, F32)
+        xr_a = tile("xr_a", width(A_POOL), F32)
         res = {A: tile("res_a", T, F32)}
 
         zero = tile("zero", 16, F32)
@@ -94,7 +95,7 @@ def tile_moe_mod_silu_kernel(
         nc.sync.dma_start(out=g1[:, REST], in_=gate1[:, REST])
         load_live_rows(s2_raw, w2_scales[0])
         nc.sync.dma_start(idx2[:], offs2)
-        nc.sync.dma_start(out=xr_a[:], in_=xr_rows[A])
+        nc.sync.dma_start(out=xr_a[:], in_=xr_rows[A][:, A_POOL])
         nc.sync.dma_start(out=g2_rows[:], in_=gate2[0:16, :].rearrange("a (m j) -> (a m) j", j=P))
         nc.sync.dma_start(out=g2[:], in_=gate2)
 
@@ -203,10 +204,13 @@ def tile_moe_mod_silu_kernel(
         for piece in THIRDS[1:]:
             forth(nc.scalar, B, piece)
             forth(nc.scalar, D, piece)
+        xr_a_end = tile("xr_a_end", width(A_VECTOR), F32, tag="y1_%d" % A)
+        nc.sync.dma_start(out=xr_a_end[:], in_=xr_rows[A][:, A_VECTOR])
         for t in (C, B, D):
             res[t] = tile("res_%d" % t, T, F32, tag="raw1_%d" % t)
             nc.sync.dma_start(out=res[t][:], in_=xr_rows[t])
-        nc.gpsimd.tensor_tensor(res[A][:], xr_a[:], z1[A][:], ADD)
+        nc.gpsimd.tensor_tensor(res[A][:, A_POOL], xr_a[:], z1[A][:, A_POOL], ADD)
+        nc.vector.tensor_tensor(res[A][:, A_VECTOR], xr_a_end[:], z1[A][:, A_VECTOR], ADD)
         for t in (C, B):
             nc.vector.tensor_tensor(res[t][:], res[t][:], z1[t][:], ADD)
         xr_d = res[D]

from contextlib import ExitStack

import concourse.mybir as mybir
from concourse.masks import make_identity

K, T, S = 512, 2048, 1024
P = 128
PACK = 4
BANK = 512
FLOPS = 2 * 2 * K * K * S

F32 = mybir.dt.float32
BF16 = mybir.dt.bfloat16
I32 = mybir.dt.int32
U32 = mybir.dt.uint32
U16 = mybir.dt.uint16
U8 = mybir.dt.uint8
FP8X4 = mybir.dt.float8_e4m3fn_x4
FP4X4 = mybir.dt.float4_e2m1fn_x4
SILU = mybir.ActivationFunctionType.Silu
COPY = mybir.ActivationFunctionType.Copy
MULT = mybir.AluOpType.mult
ADD = mybir.AluOpType.add

A, B, C, D = 0, 1, 2, 3
Q = [slice(256 * q, 256 * (q + 1)) for q in range(4)]
H = [slice(0, 512), slice(512, 1024)]
REST = slice(256, 1024)
THIRDS = [slice(0, 256), slice(256, 640), slice(640, 1024)]
TH = [slice(0, 1024), slice(1024, 2048)]
A_POOL, A_VECTOR = slice(0, 1792), slice(1792, 2048)


def width(piece):
    return piece.stop - piece.start


def tile_moe_mod_silu_kernel(
    tc, x_words, x_scales, xr, w1_words, w1_scales, w2_words, w2_scales, gate1, gate2, offs, offs2, out
):
    nc = tc.nc
    with ExitStack() as ctx:
        lists = ctx.enter_context(tc.tile_pool(name="lists", bufs=1))
        keep = ctx.enter_context(tc.tile_pool(name="keep", bufs=1))
        psum = ctx.enter_context(tc.psum_pool(name="psum", bufs=1))

        def tile(name, cols, dtype, tag=None):
            return keep.tile([P, cols], dtype, name=name, tag=tag or name, align_bytes=64)

        def entries(lst, piece):
            return lst[:, piece.start // 16 : piece.stop // 16]

        def load_live_rows(plane, rows):
            words = rows.bitcast(I32)
            for q in range(4):
                nc.sync.dma_start(out=plane[32 * q : 32 * q + 4, :].bitcast(I32), in_=words[4 * q : 4 * (q + 1), :])

        idx1 = lists.tile([P, S // 16], U16, name="idx1")
        idx2 = lists.tile([P, S // 16], U16, name="idx2")
        xs = tile("xs", T, U8)
        xw = tile("xw", T, U32)
        w1_raw = tile("w1_raw", 2 * K, U8)
        s1_raw = tile("s1_raw", K, U8)
        w2_raw = tile("w2_raw", K, U32)
        s2_raw = tile("s2_raw", K, U8)
        g1 = tile("g1", S, F32)
        g2 = tile("g2", S, F32)
        g2_rows = tile("g2_rows", P, F32)
        xr_a = tile("xr_a", width(A_POOL), F32)
        res = {A: tile("res_a", T, F32)}

        zero = tile("zero", 16, F32)
        ident = tile("ident", P, F32)
        nc.vector.memset(xs[:].bitcast(I32), 0)
        nc.vector.memset(zero[:], 0.0)
        nc.vector.memset(ident[:], 0.0)
        nc.vector.memset(s1_raw[:].bitcast(I32), 0)
        nc.vector.memset(s2_raw[:].bitcast(I32), 0)
        zeros = zero[:, 0:1].to_broadcast([P, T])
        z1 = {t: tile("z1_%d" % t, T, F32) for t in (A, B, D)}
        nc.vector.memset(z1[A][:], 0.0)
        make_identity(nc, ident[:], nomemset=True)
        nc.scalar.activation(z1[B][:], zeros, SILU)
        nc.scalar.copy(z1[D][:], zeros)

        xr_rows = xr.rearrange("(p t) w -> t p w", t=PACK)
        out_rows = out.rearrange("(p t) w -> t p w", t=PACK)
        nc.sync.dma_start(idx1[:], offs)
        nc.sync.dma_start(out=w1_raw[:].bitcast(I32), in_=w1_words[0].bitcast(I32))
        load_live_rows(xs, x_scales[0])
        nc.sync.dma_start(out=xw[:].bitcast(I32), in_=x_words[0].rearrange("p t d -> p (t d)").bitcast(I32))
        load_live_rows(s1_raw, w1_scales[0])
        nc.sync.dma_start(out=g1[:, Q[0]], in_=gate1[:, Q[0]])
        nc.sync.dma_start(out=w2_raw[:].bitcast(I32), in_=w2_words[0].rearrange("p n d -> p (n d)").bitcast(I32))
        nc.sync.dma_start(out=g1[:, REST], in_=gate1[:, REST])
        load_live_rows(s2_raw, w2_scales[0])
        nc.sync.dma_start(idx2[:], offs2)
        nc.sync.dma_start(out=xr_a[:], in_=xr_rows[A][:, A_POOL])
        nc.sync.dma_start(out=g2_rows[:], in_=gate2[0:16, :].rearrange("a (m j) -> (a m) j", j=P))
        nc.sync.dma_start(out=g2[:], in_=gate2)

        gs = tile("gs", S, U8)
        gw = tile("gw", S, U32)
        w1 = tile("w1", 2 * K, U8)
        s1_pairs = [tile("s1_%d" % e, 2 * P, U8) for e in range(2)]
        s1 = {t: s1_pairs[t % 2][:, t // 2 * P : (t // 2 + 1) * P] for t in range(PACK)}
        nc.vector.tensor_copy(
            w1[:].bitcast(U16).rearrange("p (e u m) -> p e u m", e=2, u=2),
            w1_raw[:].bitcast(U16).rearrange("p (m u e) -> p e u m", u=2, e=2),
        )
        z1[C] = tile("z1_c", T, F32, tag="w1_raw")
        nc.gpsimd.memset(z1[C][:], 0.0)
        nc.vector.tensor_copy(gs[:], xs[:].indirect(idx1[:]))
        nc.vector.tensor_copy(gw[:, Q[0]], xw[:].indirect(entries(idx1, Q[0])))
        s1_planes = s1_raw[:].rearrange("p (m u e) -> p e u m", u=2, e=2)
        for e in range(2):
            nc.gpsimd.tensor_copy(s1_pairs[e][:].rearrange("p (u m) -> p u m", u=2), s1_planes[:, e])

        def permuted(raw, dtype, name, tag):
            dst = tile(name, K, dtype, tag=tag)
            nc.gpsimd.tensor_copy(dst[:].rearrange("p (t m) -> p t m", t=PACK), raw[:].rearrange("p (m t) -> p t m", t=PACK))
            return dst

        w2 = permuted(w2_raw, U32, "w2", "w2")
        nc.vector.tensor_copy(gw[:, Q[1]], xw[:].indirect(entries(idx1, Q[1])))
        nc.vector.tensor_copy(gw[:, H[1]], xw[:].indirect(entries(idx1, H[1])))

        turns = []

        def product(y, lhs, lhs_scale, rhs, rhs_scale, n):
            acc = psum.tile([P, BANK], F32, name="acc", tag="acc%d" % (len(turns) % 6))
            turns.append(n)
            nc.tensor.matmul_mx(out=acc[:, :n], lhsT=lhs, lhsT_scale=lhs_scale, rhs=rhs, rhs_scale=rhs_scale, start=True, stop=True)
            nc.scalar.activation(y, acc[:, :n], SILU)

        raw1 = {t: tile("raw1_%d" % t, S, F32) for t in (A, B, C, D)}
        y1 = {t: tile("y1_%d" % t, S, F32) for t in (A, B, C, D)}

        def w1_of(t):
            e, u = t % 2, t // 2
            return w1[:, 2 * P * (2 * e + u) : 2 * P * (2 * e + u + 1)].bitcast(FP4X4)

        def first(t, piece, bank, dst=None):
            acc = psum.tile([P, BANK], F32, name="acc", tag="acc%d" % bank)
            n = width(piece)
            nc.tensor.matmul_mx(out=acc[:, :n], lhsT=w1_of(t), lhsT_scale=s1[t], rhs=gw[:, piece].bitcast(FP8X4), rhs_scale=gs[:, piece],
                                start=True, stop=True)
            nc.scalar.activation(raw1[t][:, piece] if dst is None else dst, acc[:, :n], SILU)

        def gate1_on(engine, t, piece):
            engine.tensor_tensor(y1[t][:, piece], raw1[t][:, piece], g1[:, piece], MULT)

        def scatter(engine, window, lst, piece, src):
            if engine is nc.vector:
                nc.vector.tensor_copy(window[:].indirect(entries(lst, piece)), src)
            else:
                nc.scalar.activation(window[:].indirect(entries(lst, piece)), src, COPY)

        def forth(engine, t, piece):
            scatter(engine, z1[t], idx1, piece, y1[t][:, piece])

        def first_pair(pair, engine, name):
            raw = keep.tile([P, 2, 256], F32, name=name + "_raw", align_bytes=64)
            for j, t in enumerate(pair):
                first(t, Q[0], t, raw[:, j, :])
            gated = keep.tile([P, 2, 256], F32, name=name, align_bytes=64)
            if engine is nc.vector:
                for j in range(2):
                    engine.tensor_tensor(gated[:, j, :], raw[:, j, :], g1[:, Q[0]], MULT)
            else:
                engine.tensor_tensor(gated[:], raw[:], g1[:, Q[0]].unsqueeze(1).to_broadcast([P, 2, 256]), MULT)
            return gated

        lead_v = first_pair((A, C), nc.vector, "lead_v")
        lead_s = first_pair((B, D), nc.gpsimd, "lead_s")
        first(A, Q[1], A)
        first(A, H[1], C)
        scatter(nc.vector, z1[A], idx1, Q[0], lead_v[:, 0, :])
        scatter(nc.vector, z1[C], idx1, Q[0], lead_v[:, 1, :])
        first(B, Q[1], B)
        first(B, H[1], D)
        first(C, Q[1], A)
        first(C, H[1], C)
        scatter(nc.scalar, z1[B], idx1, Q[0], lead_s[:, 0, :])
        first(D, Q[1], B)
        first(D, H[1], D)
        for t, piece in ((A, REST), (B, THIRDS[1]), (C, REST), (D, THIRDS[1]), (B, THIRDS[2]), (D, THIRDS[2])):
            gate1_on(nc.gpsimd, t, piece)
        forth(nc.vector, A, REST)
        forth(nc.vector, C, REST)

        gate_cols = tile("gate_cols", S // P, F32)
        turned = psum.tile([P, P], F32, name="turned", tag="gate0")
        nc.tensor.transpose(turned[:], g2_rows[:], ident[:])
        nc.scalar.copy(gate_cols[:], turned[:, 0 : S // P])
        g2_banks = []
        for h in range(2):
            bank = psum.tile([P, BANK], F32, name="gate_bank", tag="gate%d" % h)
            for j in range(BANK // P):
                nc.tensor.transpose(bank[:, j * P : (j + 1) * P], gate_cols[:, 4 * h + j : 4 * h + j + 1].to_broadcast([P, P]), ident[:])
            g2_banks.append(bank)

        scatter(nc.scalar, z1[D], idx1, Q[0], lead_s[:, 1, :])
        for piece in THIRDS[1:]:
            forth(nc.scalar, B, piece)
            forth(nc.scalar, D, piece)
        xr_a_end = tile("xr_a_end", width(A_VECTOR), F32, tag="y1_%d" % A)
        nc.sync.dma_start(out=xr_a_end[:], in_=xr_rows[A][:, A_VECTOR])
        for t in (C, B, D):
            res[t] = tile("res_%d" % t, T, F32, tag="raw1_%d" % t)
            nc.sync.dma_start(out=res[t][:], in_=xr_rows[t])
        nc.gpsimd.tensor_tensor(res[A][:, A_POOL], xr_a[:], z1[A][:, A_POOL], ADD)
        nc.vector.tensor_tensor(res[A][:, A_VECTOR], xr_a_end[:], z1[A][:, A_VECTOR], ADD)
        for t in (C, B):
            nc.vector.tensor_tensor(res[t][:], res[t][:], z1[t][:], ADD)
        xr_d = res[D]
        res[D] = tile("res_d", T, F32)
        nc.vector.tensor_tensor(res[D][:], xr_d[:], z1[D][:], ADD)

        s2_all = permuted(s2_raw, U8, "s2", "raw1_%d" % D)

        PIECES = (Q[0], Q[1], H[1])
        kept_first = keep.tile([P, 2, PACK, 256], F32, name="kept_first", tag="xr_a", align_bytes=64)
        kept_rest = keep.tile([P, PACK, BANK], F32, name="kept_rest", tag="z1_%d" % D, align_bytes=64)
        kept = [kept_first[:, 0], kept_first[:, 1], kept_rest[:]]
        codes = tile("codes", S, U32)
        scales = tile("scales", S, U8)

        def kept_at(t, piece):
            if piece.start < BANK:
                return kept[piece.start // 256][:, t, :]
            return kept_rest[:, t, piece.start - BANK : piece.stop - BANK]

        def gather(engine, t, piece):
            src = res[t][:].indirect(entries(idx2, piece))
            if engine is nc.vector:
                nc.vector.tensor_copy(kept_at(t, piece), src)
            else:
                nc.scalar.activation(kept_at(t, piece), src, COPY)

        grouped = {}

        def weave(k, tag):
            planes = kept[k]
            if tag is None:
                grouped[k] = kept_rest[:, D, :].bitcast(BF16).rearrange("p (s t) -> p s t", t=PACK)
            else:
                grouped[k] = keep.tile([P, width(PIECES[k]), PACK], BF16, name="grouped%d" % k, tag=tag, align_bytes=64)[:]
            nc.vector.tensor_copy(grouped[k].rearrange("p (c i) t -> p c t i", i=4), planes.rearrange("p t (c i) -> p c t i", i=4))

        def quantise(k):
            nc.vector.quantize_mx(out=codes[:, PIECES[k]].bitcast(FP8X4), scales=scales[:, PIECES[k]], in_=grouped[k].rearrange("p s t -> p (s t)"))

        y2 = {t: tile("y2_%d" % t, S, F32) for t in (A, B, D)}
        raw2 = {}

        def second(t, piece, dst=None):
            raw2[t, piece.start] = tile("raw2_%d_%d" % (t, piece.start), width(piece), F32)[:] if dst is None else dst
            product(raw2[t, piece.start], w2[:, t * P : (t + 1) * P].bitcast(FP8X4), s2_all[:, t * P : (t + 1) * P],
                    codes[:, piece].bitcast(FP8X4), scales[:, piece], width(piece))

        def vector_gate(t, piece):
            at = piece.start % BANK
            nc.vector.tensor_tensor(y2[t][:, piece], raw2[t, piece.start], g2_banks[piece.start // BANK][:, at : at + width(piece)], MULT)

        def add_on(engine, t, piece):
            engine.tensor_tensor(y2[t][:, piece], y2[t][:, piece], kept_at(t, piece), ADD)

        def back(engine, t, piece):
            scatter(engine, res[t], idx2, piece, y2[t][:, piece])

        for t, piece in ((A, Q[0]), (A, Q[1]), (C, Q[0]), (C, Q[1]), (B, Q[0]), (B, Q[1]), (A, H[1]), (C, H[1]), (B, H[1])):
            gather(nc.scalar, t, piece)
        gather(nc.vector, D, Q[0])
        gather(nc.vector, D, Q[1])
        weave(0, None)
        weave(1, "grouped1")
        quantise(0)
        quantise(1)
        gather(nc.vector, D, Q[2])
        FIRST = ((B, Q[0]), (D, H[0]), (A, H[0]), (B, Q[1]))
        second(B, Q[0], kept_at(D, Q[3]))
        vector_gate(B, Q[0])
        for t, piece in FIRST[1:]:
            second(t, piece)
        gather(nc.scalar, D, Q[3])
        second(C, H[0])
        for t, piece in FIRST[1:]:
            vector_gate(t, piece)
        weave(2, "raw2_%d_0" % D)
        add_on(nc.gpsimd, B, Q[0])
        add_on(nc.gpsimd, D, Q[0])
        add_on(nc.vector, A, Q[0])
        quantise(2)
        back(nc.scalar, B, Q[0])
        back(nc.scalar, D, Q[0])
        back(nc.vector, A, Q[0])
        for t in (A, B, D):
            second(t, H[1])
        early = tile("early", BANK + 256, F32, tag="raw2_%d_0" % D)
        early_c, early_b = early[:, 0:BANK], early[:, BANK:]
        nc.gpsimd.tensor_tensor(early_c, raw2[C, 0], g2[:, H[0]], MULT)
        nc.gpsimd.tensor_tensor(early_b, y2[B][:, Q[1]], kept_at(B, Q[1]), ADD)
        scatter(nc.scalar, res[B], idx2, Q[1], early_b)
        second(C, H[1])
        for t in (A, B, D):
            vector_gate(t, H[1])
        late_a = tile("late_a", 256, F32, tag="raw2_%d_%d" % (A, BANK))
        late = tile("late", width(REST) + BANK, F32, tag="raw2_%d_%d" % (B, BANK))
        late_d, last_a = late[:, 0 : width(REST)], late[:, width(REST) :]

        def add_d(piece):
            nc.gpsimd.tensor_tensor(late_d[:, piece.start - 256 : piece.stop - 256], y2[D][:, piece], kept_at(D, piece), ADD)

        nc.gpsimd.tensor_tensor(late_a[:], y2[A][:, Q[1]], kept_at(A, Q[1]), ADD)
        add_on(nc.gpsimd, B, Q[2])
        nc.gpsimd.tensor_tensor(last_a, y2[A][:, H[1]], kept_at(A, H[1]), ADD)
        add_d(Q[1])
        add_d(slice(BANK, 640))
        scatter(nc.vector, res[A], idx2, Q[1], late_a[:])
        scatter(nc.vector, res[A], idx2, H[1], last_a)
        gated_c = tile("gated_c", S, F32, tag="raw2_%d_%d" % (A, BANK))
        nc.gpsimd.tensor_tensor(gated_c[:, H[0]].rearrange("p (q s) -> p q s", q=2), early_c.rearrange("p (q s) -> p q s", q=2), kept_first[:, :, C, :], ADD)
        add_on(nc.gpsimd, B, Q[3])
        add_d(THIRDS[2])
        nc.gpsimd.tensor_tensor(gated_c[:, H[1]], raw2[C, BANK], g2[:, H[1]], MULT)
        nc.sync.dma_start(out=out_rows[A], in_=res[A][:])
        back(nc.scalar, B, Q[2])
        scatter(nc.scalar, res[D], idx2, THIRDS[1], late_d[:, 0:384])
        back(nc.scalar, B, Q[3])
        scatter(nc.scalar, res[D], idx2, THIRDS[2], late_d[:, 384:768])
        nc.sync.dma_start(out=out_rows[B], in_=res[B][:])
        scatter(nc.vector, res[C], idx2, H[0], gated_c[:, H[0]])
        nc.vector.tensor_tensor(res[C][:].indirect(entries(idx2, H[1])), gated_c[:, H[1]], kept_at(C, H[1]), ADD)
        for cols in TH:
            nc.scalar.dma_start(out=out_rows[D][:, cols], in_=res[D][:, cols])
        for cols in TH:
            nc.sync.dma_start(out=out_rows[C][:, cols], in_=res[C][:, cols])
